import numpy as np
import ml_dtypes


def mxq(x, axis, fmt="e4m3"):
    dtype, down = {"e4m3": (ml_dtypes.float8_e4m3fn, 7), "e5m2": (ml_dtypes.float8_e5m2, 14)}[fmt]
    v = np.moveaxis(np.asarray(x, np.float32).astype(ml_dtypes.bfloat16).astype(np.float64), axis, -1)
    blocks = v.reshape(v.shape[:-1] + (-1, 32))
    amax = np.abs(blocks).max(-1, keepdims=True)
    byte = np.maximum(np.where(amax > 0, np.frexp(amax)[1] - 1 + 127, 0) - down, 1)
    scale = np.exp2(byte - 127.0)
    codes = (blocks / scale).astype(np.float32).astype(dtype).astype(np.float64)
    return np.moveaxis((codes * scale).reshape(v.shape), -1, axis)


WIDE = False


def mx_kscale(k):
    if not WIDE:
        return np.ones(k)
    levels = np.array([10, -10, 5, -5, 0])
    if k % 512:
        return np.exp2(np.random.permutation(np.resize(levels, k // 32))).repeat(32)
    a = np.empty((k // 512, 16))
    for p in range(k // 512):
        a[p, :8] = np.random.permutation(np.resize(levels, 8))
        for g in range(8):
            far = levels[np.abs(levels - a[p, g]) >= 10]
            a[p, g + 8] = far[np.random.randint(len(far))]
    return np.exp2(a.ravel()).repeat(32)


def f64(x):
    return np.asarray(x).astype(np.float64)


def striped(idx):
    return np.tile(idx.reshape(-1, 16).T, (8, 1)).astype(np.uint16)


def unstriped(offs):
    return offs[:16].T.reshape(-1).astype(np.int64)


E2M1 = np.array([0.0, 0.5, 1.0, 1.5, 2.0, 3.0, 4.0, 6.0, -0.0, -0.5, -1.0, -1.5, -2.0, -3.0, -4.0, -6.0])


def pack_weight(w, fmt):
    k, n = w.shape
    w = f64(np.asarray(w, np.float32).astype(ml_dtypes.bfloat16)).reshape(k // 32, 32, n)
    amax = np.abs(w).max(1)
    if fmt == "e4m3":
        byte = np.frexp(amax)[1] - 1 + 127 - 7
    else:
        mant, ex = np.frexp(amax / 6.0)
        byte = np.where(mant > 0.5, ex, ex - 1) + 127
    byte = np.clip(np.where(amax > 0, byte, 1), 1, 254)
    scaled = (w * np.exp2(127.0 - byte)[:, None, :]).reshape(k, n).astype(np.float32)
    by_word = np.ascontiguousarray(scaled.reshape(k // 512, 128, 4, n).transpose(0, 1, 3, 2))
    if fmt == "e4m3":
        words = by_word.astype(ml_dtypes.float8_e4m3fn).view(np.uint8)
    else:
        c = by_word.astype(ml_dtypes.float4_e2m1fn).view(np.uint8) & 0xF
        words = (c[..., 0::2] | (c[..., 1::2] << 4)).reshape(k // 512, 128, 2 * n)
    return np.ascontiguousarray(words), np.ascontiguousarray(byte.astype(np.uint8).reshape(k // 512, 16, n))


def unpack_weight(words, scales, fmt):
    g, _, n = scales.shape
    words = np.ascontiguousarray(words).reshape(g, 128, n, -1)
    if fmt == "e4m3":
        vals = words.view(ml_dtypes.float8_e4m3fn).astype(np.float64)
    else:
        nib = np.empty((g, 128, n, 4), np.uint8)
        nib[..., 0::2] = words & 0xF
        nib[..., 1::2] = words >> 4
        vals = E2M1[nib]
    vals = vals * np.repeat(np.exp2(scales.astype(np.float64) - 127.0), 8, axis=1)[..., None]
    return vals.transpose(0, 1, 3, 2).reshape(g * 512, n)


def gelu(v):
    return 0.5 * v * (1.0 + np.tanh(np.sqrt(2.0 / np.pi) * (v + 0.044715 * v**3)))


def often(T, S):
    return np.random.permutation(T)[(T * np.random.uniform(0, 1, S) ** 4).astype(np.int64)]


K, K2, T, S, H, N = 1024, 512, 4096, 1024, 1024, 512

def setup_inputs():
    n = np.random.standard_normal
    s = mx_kscale(K)[:, None]
    s2 = mx_kscale(K2)[:, None]
    u = mx_kscale(H)[:, None]
    tab_words, tab_scales = pack_weight(n((K, T)) * s, "e4m3")
    tab2_words, tab2_scales = pack_weight(n((K2, T)) * s2, "e2m1")
    w1_words, w1_scales = pack_weight(n((K, H)) / np.sqrt(K) / s, "e2m1")
    w2 = (n((K2, H)) / np.sqrt(K2) / s2).astype(np.float32)
    emis = (np.random.uniform(0.5, 1.5, H) * u[:, 0]).astype(np.float32)
    w3 = (n((H, N)) / np.sqrt(H) / u).astype(np.float32)
    return {"tab_words": tab_words, "tab_scales": tab_scales,
            "tab2_words": tab2_words, "tab2_scales": tab2_scales,
            "offs": striped(often(T, S)), "offs2": striped(often(T, S)),
            "w1_words": w1_words, "w1_scales": w1_scales,
            "w2": w2, "emis": emis, "w3": w3}

def reference(tab_words, tab_scales, tab2_words, tab2_scales, offs, offs2,
              w1_words, w1_scales, w2, emis, w3):
    v = unpack_weight(tab_words, tab_scales, "e4m3")[:, unstriped(offs)]
    v2 = unpack_weight(tab2_words, tab2_scales, "e2m1")[:, unstriped(offs2)]
    w1 = unpack_weight(w1_words, w1_scales, "e2m1")
    a = w1.T @ v
    b = mxq(f64(w2), 0, "e4m3").T @ v2
    x = a / (1.0 + np.square(b))
    h = f64(emis)[:, None] * np.sqrt(np.abs(x))
    return mxq(f64(w3), 0, "e4m3").T @ mxq(h, 0, "e4m3")

@@ -1,0 +1,277 @@
+from contextlib import ExitStack
+
+import concourse.mybir as mybir
+from concourse.masks import make_identity
+
+K, K2, T, S, H, N = 1024, 512, 4096, 1024, 1024, 512
+FLOPS = 2 * S * (K * H + K2 * H + H * N)
+
+F32 = mybir.dt.float32
+BF16 = mybir.dt.bfloat16
+I32 = mybir.dt.int32
+U32 = mybir.dt.uint32
+U16 = mybir.dt.uint16
+U8 = mybir.dt.uint8
+FP8X4 = mybir.dt.float8_e4m3fn_x4
+FP4X4 = mybir.dt.float4_e2m1fn_x4
+ACT = mybir.ActivationFunctionType
+MULT = mybir.AluOpType.mult
+MAX = mybir.AluOpType.max
+
+P = 128
+PACK = 4
+PASS = P * PACK
+HALF = 512
+RUN = 8
+SQ_ON_VECTOR = {(1, 0, 0), (1, 0, 1), (1, 0, 2)}
+ABS_ON_VECTOR = {(0, 0, 2), (0, 0, 3)}
+
+
+def tile_list_asteroid_band_fluxes_kernel(
+    tc, tab_words, tab_scales, tab2_words, tab2_scales, offs, offs2, w1_words, w1_scales, w2, emis, w3, out
+):
+    nc = tc.nc
+    halves = S // HALF
+    groups = H // PASS
+    kpasses = K // PASS
+    with ExitStack() as ctx:
+        keep = ctx.enter_context(tc.tile_pool(name="keep", bufs=1))
+        ring = ctx.enter_context(tc.tile_pool(name="ring", bufs=2))
+        psum_ab = ctx.enter_context(tc.psum_pool(name="psum_ab", bufs=6))
+        psum_out = ctx.enter_context(tc.psum_pool(name="psum_out", bufs=2))
+
+        def held(shape, dtype, name):
+            return keep.tile(shape, dtype, name=name, align_bytes=64)
+
+        idx = keep.tile([P, S // 16], U16, name="idx")
+        idx2 = keep.tile([P, S // 16], U16, name="idx2")
+        tab2_s = held([P, T], U8, "tab2_s")
+        tab_s = held([P, T], U8, "tab_s")
+        w1_s = held([P, kpasses * H], U8, "w1_s")
+        v2_s = held([P, S], U8, "v2_s")
+        v_s = [held([P, S], U8, "v_s%d" % a) for a in range(kpasses)]
+        v2_rows = held([P, S], U8, "v2_rows")
+        v_rows = held([P, S], U8, "v_rows")
+
+        nc.vector.memset(tab2_s[0 : P - 16, :].bitcast(I32), 0)
+        nc.vector.memset(v2_s[:].bitcast(I32), 0)
+        one = held([P, 1], F32, "one")
+        warm = held([P, 1], F32, "warm")
+        nc.gpsimd.memset(one[:], 1.0)
+        nc.scalar.activation(warm[:], one[:], ACT.Abs_reciprocal_sqrt)
+
+        w2_raw = [ring.tile([P, PACK, PASS], F32, name="w_raw", align_bytes=64) for g in range(groups)]
+        w3_raw = [ring.tile([P, PACK, N], F32, name="w_raw", align_bytes=64) for g in range(groups)]
+        tab2_w = held([P, T], U16, "tab2_w")
+        tab_w = [held([P, T], I32, "tab_w%d" % a) for a in range(kpasses)]
+        w1_w = held([P, kpasses * H], U16, "w1_w")
+        emis_rows = held([P, P], F32, "emis_rows")
+        ident = held([P, P], F32, "ident")
+        nc.gpsimd.memset(emis_rows[:], 0.0)
+        make_identity(nc, ident[:])
+
+        w2_bf = [held([P, PACK, P // RUN, RUN, PACK], BF16, "w2_bf%d" % g) for g in range(groups)]
+        w2_c = [held([P, PASS], U32, "w2_c%d" % g) for g in range(groups)]
+        w2_q = [held([P, PASS], U8, "w2_q%d" % g) for g in range(groups)]
+        w3_bf = [held([P, N, PACK], BF16, "w3_bf%d" % g) for g in range(groups)]
+        w3_c = [held([P, N], U32, "w3_c%d" % g) for g in range(groups)]
+        w3_q = [held([P, N], U8, "w3_q%d" % g) for g in range(groups)]
+
+        def cast_w2(copy, g, b0, b1):
+            dst = w2_bf[g][:].rearrange("p t b i j -> p b t j i")
+            src = w2_raw[g][:].rearrange("p j (b t i) -> p b t j i", t=PACK, i=RUN)
+            copy(dst[:, b0:b1], src[:, b0:b1])
+
+        def load_w3(g):
+            rows = w3[g * PASS : (g + 1) * PASS, :].rearrange("(b t i) n -> t b i n", t=PACK, i=RUN)
+            for t in range(PACK):
+                nc.sync.dma_start(w3_raw[g][:, t, :], rows[t])
+
+        def load_tab(a):
+            nc.sync.dma_start(tab_w[a][:], tab_words[a].rearrange("p t i -> p (t i)").bitcast(I32))
+
+        w2_rows = w2.rearrange("(p j) r -> p j r", j=PACK)
+        def spread(plane, rows, first):
+            for q in range(4):
+                src = rows[first + 4 * q : first + 4 * q + 4, :]
+                nc.sync.dma_start(plane[32 * q : 32 * q + 4, :].bitcast(I32), src.bitcast(I32))
+
+        nc.sync.dma_start(idx2[:], offs2)
+        nc.sync.dma_start(tab2_s[P - 16 : P, :].bitcast(I32), tab2_scales[0].bitcast(I32))
+        nc.sync.dma_start(w2_raw[0][:], w2_rows[:, :, 0:PASS])
+        nc.sync.dma_start(tab2_w[:].bitcast(I32), tab2_words[0].bitcast(I32))
+        nc.vector.tensor_copy(v2_rows[:], tab2_s[:].indirect(idx2[:]))
+        spread(v2_s, v2_rows, P - 16)
+        nc.gpsimd.memset(tab_s[0 : P - 32, :].bitcast(I32), 0)
+        nc.gpsimd.memset(w1_s[:].bitcast(I32), 0)
+        for a in range(kpasses):
+            nc.gpsimd.memset(v_s[a][:].bitcast(I32), 0)
+        nc.sync.dma_start(w2_raw[1][:], w2_rows[:, :, PASS : 2 * PASS])
+        nc.sync.dma_start(idx[:], offs)
+        nc.sync.dma_start(tab_s[P - 32 : P, :].bitcast(I32), tab_scales.rearrange("a q t -> (a q) t").bitcast(I32))
+        emis_runs = emis.rearrange("(g b t i) -> g t b i", g=groups, t=PACK, i=RUN)
+        for g in range(groups):
+            nc.sync.dma_start(emis_rows[g * PACK : (g + 1) * PACK, :].rearrange("t (b i) -> t b i", i=RUN), emis_runs[g])
+        cast_w2(nc.scalar.copy, 0, 0, 8)
+        cast_w2(nc.vector.tensor_copy, 0, 8, 16)
+        load_w3(0)
+        nc.sync.dma_start(
+            w1_w[:].bitcast(I32).rearrange("p (a c) -> p a c", a=kpasses),
+            w1_words.bitcast(I32).rearrange("a p c -> p a c"),
+        )
+        for q in range(4):
+            nc.sync.dma_start(
+                w1_s[32 * q : 32 * q + 4, :].bitcast(I32).rearrange("p (a c) -> p a c", a=kpasses),
+                w1_scales[:, 4 * q : 4 * q + 4, :].bitcast(I32).rearrange("a r c -> r a c"),
+            )
+        load_tab(0)
+
+        def picks(offsets, j):
+            return offsets[:, j * (HALF // 16) : (j + 1) * (HALF // 16)]
+
+        v2_w = [held([P, HALF], U16, "v2_w%d" % j) for j in range(halves)]
+        v_w = [[held([P, HALF], U32, "v_w%d_%d" % (a, j)) for j in range(halves)] for a in range(kpasses)]
+
+        def quantise(codes, scales, values):
+            nc.vector.quantize_mx(out=codes.bitcast(FP8X4), scales=scales, in_=values)
+
+        def quantise_w2(g):
+            quantise(w2_c[g][:], w2_q[g][:], w2_bf[g][:].rearrange("p t b i j -> p (t b i j)"))
+
+        def prepare_w3(g):
+            nc.vector.tensor_copy(
+                w3_bf[g][:].rearrange("p (c i) j -> p c j i", i=4), w3_raw[g][:].rearrange("p j (c i) -> p c j i", i=4)
+            )
+            quantise(w3_c[g][:], w3_q[g][:], w3_bf[g][:].rearrange("p n j -> p (n j)"))
+
+        r_t = [[held([P, PACK, HALF], F32, "r_%d_%d" % (g, j)) for j in range(halves)] for g in range(groups)]
+
+        def side_b(g, j):
+            sq = ring.tile([P, PACK, HALF], F32, name="stage", align_bytes=64, bufs=3)
+            for t in range(PACK):
+                cols = slice(t * P, (t + 1) * P)
+                bank = psum_ab.tile([P, HALF], F32, name="bank")
+                nc.tensor.matmul_mx(
+                    out=bank[:],
+                    lhsT=w2_c[g][:, cols].bitcast(FP8X4),
+                    lhsT_scale=w2_q[g][:, cols],
+                    rhs=v2_w[j][:].bitcast(FP4X4),
+                    rhs_scale=v2_s[:, j * HALF : (j + 1) * HALF],
+                    start=True,
+                    stop=True,
+                )
+                if (g, j, t) in SQ_ON_VECTOR:
+                    twin = ring.tile([P, HALF], F32, name="twin", align_bytes=64)
+                    nc.vector.tensor_copy(twin[:], bank[:])
+                    nc.vector.tensor_tensor(sq[:, t, :], bank[:], twin[:], MULT)
+                else:
+                    nc.scalar.activation(sq[:, t, :], bank[:], ACT.Square)
+            nc.scalar.activation(r_t[g][j][:], sq[:], ACT.Abs_reciprocal_sqrt, bias=1.0)
+
+        quantise_w2(0)
+        nc.vector.tensor_copy(v2_w[0][:], tab2_w[:].indirect(picks(idx2, 0)))
+        side_b(0, 0)
+        nc.vector.tensor_copy(v2_w[1][:], tab2_w[:].indirect(picks(idx2, 1)))
+        side_b(0, 1)
+        cast_w2(nc.vector.tensor_copy, 1, 0, 16)
+        quantise_w2(1)
+        nc.vector.tensor_copy(v_rows[:], tab_s[:].indirect(idx[:]))
+        side_b(1, 0)
+        for a in range(kpasses):
+            spread(v_s[a], v_rows, P - 32 + 16 * a)
+        load_tab(1)
+        load_w3(1)
+        side_b(1, 1)
+
+        emis2 = held([P, groups * PACK], F32, "emis2")
+        turned = psum_out.tile([P, P], F32, name="acc")
+        nc.tensor.transpose(turned[:], emis_rows[:], ident[:])
+        nc.scalar.activation(emis2[:], turned[:, 0 : groups * PACK], ACT.Square)
+        prepare_w3(0)
+        w1_wp = held([P, kpasses * H], U16, "w1_wp")
+        w1_sp = held([P, kpasses * H], U8, "w1_sp")
+        for dst, src in ((w1_wp, w1_w), (w1_sp, w1_s)):
+            nc.vector.tensor_copy(
+                dst[:].bitcast(I32).rearrange("p (g t b w) -> p g b t w", t=PACK, b=P // RUN, g=kpasses * groups),
+                src[:].bitcast(I32).rearrange("p (g b t w) -> p g b t w", t=PACK, b=P // RUN, g=kpasses * groups),
+            )
+        for a in range(kpasses):
+            for j in range(halves):
+                nc.vector.tensor_copy(v_w[a][j][:], tab_w[a][:].bitcast(U32).indirect(picks(idx, j)))
+
+        h_c = [held([P, S], U32, "h_c%d" % g) for g in range(groups)]
+        h_q = [held([P, S], U8, "h_q%d" % g) for g in range(groups)]
+
+        def magnitudes(g, j):
+            mag = ring.tile([P, PACK, HALF], F32, name="stage", align_bytes=64, bufs=3)
+            for t in range(PACK):
+                bank = psum_ab.tile([P, HALF], F32, name="bank")
+                for a in range(kpasses):
+                    c0 = a * H + g * PASS + t * P
+                    nc.tensor.matmul_mx(
+                        out=bank[:],
+                        lhsT=w1_wp[:, c0 : c0 + P].bitcast(FP4X4),
+                        lhsT_scale=w1_sp[:, c0 : c0 + P],
+                        rhs=v_w[a][j][:].bitcast(FP8X4),
+                        rhs_scale=v_s[a][:, j * HALF : (j + 1) * HALF],
+                        start=(a == 0),
+                        stop=(a == kpasses - 1),
+                    )
+                gain = emis2[:, g * PACK + t : g * PACK + t + 1]
+                if (g, j, t) in ABS_ON_VECTOR:
+                    twin = ring.tile([P, HALF], F32, name="twin", align_bytes=64)
+                    nc.vector.tensor_scalar(twin[:], bank[:], gain, -1.0, MULT, MULT)
+                    nc.vector.scalar_tensor_tensor(mag[:, t, :], bank[:], gain, twin[:], MULT, MAX)
+                else:
+                    nc.scalar.activation(mag[:, t, :], bank[:], ACT.Abs, scale=gain)
+            return mag
+
+        def channels(g, j, mag, widths):
+            first = 0
+            for width in widths:
+                cols = slice(first, first + width)
+                entries = slice(j * HALF + first, j * HALF + first + width)
+                first = first + width
+                root = ring.tile([P, PACK, width], F32, name="root", align_bytes=64)
+                nc.scalar.activation(root[:], mag[:, :, cols], ACT.Sqrt)
+                h_bf = ring.tile([P, width, PACK], BF16, name="h_bf", align_bytes=64)
+                nc.vector.tensor_tensor(
+                    h_bf[:].rearrange("p (c i) t -> p c t i", i=4),
+                    root[:].rearrange("p t (c i) -> p c t i", i=4),
+                    r_t[g][j][:, :, cols].rearrange("p t (c i) -> p c t i", i=4),
+                    MULT,
+                )
+                quantise(h_c[g][:, entries], h_q[g][:, entries], h_bf[:].rearrange("p n t -> p (n t)"))
+                if g == groups - 1:
+                    fluxes(entries, width)
+
+        def fluxes(entries, width):
+            tiles = HALF // width
+            for n0 in range(0, N // P, tiles):
+                acc = psum_out.tile([P, tiles, width], F32, name="acc")
+                for u in range(tiles):
+                    cols = slice((n0 + u) * P, (n0 + u + 1) * P)
+                    for g in range(groups):
+                        nc.tensor.matmul_mx(
+                            out=acc[:, u, :],
+                            lhsT=w3_c[g][:, cols].bitcast(FP8X4),
+                            lhsT_scale=w3_q[g][:, cols],
+                            rhs=h_c[g][:, entries].bitcast(FP8X4),
+                            rhs_scale=h_q[g][:, entries],
+                            start=(g == 0),
+                            stop=(g == groups - 1),
+                        )
+                res = ring.tile([P, tiles, width], F32, name="res", align_bytes=64, bufs=4)
+                if entries.stop > S - 2 * P:
+                    nc.scalar.copy(res[:], acc[:])
+                else:
+                    nc.vector.tensor_copy(res[:], acc[:])
+                rows = out[n0 * P : (n0 + tiles) * P, entries]
+                nc.sync.dma_start(rows.rearrange("(u p) j -> p u j", p=P), res[:])
+
+        for j in range(halves):
+            for g in range(groups):
+                mag = magnitudes(g, j)
+                if (g, j) == (0, 0):
+                    prepare_w3(1)
+                channels(g, j, mag, (256, 128, 128) if (g, j) == (groups - 1, halves - 1) else (HALF,) if (g, j) == (0, 1) else (256, 256))

@@ -23,8 +23,8 @@ PACK = 4
 PASS = P * PACK
 HALF = 512
 RUN = 8
-SQ_ON_VECTOR = {(1, 0, 0), (1, 0, 1), (1, 0, 2)}
-ABS_ON_VECTOR = {(0, 0, 2), (0, 0, 3)}
+SQ_ON_VECTOR = {(1, 0, 0), (1, 0, 1)}
+ABS_ON_VECTOR = set()
 
 
 def tile_list_asteroid_band_fluxes_kernel(
@@ -102,10 +102,10 @@ def tile_list_asteroid_band_fluxes_kernel(
         nc.sync.dma_start(tab2_w[:].bitcast(I32), tab2_words[0].bitcast(I32))
         nc.vector.tensor_copy(v2_rows[:], tab2_s[:].indirect(idx2[:]))
         spread(v2_s, v2_rows, P - 16)
-        nc.gpsimd.memset(tab_s[0 : P - 32, :].bitcast(I32), 0)
-        nc.gpsimd.memset(w1_s[:].bitcast(I32), 0)
+        nc.vector.memset(tab_s[0 : P - 32, :].bitcast(I32), 0)
+        nc.vector.memset(w1_s[:].bitcast(I32), 0)
         for a in range(kpasses):
-            nc.gpsimd.memset(v_s[a][:].bitcast(I32), 0)
+            nc.vector.memset(v_s[a][:].bitcast(I32), 0)
         nc.sync.dma_start(w2_raw[1][:], w2_rows[:, :, PASS : 2 * PASS])
         nc.sync.dma_start(idx[:], offs)
         nc.sync.dma_start(tab_s[P - 32 : P, :].bitcast(I32), tab_scales.rearrange("a q t -> (a q) t").bitcast(I32))
@@ -114,7 +114,6 @@ def tile_list_asteroid_band_fluxes_kernel(
             nc.sync.dma_start(emis_rows[g * PACK : (g + 1) * PACK, :].rearrange("t (b i) -> t b i", i=RUN), emis_runs[g])
         cast_w2(nc.scalar.copy, 0, 0, 8)
         cast_w2(nc.vector.tensor_copy, 0, 8, 16)
-        load_w3(0)
         nc.sync.dma_start(
             w1_w[:].bitcast(I32).rearrange("p (a c) -> p a c", a=kpasses),
             w1_words.bitcast(I32).rearrange("a p c -> p a c"),
@@ -177,9 +176,10 @@ def tile_list_asteroid_band_fluxes_kernel(
         quantise_w2(1)
         nc.vector.tensor_copy(v_rows[:], tab_s[:].indirect(idx[:]))
         side_b(1, 0)
-        for a in range(kpasses):
-            spread(v_s[a], v_rows, P - 32 + 16 * a)
+        spread(v_s[0], v_rows, P - 32)
         load_tab(1)
+        spread(v_s[1], v_rows, P - 16)
+        load_w3(0)
         load_w3(1)
         side_b(1, 1)
 
@@ -187,7 +187,6 @@ def tile_list_asteroid_band_fluxes_kernel(
         turned = psum_out.tile([P, P], F32, name="acc")
         nc.tensor.transpose(turned[:], emis_rows[:], ident[:])
         nc.scalar.activation(emis2[:], turned[:, 0 : groups * PACK], ACT.Square)
-        prepare_w3(0)
         w1_wp = held([P, kpasses * H], U16, "w1_wp")
         w1_sp = held([P, kpasses * H], U8, "w1_sp")
         for dst, src in ((w1_wp, w1_w), (w1_sp, w1_s)):
@@ -232,7 +231,7 @@ def tile_list_asteroid_band_fluxes_kernel(
                 cols = slice(first, first + width)
                 entries = slice(j * HALF + first, j * HALF + first + width)
                 first = first + width
-                root = ring.tile([P, PACK, width], F32, name="root", align_bytes=64)
+                root = ring.tile([P, PACK, width], F32, name="root", align_bytes=64, bufs=3)
                 nc.scalar.activation(root[:], mag[:, :, cols], ACT.Sqrt)
                 h_bf = ring.tile([P, width, PACK], BF16, name="h_bf", align_bytes=64)
                 nc.vector.tensor_tensor(
@@ -246,7 +245,7 @@ def tile_list_asteroid_band_fluxes_kernel(
                     fluxes(entries, width)
 
         def fluxes(entries, width):
-            tiles = HALF // width
+            tiles = min(2, HALF // width)
             for n0 in range(0, N // P, tiles):
                 acc = psum_out.tile([P, tiles, width], F32, name="acc")
                 for u in range(tiles):
@@ -262,7 +261,7 @@ def tile_list_asteroid_band_fluxes_kernel(
                             stop=(g == groups - 1),
                         )
                 res = ring.tile([P, tiles, width], F32, name="res", align_bytes=64, bufs=4)
-                if entries.stop > S - 2 * P:
+                if n0 + tiles == N // P or entries.stop == S - P:
                     nc.scalar.copy(res[:], acc[:])
                 else:
                     nc.vector.tensor_copy(res[:], acc[:])
@@ -273,5 +272,6 @@ def tile_list_asteroid_band_fluxes_kernel(
             for g in range(groups):
                 mag = magnitudes(g, j)
                 if (g, j) == (0, 0):
+                    prepare_w3(0)
                     prepare_w3(1)
-                channels(g, j, mag, (256, 128, 128) if (g, j) == (groups - 1, halves - 1) else (HALF,) if (g, j) == (0, 1) else (256, 256))
+                channels(g, j, mag, (256, 128, 128) if (g, j) == (groups - 1, halves - 1) else (256, 256) if (g, j) == (0, 0) else (HALF,))

@@ -23,8 +23,10 @@ PACK = 4
 PASS = P * PACK
 HALF = 512
 RUN = 8
-SQ_ON_VECTOR = {(1, 0, 0), (1, 0, 1)}
-ABS_ON_VECTOR = set()
+QUADS = 4
+SQUARES_ON_VECTOR = {(1, 0, 0), (1, 0, 1), (1, 1, 0)}
+MAGNITUDES_ON_VECTOR = {(0, 0, 0), (0, 0, 1)}
+FIRST_CASTS_ON_SCALAR = (1, 2)
 
 
 def tile_list_asteroid_band_fluxes_kernel(
@@ -49,144 +51,140 @@ def tile_list_asteroid_band_fluxes_kernel(
         tab_s = held([P, T], U8, "tab_s")
         w1_s = held([P, kpasses * H], U8, "w1_s")
         v2_s = held([P, S], U8, "v2_s")
-        v_s = [held([P, S], U8, "v_s%d" % a) for a in range(kpasses)]
+        v_s = held([P, kpasses * S], U8, "v_s")
         v2_rows = held([P, S], U8, "v2_rows")
         v_rows = held([P, S], U8, "v_rows")
+        tab2_w = held([P, T], U16, "tab2_w")
+        tab_w = [held([P, T], I32, "tab_w%d" % a) for a in range(kpasses)]
+        w1_w = held([P, kpasses * H], U16, "w1_w")
+        w_raw = [held([P, PACK, PASS], F32, "w_raw%d" % g) for g in range(groups)]
+        emis_rows = held([P, P], F32, "emis_rows")
+        ident = held([P, P], F32, "ident")
+        emis2 = held([P, groups * PACK], F32, "emis2")
 
         nc.vector.memset(tab2_s[0 : P - 16, :].bitcast(I32), 0)
         nc.vector.memset(v2_s[:].bitcast(I32), 0)
+        nc.vector.memset(tab_s[0 : P - 32, :].bitcast(I32), 0)
+        nc.vector.memset(w1_s[:].bitcast(I32), 0)
+        nc.vector.memset(v_s[:].bitcast(I32), 0)
         one = held([P, 1], F32, "one")
         warm = held([P, 1], F32, "warm")
         nc.gpsimd.memset(one[:], 1.0)
         nc.scalar.activation(warm[:], one[:], ACT.Abs_reciprocal_sqrt)
 
-        w2_raw = [ring.tile([P, PACK, PASS], F32, name="w_raw", align_bytes=64) for g in range(groups)]
-        w3_raw = [ring.tile([P, PACK, N], F32, name="w_raw", align_bytes=64) for g in range(groups)]
-        tab2_w = held([P, T], U16, "tab2_w")
-        tab_w = [held([P, T], I32, "tab_w%d" % a) for a in range(kpasses)]
-        w1_w = held([P, kpasses * H], U16, "w1_w")
-        emis_rows = held([P, P], F32, "emis_rows")
-        ident = held([P, P], F32, "ident")
         nc.gpsimd.memset(emis_rows[:], 0.0)
         make_identity(nc, ident[:])
 
-        w2_bf = [held([P, PACK, P // RUN, RUN, PACK], BF16, "w2_bf%d" % g) for g in range(groups)]
-        w2_c = [held([P, PASS], U32, "w2_c%d" % g) for g in range(groups)]
-        w2_q = [held([P, PASS], U8, "w2_q%d" % g) for g in range(groups)]
-        w3_bf = [held([P, N, PACK], BF16, "w3_bf%d" % g) for g in range(groups)]
-        w3_c = [held([P, N], U32, "w3_c%d" % g) for g in range(groups)]
-        w3_q = [held([P, N], U8, "w3_q%d" % g) for g in range(groups)]
-
-        def cast_w2(copy, g, b0, b1):
-            dst = w2_bf[g][:].rearrange("p t b i j -> p b t j i")
-            src = w2_raw[g][:].rearrange("p j (b t i) -> p b t j i", t=PACK, i=RUN)
-            copy(dst[:, b0:b1], src[:, b0:b1])
-
-        def load_w3(g):
-            rows = w3[g * PASS : (g + 1) * PASS, :].rearrange("(b t i) n -> t b i n", t=PACK, i=RUN)
-            for t in range(PACK):
-                nc.sync.dma_start(w3_raw[g][:, t, :], rows[t])
-
-        def load_tab(a):
-            nc.sync.dma_start(tab_w[a][:], tab_words[a].rearrange("p t i -> p (t i)").bitcast(I32))
-
         w2_rows = w2.rearrange("(p j) r -> p j r", j=PACK)
-        def spread(plane, rows, first):
-            for q in range(4):
-                src = rows[first + 4 * q : first + 4 * q + 4, :]
-                nc.sync.dma_start(plane[32 * q : 32 * q + 4, :].bitcast(I32), src.bitcast(I32))
-
         nc.sync.dma_start(idx2[:], offs2)
         nc.sync.dma_start(tab2_s[P - 16 : P, :].bitcast(I32), tab2_scales[0].bitcast(I32))
-        nc.sync.dma_start(w2_raw[0][:], w2_rows[:, :, 0:PASS])
         nc.sync.dma_start(tab2_w[:].bitcast(I32), tab2_words[0].bitcast(I32))
-        nc.vector.tensor_copy(v2_rows[:], tab2_s[:].indirect(idx2[:]))
-        spread(v2_s, v2_rows, P - 16)
-        nc.vector.memset(tab_s[0 : P - 32, :].bitcast(I32), 0)
-        nc.vector.memset(w1_s[:].bitcast(I32), 0)
-        for a in range(kpasses):
-            nc.vector.memset(v_s[a][:].bitcast(I32), 0)
-        nc.sync.dma_start(w2_raw[1][:], w2_rows[:, :, PASS : 2 * PASS])
+        nc.sync.dma_start(w_raw[0][:], w2_rows[:, :, 0:PASS])
         nc.sync.dma_start(idx[:], offs)
-        nc.sync.dma_start(tab_s[P - 32 : P, :].bitcast(I32), tab_scales.rearrange("a q t -> (a q) t").bitcast(I32))
-        emis_runs = emis.rearrange("(g b t i) -> g t b i", g=groups, t=PACK, i=RUN)
-        for g in range(groups):
-            nc.sync.dma_start(emis_rows[g * PACK : (g + 1) * PACK, :].rearrange("t (b i) -> t b i", i=RUN), emis_runs[g])
-        cast_w2(nc.scalar.copy, 0, 0, 8)
-        cast_w2(nc.vector.tensor_copy, 0, 8, 16)
-        nc.sync.dma_start(
-            w1_w[:].bitcast(I32).rearrange("p (a c) -> p a c", a=kpasses),
-            w1_words.bitcast(I32).rearrange("a p c -> p a c"),
-        )
-        for q in range(4):
+        nc.sync.dma_start(tab_s[P - 32 : P, :].bitcast(I32), tab_scales.rearrange("a q t -> q a t").bitcast(I32))
+        nc.sync.dma_start(w_raw[1][:], w2_rows[:, :, PASS : 2 * PASS])
+        for q in range(QUADS):
             nc.sync.dma_start(
                 w1_s[32 * q : 32 * q + 4, :].bitcast(I32).rearrange("p (a c) -> p a c", a=kpasses),
                 w1_scales[:, 4 * q : 4 * q + 4, :].bitcast(I32).rearrange("a r c -> r a c"),
             )
+        nc.sync.dma_start(
+            w1_w[:].bitcast(I32).rearrange("p (a c) -> p a c", a=kpasses),
+            w1_words.bitcast(I32).rearrange("a p c -> p a c"),
+        )
+
+        def load_tab(a):
+            nc.sync.dma_start(tab_w[a][:], tab_words[a].rearrange("p t i -> p (t i)").bitcast(I32))
+
         load_tab(0)
+
+        nc.vector.tensor_copy(v2_rows[:], tab2_s[:].indirect(idx2[:]))
+        for q in range(QUADS):
+            src = v2_rows[P - 16 + 4 * q : P - 12 + 4 * q, :]
+            nc.scalar.dma_start(v2_s[32 * q : 32 * q + 4, :].bitcast(I32), src.bitcast(I32))
 
         def picks(offsets, j):
             return offsets[:, j * (HALF // 16) : (j + 1) * (HALF // 16)]
 
         v2_w = [held([P, HALF], U16, "v2_w%d" % j) for j in range(halves)]
         v_w = [[held([P, HALF], U32, "v_w%d_%d" % (a, j)) for j in range(halves)] for a in range(kpasses)]
+        for j in range(halves):
+            nc.vector.tensor_copy(v2_w[j][:], tab2_w[:].indirect(picks(idx2, j)))
 
         def quantise(codes, scales, values):
             nc.vector.quantize_mx(out=codes.bitcast(FP8X4), scales=scales, in_=values)
 
-        def quantise_w2(g):
-            quantise(w2_c[g][:], w2_q[g][:], w2_bf[g][:].rearrange("p t b i j -> p (t b i j)"))
+        staged = [held([P, PASS * PACK], BF16, "staged%d" % u) for u in range(2)]
+        first_bf = [held([P, PASS], BF16, "first_bf%d" % t) for t in range(PACK)]
+        w2_c = [held([P, PASS], U32, "w2_c%d" % g) for g in range(groups)]
+        w2_q = [held([P, PASS], U8, "w2_q%d" % g) for g in range(groups)]
+        w3_c = [held([P, N], U32, "w3_c%d" % g) for g in range(groups)]
+        w3_q = [held([P, N], U8, "w3_q%d" % g) for g in range(groups)]
 
-        def prepare_w3(g):
-            nc.vector.tensor_copy(
-                w3_bf[g][:].rearrange("p (c i) j -> p c j i", i=4), w3_raw[g][:].rearrange("p j (c i) -> p c j i", i=4)
+        for t in range(PACK):
+            copy = nc.scalar.copy if t in FIRST_CASTS_ON_SCALAR else nc.vector.tensor_copy
+            copy(
+                first_bf[t][:].rearrange("p (b i j) -> p b j i", i=RUN, j=PACK),
+                w_raw[0][:].rearrange("p j (b t i) -> p t b j i", t=PACK, i=RUN)[:, t],
             )
-            quantise(w3_c[g][:], w3_q[g][:], w3_bf[g][:].rearrange("p n j -> p (n j)"))
+        for t in range(PACK):
+            cols = slice(t * P, (t + 1) * P)
+            quantise(w2_c[0][:, cols], w2_q[0][:, cols], first_bf[t][:])
 
-        r_t = [[held([P, PACK, HALF], F32, "r_%d_%d" % (g, j)) for j in range(halves)] for g in range(groups)]
+        damp = [[held([P, PACK, HALF], F32, "damp%d_%d" % (g, j)) for j in range(halves)] for g in range(groups)]
 
-        def side_b(g, j):
-            sq = ring.tile([P, PACK, HALF], F32, name="stage", align_bytes=64, bufs=3)
+        def product_b(g, j, t, pool, name):
+            cols = slice(t * P, (t + 1) * P)
+            bank = pool.tile([P, HALF], F32, name=name)
+            nc.tensor.matmul_mx(
+                out=bank[:],
+                lhsT=w2_c[g][:, cols].bitcast(FP8X4),
+                lhsT_scale=w2_q[g][:, cols],
+                rhs=v2_w[j][:].bitcast(FP4X4),
+                rhs_scale=v2_s[:, j * HALF : (j + 1) * HALF],
+                start=True,
+                stop=True,
+            )
+            return bank
+
+        def squares_on_vector(g, j):
             for t in range(PACK):
-                cols = slice(t * P, (t + 1) * P)
-                bank = psum_ab.tile([P, HALF], F32, name="bank")
-                nc.tensor.matmul_mx(
-                    out=bank[:],
-                    lhsT=w2_c[g][:, cols].bitcast(FP8X4),
-                    lhsT_scale=w2_q[g][:, cols],
-                    rhs=v2_w[j][:].bitcast(FP4X4),
-                    rhs_scale=v2_s[:, j * HALF : (j + 1) * HALF],
-                    start=True,
-                    stop=True,
-                )
-                if (g, j, t) in SQ_ON_VECTOR:
+                if (g, j, t) in SQUARES_ON_VECTOR:
+                    bank = product_b(g, j, t, psum_out, "acc")
                     twin = ring.tile([P, HALF], F32, name="twin", align_bytes=64)
                     nc.vector.tensor_copy(twin[:], bank[:])
-                    nc.vector.tensor_tensor(sq[:, t, :], bank[:], twin[:], MULT)
-                else:
-                    nc.scalar.activation(sq[:, t, :], bank[:], ACT.Square)
-            nc.scalar.activation(r_t[g][j][:], sq[:], ACT.Abs_reciprocal_sqrt, bias=1.0)
+                    nc.vector.tensor_tensor(damp[g][j][:, t, :], bank[:], twin[:], MULT)
 
-        quantise_w2(0)
-        nc.vector.tensor_copy(v2_w[0][:], tab2_w[:].indirect(picks(idx2, 0)))
+        def side_b(g, j):
+            for t in range(PACK):
+                if (g, j, t) not in SQUARES_ON_VECTOR:
+                    bank = product_b(g, j, t, psum_ab, "bank")
+                    nc.scalar.activation(damp[g][j][:, t, :], bank[:], ACT.Square)
+            nc.scalar.activation(damp[g][j][:], damp[g][j][:], ACT.Abs_reciprocal_sqrt, bias=1.0)
+
         side_b(0, 0)
-        nc.vector.tensor_copy(v2_w[1][:], tab2_w[:].indirect(picks(idx2, 1)))
         side_b(0, 1)
-        cast_w2(nc.vector.tensor_copy, 1, 0, 16)
-        quantise_w2(1)
         nc.vector.tensor_copy(v_rows[:], tab_s[:].indirect(idx[:]))
-        side_b(1, 0)
-        spread(v_s[0], v_rows, P - 32)
+        for q in range(QUADS):
+            src = v_rows[P - 32 + 8 * q : P - 24 + 8 * q, :]
+            nc.sync.dma_start(v_s[32 * q : 32 * q + 4, :].bitcast(I32), src.bitcast(I32))
         load_tab(1)
-        spread(v_s[1], v_rows, P - 16)
-        load_w3(0)
-        load_w3(1)
-        side_b(1, 1)
+        emis_runs = emis.rearrange("(g b t i) -> g t b i", g=groups, t=PACK, i=RUN)
+        for g in range(groups):
+            nc.sync.dma_start(emis_rows[g * PACK : (g + 1) * PACK, :].rearrange("t (b i) -> t b i", i=RUN), emis_runs[g])
 
-        emis2 = held([P, groups * PACK], F32, "emis2")
-        turned = psum_out.tile([P, P], F32, name="acc")
-        nc.tensor.transpose(turned[:], emis_rows[:], ident[:])
-        nc.scalar.activation(emis2[:], turned[:, 0 : groups * PACK], ACT.Square)
+        nc.vector.tensor_copy(
+            staged[1][:].rearrange("p (t b i j) -> p b t j i", t=PACK, i=RUN, j=PACK),
+            w_raw[1][:].rearrange("p j (b t i) -> p b t j i", t=PACK, i=RUN),
+        )
+        quantise(w2_c[1][:], w2_q[1][:], staged[1][:])
+        for g in range(groups):
+            rows = w3[g * PASS : (g + 1) * PASS, :].rearrange("(b t i) n -> t b i n", t=PACK, i=RUN)
+            for t in range(PACK):
+                nc.sync.dma_start(w_raw[g][:, t, :], rows[t])
+
+        for j in range(halves):
+            squares_on_vector(1, j)
         w1_wp = held([P, kpasses * H], U16, "w1_wp")
         w1_sp = held([P, kpasses * H], U8, "w1_sp")
         for dst, src in ((w1_wp, w1_w), (w1_sp, w1_s)):
@@ -194,55 +192,48 @@ def tile_list_asteroid_band_fluxes_kernel(
                 dst[:].bitcast(I32).rearrange("p (g t b w) -> p g b t w", t=PACK, b=P // RUN, g=kpasses * groups),
                 src[:].bitcast(I32).rearrange("p (g b t w) -> p g b t w", t=PACK, b=P // RUN, g=kpasses * groups),
             )
+        side_b(1, 0)
+        side_b(1, 1)
         for a in range(kpasses):
             for j in range(halves):
                 nc.vector.tensor_copy(v_w[a][j][:], tab_w[a][:].bitcast(U32).indirect(picks(idx, j)))
+        turned = psum_out.tile([P, P], F32, name="acc")
+        nc.tensor.transpose(turned[:], emis_rows[:], ident[:])
+        nc.scalar.activation(emis2[:], turned[:, 0 : groups * PACK], ACT.Square)
 
         h_c = [held([P, S], U32, "h_c%d" % g) for g in range(groups)]
         h_q = [held([P, S], U8, "h_q%d" % g) for g in range(groups)]
+        roots = [held([P, PACK, HALF], F32, "root%d" % u) for u in range(3)]
 
-        def magnitudes(g, j):
-            mag = ring.tile([P, PACK, HALF], F32, name="stage", align_bytes=64, bufs=3)
+        def magnitudes(g, j, mag):
             for t in range(PACK):
                 bank = psum_ab.tile([P, HALF], F32, name="bank")
                 for a in range(kpasses):
                     c0 = a * H + g * PASS + t * P
+                    s0 = a * S + j * HALF
                     nc.tensor.matmul_mx(
                         out=bank[:],
                         lhsT=w1_wp[:, c0 : c0 + P].bitcast(FP4X4),
                         lhsT_scale=w1_sp[:, c0 : c0 + P],
                         rhs=v_w[a][j][:].bitcast(FP8X4),
-                        rhs_scale=v_s[a][:, j * HALF : (j + 1) * HALF],
+                        rhs_scale=v_s[:, s0 : s0 + HALF],
                         start=(a == 0),
                         stop=(a == kpasses - 1),
                     )
                 gain = emis2[:, g * PACK + t : g * PACK + t + 1]
-                if (g, j, t) in ABS_ON_VECTOR:
+                if (g, j, t) in MAGNITUDES_ON_VECTOR:
                     twin = ring.tile([P, HALF], F32, name="twin", align_bytes=64)
                     nc.vector.tensor_scalar(twin[:], bank[:], gain, -1.0, MULT, MULT)
                     nc.vector.scalar_tensor_tensor(mag[:, t, :], bank[:], gain, twin[:], MULT, MAX)
                 else:
                     nc.scalar.activation(mag[:, t, :], bank[:], ACT.Abs, scale=gain)
-            return mag
 
-        def channels(g, j, mag, widths):
-            first = 0
-            for width in widths:
-                cols = slice(first, first + width)
-                entries = slice(j * HALF + first, j * HALF + first + width)
-                first = first + width
-                root = ring.tile([P, PACK, width], F32, name="root", align_bytes=64, bufs=3)
-                nc.scalar.activation(root[:], mag[:, :, cols], ACT.Sqrt)
-                h_bf = ring.tile([P, width, PACK], BF16, name="h_bf", align_bytes=64)
-                nc.vector.tensor_tensor(
-                    h_bf[:].rearrange("p (c i) t -> p c t i", i=4),
-                    root[:].rearrange("p t (c i) -> p c t i", i=4),
-                    r_t[g][j][:, :, cols].rearrange("p t (c i) -> p c t i", i=4),
-                    MULT,
-                )
-                quantise(h_c[g][:, entries], h_q[g][:, entries], h_bf[:].rearrange("p n t -> p (n t)"))
-                if g == groups - 1:
-                    fluxes(entries, width)
+        def prepare_w3(g):
+            nc.vector.tensor_copy(
+                staged[g][:].rearrange("p (c i j) -> p c j i", i=4, j=PACK),
+                w_raw[g][:].rearrange("p j (c i) -> p c j i", i=4),
+            )
+            quantise(w3_c[g][:], w3_q[g][:], staged[g][:])
 
         def fluxes(entries, width):
             tiles = min(2, HALF // width)
@@ -261,17 +252,37 @@ def tile_list_asteroid_band_fluxes_kernel(
                             stop=(g == groups - 1),
                         )
                 res = ring.tile([P, tiles, width], F32, name="res", align_bytes=64, bufs=4)
-                if n0 + tiles == N // P or entries.stop == S - P:
+                if entries.stop > S - 2 * P and n0 + tiles == N // P:
                     nc.scalar.copy(res[:], acc[:])
                 else:
                     nc.vector.tensor_copy(res[:], acc[:])
                 rows = out[n0 * P : (n0 + tiles) * P, entries]
                 nc.sync.dma_start(rows.rearrange("(u p) j -> p u j", p=P), res[:])
 
+        def channels(g, j, mag, stage, widths):
+            first = 0
+            for width in widths:
+                cols = slice(first, first + width)
+                entries = slice(j * HALF + first, j * HALF + first + width)
+                h_bf = stage[:, first * PACK : (first + width) * PACK]
+                first = first + width
+                nc.scalar.activation(mag[:, :, cols], mag[:, :, cols], ACT.Sqrt)
+                nc.vector.tensor_tensor(
+                    h_bf.rearrange("p (c i t) -> p c t i", i=4, t=PACK),
+                    mag[:, :, cols].rearrange("p t (c i) -> p c t i", i=4),
+                    damp[g][j][:, :, cols].rearrange("p t (c i) -> p c t i", i=4),
+                    MULT,
+                )
+                quantise(h_c[g][:, entries], h_q[g][:, entries], h_bf)
+                if g == groups - 1:
+                    fluxes(entries, width)
+
         for j in range(halves):
             for g in range(groups):
-                mag = magnitudes(g, j)
+                mag = roots[(j * groups + g) % len(roots)]
+                magnitudes(g, j, mag)
                 if (g, j) == (0, 0):
                     prepare_w3(0)
                     prepare_w3(1)
-                channels(g, j, mag, (256, 128, 128) if (g, j) == (groups - 1, halves - 1) else (256, 256) if (g, j) == (0, 0) else (HALF,))
+                last = (g, j) == (groups - 1, halves - 1)
+                channels(g, j, mag, staged[g], (256, 128, 128) if last else (256, 256) if (g, j) == (0, 0) else (HALF,))

@@ -24,8 +24,8 @@ PASS = P * PACK
 HALF = 512
 RUN = 8
 QUADS = 4
-SQUARES_ON_VECTOR = {(1, 0, 0), (1, 0, 1), (1, 1, 0)}
-MAGNITUDES_ON_VECTOR = {(0, 0, 0), (0, 0, 1)}
+SQUARES_ON_VECTOR = {(1, 0, 0), (1, 0, 1)}
+MAGNITUDES_ON_VECTOR = {(0, 0, 0), (1, 0, 0)}
 FIRST_CASTS_ON_SCALAR = (1, 2)
 
 
@@ -64,9 +64,9 @@ def tile_list_asteroid_band_fluxes_kernel(
 
         nc.vector.memset(tab2_s[0 : P - 16, :].bitcast(I32), 0)
         nc.vector.memset(v2_s[:].bitcast(I32), 0)
-        nc.vector.memset(tab_s[0 : P - 32, :].bitcast(I32), 0)
-        nc.vector.memset(w1_s[:].bitcast(I32), 0)
-        nc.vector.memset(v_s[:].bitcast(I32), 0)
+        nc.gpsimd.memset(tab_s[0 : P - 32, :].bitcast(I32), 0)
+        nc.gpsimd.memset(w1_s[:].bitcast(I32), 0)
+        nc.gpsimd.memset(v_s[:].bitcast(I32), 0)
         one = held([P, 1], F32, "one")
         warm = held([P, 1], F32, "warm")
         nc.gpsimd.memset(one[:], 1.0)
@@ -82,6 +82,10 @@ def tile_list_asteroid_band_fluxes_kernel(
         nc.sync.dma_start(w_raw[0][:], w2_rows[:, :, 0:PASS])
         nc.sync.dma_start(idx[:], offs)
         nc.sync.dma_start(tab_s[P - 32 : P, :].bitcast(I32), tab_scales.rearrange("a q t -> q a t").bitcast(I32))
+        nc.vector.tensor_copy(v2_rows[:], tab2_s[:].indirect(idx2[:]))
+        for q in range(QUADS):
+            src = v2_rows[P - 16 + 4 * q : P - 12 + 4 * q, :]
+            nc.sync.dma_start(v2_s[32 * q : 32 * q + 4, :].bitcast(I32), src.bitcast(I32))
         nc.sync.dma_start(w_raw[1][:], w2_rows[:, :, PASS : 2 * PASS])
         for q in range(QUADS):
             nc.sync.dma_start(
@@ -98,10 +102,6 @@ def tile_list_asteroid_band_fluxes_kernel(
 
         load_tab(0)
 
-        nc.vector.tensor_copy(v2_rows[:], tab2_s[:].indirect(idx2[:]))
-        for q in range(QUADS):
-            src = v2_rows[P - 16 + 4 * q : P - 12 + 4 * q, :]
-            nc.scalar.dma_start(v2_s[32 * q : 32 * q + 4, :].bitcast(I32), src.bitcast(I32))
 
         def picks(offsets, j):
             return offsets[:, j * (HALF // 16) : (j + 1) * (HALF // 16)]
@@ -235,29 +235,43 @@ def tile_list_asteroid_band_fluxes_kernel(
             )
             quantise(w3_c[g][:], w3_q[g][:], staged[g][:])
 
-        def fluxes(entries, width):
-            tiles = min(2, HALF // width)
-            for n0 in range(0, N // P, tiles):
-                acc = psum_out.tile([P, tiles, width], F32, name="acc")
-                for u in range(tiles):
-                    cols = slice((n0 + u) * P, (n0 + u + 1) * P)
-                    for g in range(groups):
-                        nc.tensor.matmul_mx(
-                            out=acc[:, u, :],
-                            lhsT=w3_c[g][:, cols].bitcast(FP8X4),
-                            lhsT_scale=w3_q[g][:, cols],
-                            rhs=h_c[g][:, entries].bitcast(FP8X4),
-                            rhs_scale=h_q[g][:, entries],
-                            start=(g == 0),
-                            stop=(g == groups - 1),
-                        )
-                res = ring.tile([P, tiles, width], F32, name="res", align_bytes=64, bufs=4)
-                if entries.stop > S - 2 * P and n0 + tiles == N // P:
+        def flux_pass(acc, n0, entries, g):
+            tiles = acc.shape[1]
+            for u in range(tiles):
+                cols = slice((n0 + u) * P, (n0 + u + 1) * P)
+                nc.tensor.matmul_mx(
+                    out=acc[:, u, :],
+                    lhsT=w3_c[g][:, cols].bitcast(FP8X4),
+                    lhsT_scale=w3_q[g][:, cols],
+                    rhs=h_c[g][:, entries].bitcast(FP8X4),
+                    rhs_scale=h_q[g][:, entries],
+                    start=(g == 0 and u == 0),
+                    stop=(g == groups - 1 and u == tiles - 1),
+                )
+
+        def open_fluxes(entries, width):
+            late = entries.start >= S - 2 * P
+            accs = []
+            for n0 in range(0, N // P, 2):
+                if late:
+                    acc = psum_ab.tile([P, 2, width], F32, name="bank")
+                else:
+                    acc = psum_out.tile([P, 2, width], F32, name="acc")
+                flux_pass(acc, n0, entries, 0)
+                accs.append(acc)
+            return accs
+
+        def close_fluxes(accs, entries, width):
+            for n0 in range(0, N // P, 2):
+                acc = accs[n0 // 2]
+                flux_pass(acc, n0, entries, 1)
+                res = ring.tile([P, 2, width], F32, name="res", align_bytes=64, bufs=6)
+                rows = out[n0 * P : (n0 + 2) * P, entries].rearrange("(u p) j -> p u j", p=P)
+                if entries.stop > HALF and (n0 > 0 or entries.stop == S - P):
                     nc.scalar.copy(res[:], acc[:])
                 else:
                     nc.vector.tensor_copy(res[:], acc[:])
-                rows = out[n0 * P : (n0 + tiles) * P, entries]
-                nc.sync.dma_start(rows.rearrange("(u p) j -> p u j", p=P), res[:])
+                nc.sync.dma_start(rows, res[:])
 
         def channels(g, j, mag, stage, widths):
             first = 0
@@ -266,6 +280,8 @@ def tile_list_asteroid_band_fluxes_kernel(
                 entries = slice(j * HALF + first, j * HALF + first + width)
                 h_bf = stage[:, first * PACK : (first + width) * PACK]
                 first = first + width
+                if g == groups - 1:
+                    accs = open_fluxes(entries, width)
                 nc.scalar.activation(mag[:, :, cols], mag[:, :, cols], ACT.Sqrt)
                 nc.vector.tensor_tensor(
                     h_bf.rearrange("p (c i t) -> p c t i", i=4, t=PACK),
@@ -275,7 +291,7 @@ def tile_list_asteroid_band_fluxes_kernel(
                 )
                 quantise(h_c[g][:, entries], h_q[g][:, entries], h_bf)
                 if g == groups - 1:
-                    fluxes(entries, width)
+                    close_fluxes(accs, entries, width)
 
         for j in range(halves):
             for g in range(groups):
@@ -285,4 +301,4 @@ def tile_list_asteroid_band_fluxes_kernel(
                     prepare_w3(0)
                     prepare_w3(1)
                 last = (g, j) == (groups - 1, halves - 1)
-                channels(g, j, mag, staged[g], (256, 128, 128) if last else (256, 256) if (g, j) == (0, 0) else (HALF,))
+                channels(g, j, mag, staged[g], (256, 128, 128) if last else (256, 256))

@@ -17,6 +17,7 @@ FP4X4 = mybir.dt.float4_e2m1fn_x4
 ACT = mybir.ActivationFunctionType
 MULT = mybir.AluOpType.mult
 MAX = mybir.AluOpType.max
+ADD = mybir.AluOpType.add
 
 P = 128
 PACK = 4
@@ -24,8 +25,10 @@ PASS = P * PACK
 HALF = 512
 RUN = 8
 QUADS = 4
-SQUARES_ON_VECTOR = {(1, 0, 0), (1, 0, 1)}
-MAGNITUDES_ON_VECTOR = {(0, 0, 0), (1, 0, 0)}
+SQUARES_ON_VECTOR = set()
+MAGNITUDES_ON_VECTOR = set()
+ONE_ROOT = {(0, 0)}
+TINY = 1e-36
 FIRST_CASTS_ON_SCALAR = (1, 2)
 
 
@@ -160,7 +163,8 @@ def tile_list_asteroid_band_fluxes_kernel(
                 if (g, j, t) not in SQUARES_ON_VECTOR:
                     bank = product_b(g, j, t, psum_ab, "bank")
                     nc.scalar.activation(damp[g][j][:, t, :], bank[:], ACT.Square)
-            nc.scalar.activation(damp[g][j][:], damp[g][j][:], ACT.Abs_reciprocal_sqrt, bias=1.0)
+            if (g, j) not in ONE_ROOT:
+                nc.scalar.activation(damp[g][j][:], damp[g][j][:], ACT.Abs_reciprocal_sqrt, bias=1.0)
 
         side_b(0, 0)
         side_b(0, 1)
@@ -173,11 +177,14 @@ def tile_list_asteroid_band_fluxes_kernel(
         for g in range(groups):
             nc.sync.dma_start(emis_rows[g * PACK : (g + 1) * PACK, :].rearrange("t (b i) -> t b i", i=RUN), emis_runs[g])
 
-        nc.vector.tensor_copy(
-            staged[1][:].rearrange("p (t b i j) -> p b t j i", t=PACK, i=RUN, j=PACK),
-            w_raw[1][:].rearrange("p j (b t i) -> p b t j i", t=PACK, i=RUN),
-        )
-        quantise(w2_c[1][:], w2_q[1][:], staged[1][:])
+        for u in range(2):
+            nc.vector.tensor_copy(
+                staged[1][:].rearrange("p (t b i j) -> p b t j i", t=PACK, i=RUN, j=PACK)[:, :, 2 * u : 2 * u + 2],
+                w_raw[1][:].rearrange("p j (b t i) -> p b t j i", t=PACK, i=RUN)[:, :, 2 * u : 2 * u + 2],
+            )
+        for u in range(2):
+            cols = slice(2 * u * P, (2 * u + 2) * P)
+            quantise(w2_c[1][:, cols], w2_q[1][:, cols], staged[1][:, cols.start * PACK : cols.stop * PACK])
         for g in range(groups):
             rows = w3[g * PASS : (g + 1) * PASS, :].rearrange("(b t i) n -> t b i n", t=PACK, i=RUN)
             for t in range(PACK):
@@ -229,11 +236,14 @@ def tile_list_asteroid_band_fluxes_kernel(
                     nc.scalar.activation(mag[:, t, :], bank[:], ACT.Abs, scale=gain)
 
         def prepare_w3(g):
-            nc.vector.tensor_copy(
-                staged[g][:].rearrange("p (c i j) -> p c j i", i=4, j=PACK),
-                w_raw[g][:].rearrange("p j (c i) -> p c j i", i=4),
-            )
-            quantise(w3_c[g][:], w3_q[g][:], staged[g][:])
+            for u in range(2):
+                nc.vector.tensor_copy(
+                    staged[g][:].rearrange("p (c i j) -> p c j i", i=4, j=PACK)[:, 64 * u : 64 * u + 64],
+                    w_raw[g][:].rearrange("p j (c i) -> p c j i", i=4)[:, 64 * u : 64 * u + 64],
+                )
+            for u in range(2):
+                cols = slice(2 * u * P, (2 * u + 2) * P)
+                quantise(w3_c[g][:, cols], w3_q[g][:, cols], staged[g][:, cols.start * PACK : cols.stop * PACK])
 
         def flux_pass(acc, n0, entries, g):
             tiles = acc.shape[1]
@@ -273,32 +283,48 @@ def tile_list_asteroid_band_fluxes_kernel(
                     nc.vector.tensor_copy(res[:], acc[:])
                 nc.sync.dma_start(rows, res[:])
 
-        def channels(g, j, mag, stage, widths):
-            first = 0
-            for width in widths:
-                cols = slice(first, first + width)
-                entries = slice(j * HALF + first, j * HALF + first + width)
-                h_bf = stage[:, first * PACK : (first + width) * PACK]
-                first = first + width
-                if g == groups - 1:
-                    accs = open_fluxes(entries, width)
+        def weave(g, j, mag, first, width):
+            cols = slice(first, first + width)
+            entries = slice(j * HALF + first, j * HALF + first + width)
+            h_bf = staged[g][:, first * PACK : (first + width) * PACK]
+            accs = open_fluxes(entries, width) if g == groups - 1 else None
+            if (g, j) not in ONE_ROOT:
                 nc.scalar.activation(mag[:, :, cols], mag[:, :, cols], ACT.Sqrt)
-                nc.vector.tensor_tensor(
-                    h_bf.rearrange("p (c i t) -> p c t i", i=4, t=PACK),
-                    mag[:, :, cols].rearrange("p t (c i) -> p c t i", i=4),
-                    damp[g][j][:, :, cols].rearrange("p t (c i) -> p c t i", i=4),
-                    MULT,
-                )
-                quantise(h_c[g][:, entries], h_q[g][:, entries], h_bf)
-                if g == groups - 1:
-                    close_fluxes(accs, entries, width)
+            nc.vector.tensor_tensor(
+                h_bf.rearrange("p (c i t) -> p c t i", i=4, t=PACK),
+                mag[:, :, cols].rearrange("p t (c i) -> p c t i", i=4),
+                damp[g][j][:, :, cols].rearrange("p t (c i) -> p c t i", i=4),
+                MULT,
+            )
+            return g, entries, width, h_bf, accs
 
+        def finish(g, entries, width, h_bf, accs):
+            quantise(h_c[g][:, entries], h_q[g][:, entries], h_bf)
+            if g == groups - 1:
+                close_fluxes(accs, entries, width)
+
+        waiting = None
         for j in range(halves):
             for g in range(groups):
                 mag = roots[(j * groups + g) % len(roots)]
                 magnitudes(g, j, mag)
+                if (g, j) in ONE_ROOT:
+                    for first in range(0, HALF, 256):
+                        part = damp[g][j][:, :, first : first + 256]
+                        nc.vector.scalar_tensor_tensor(part, part, 1.0, mag[:, :, first : first + 256], ADD, MULT)
+                        nc.scalar.activation(part, part, ACT.Abs_reciprocal_sqrt, bias=TINY)
                 if (g, j) == (0, 0):
                     prepare_w3(0)
                     prepare_w3(1)
                 last = (g, j) == (groups - 1, halves - 1)
-                channels(g, j, mag, staged[g], (256, 128, 128) if last else (256, 256))
+                first = 0
+                for width in (256, 128, 128) if last else (256, 256):
+                    if waiting is not None and g == groups - 1 and first == 0:
+                        finish(*waiting)
+                        waiting = None
+                    woven = weave(g, j, mag, first, width)
+                    if waiting is not None:
+                        finish(*waiting)
+                    waiting = woven
+                    first = first + width
+        finish(*waiting)

@@ -25,8 +25,7 @@ PASS = P * PACK
 HALF = 512
 RUN = 8
 QUADS = 4
-SQUARES_ON_VECTOR = set()
-MAGNITUDES_ON_VECTOR = set()
+SQUARES_ON_VECTOR = {(1, 0, 0), (1, 0, 1)}
 ONE_ROOT = {(0, 0)}
 TINY = 1e-36
 FIRST_CASTS_ON_SCALAR = (1, 2)
@@ -42,8 +41,8 @@ def tile_list_asteroid_band_fluxes_kernel(
     with ExitStack() as ctx:
         keep = ctx.enter_context(tc.tile_pool(name="keep", bufs=1))
         ring = ctx.enter_context(tc.tile_pool(name="ring", bufs=2))
-        psum_ab = ctx.enter_context(tc.psum_pool(name="psum_ab", bufs=6))
-        psum_out = ctx.enter_context(tc.psum_pool(name="psum_out", bufs=2))
+        psum_ab = ctx.enter_context(tc.psum_pool(name="psum_ab", bufs=5))
+        psum_out = ctx.enter_context(tc.psum_pool(name="psum_out", bufs=3))
 
         def held(shape, dtype, name):
             return keep.tile(shape, dtype, name=name, align_bytes=64)
@@ -59,7 +58,7 @@ def tile_list_asteroid_band_fluxes_kernel(
         v_rows = held([P, S], U8, "v_rows")
         tab2_w = held([P, T], U16, "tab2_w")
         tab_w = [held([P, T], I32, "tab_w%d" % a) for a in range(kpasses)]
-        w1_w = held([P, kpasses * H], U16, "w1_w")
+        w1_w = [held([P, kpasses * PASS], U16, "w1_w%d" % g) for g in range(groups)]
         w_raw = [held([P, PACK, PASS], F32, "w_raw%d" % g) for g in range(groups)]
         emis_rows = held([P, P], F32, "emis_rows")
         ident = held([P, P], F32, "ident")
@@ -95,10 +94,14 @@ def tile_list_asteroid_band_fluxes_kernel(
                 w1_s[32 * q : 32 * q + 4, :].bitcast(I32).rearrange("p (a c) -> p a c", a=kpasses),
                 w1_scales[:, 4 * q : 4 * q + 4, :].bitcast(I32).rearrange("a r c -> r a c"),
             )
-        nc.sync.dma_start(
-            w1_w[:].bitcast(I32).rearrange("p (a c) -> p a c", a=kpasses),
-            w1_words.bitcast(I32).rearrange("a p c -> p a c"),
-        )
+
+        def load_w1(g):
+            nc.sync.dma_start(
+                w1_w[g][:].bitcast(I32).rearrange("p (a c) -> p a c", a=kpasses),
+                w1_words.bitcast(I32).rearrange("a p (g c) -> g p a c", g=groups)[g],
+            )
+
+        load_w1(0)
 
         def load_tab(a):
             nc.sync.dma_start(tab_w[a][:], tab_words[a].rearrange("p t i -> p (t i)").bitcast(I32))
@@ -117,22 +120,28 @@ def tile_list_asteroid_band_fluxes_kernel(
         def quantise(codes, scales, values):
             nc.vector.quantize_mx(out=codes.bitcast(FP8X4), scales=scales, in_=values)
 
-        staged = [held([P, PASS * PACK], BF16, "staged%d" % u) for u in range(2)]
+        staged = [held([P, PASS * PACK], BF16, "staged%d" % u) for u in range(3)]
         first_bf = [held([P, PASS], BF16, "first_bf%d" % t) for t in range(PACK)]
         w2_c = [held([P, PASS], U32, "w2_c%d" % g) for g in range(groups)]
         w2_q = [held([P, PASS], U8, "w2_q%d" % g) for g in range(groups)]
         w3_c = [held([P, N], U32, "w3_c%d" % g) for g in range(groups)]
         w3_q = [held([P, N], U8, "w3_q%d" % g) for g in range(groups)]
 
-        for t in range(PACK):
+        def round_first(t):
             copy = nc.scalar.copy if t in FIRST_CASTS_ON_SCALAR else nc.vector.tensor_copy
             copy(
                 first_bf[t][:].rearrange("p (b i j) -> p b j i", i=RUN, j=PACK),
                 w_raw[0][:].rearrange("p j (b t i) -> p t b j i", t=PACK, i=RUN)[:, t],
             )
-        for t in range(PACK):
+
+        def quantise_first(t):
             cols = slice(t * P, (t + 1) * P)
             quantise(w2_c[0][:, cols], w2_q[0][:, cols], first_bf[t][:])
+
+        for t in range(PACK):
+            round_first(t)
+        for t in range(PACK):
+            quantise_first(t)
 
         damp = [[held([P, PACK, HALF], F32, "damp%d_%d" % (g, j)) for j in range(halves)] for g in range(groups)]
 
@@ -151,12 +160,15 @@ def tile_list_asteroid_band_fluxes_kernel(
             return bank
 
         def squares_on_vector(g, j):
+            taken = []
             for t in range(PACK):
                 if (g, j, t) in SQUARES_ON_VECTOR:
                     bank = product_b(g, j, t, psum_out, "acc")
                     twin = ring.tile([P, HALF], F32, name="twin", align_bytes=64)
                     nc.vector.tensor_copy(twin[:], bank[:])
-                    nc.vector.tensor_tensor(damp[g][j][:, t, :], bank[:], twin[:], MULT)
+                    taken.append((t, bank, twin))
+            for t, bank, twin in taken:
+                nc.vector.tensor_tensor(damp[g][j][:, t, :], bank[:], twin[:], MULT)
 
         def side_b(g, j):
             for t in range(PACK):
@@ -172,10 +184,11 @@ def tile_list_asteroid_band_fluxes_kernel(
         for q in range(QUADS):
             src = v_rows[P - 32 + 8 * q : P - 24 + 8 * q, :]
             nc.sync.dma_start(v_s[32 * q : 32 * q + 4, :].bitcast(I32), src.bitcast(I32))
-        load_tab(1)
         emis_runs = emis.rearrange("(g b t i) -> g t b i", g=groups, t=PACK, i=RUN)
         for g in range(groups):
             nc.sync.dma_start(emis_rows[g * PACK : (g + 1) * PACK, :].rearrange("t (b i) -> t b i", i=RUN), emis_runs[g])
+        load_tab(1)
+        load_w1(1)
 
         for u in range(2):
             nc.vector.tensor_copy(
@@ -192,18 +205,23 @@ def tile_list_asteroid_band_fluxes_kernel(
 
         for j in range(halves):
             squares_on_vector(1, j)
-        w1_wp = held([P, kpasses * H], U16, "w1_wp")
+        w1_wp = [held([P, kpasses * PASS], U16, "w1_wp%d" % g) for g in range(groups)]
         w1_sp = held([P, kpasses * H], U8, "w1_sp")
-        for dst, src in ((w1_wp, w1_w), (w1_sp, w1_s)):
+
+        def deal(dst, src, words):
             nc.vector.tensor_copy(
-                dst[:].bitcast(I32).rearrange("p (g t b w) -> p g b t w", t=PACK, b=P // RUN, g=kpasses * groups),
-                src[:].bitcast(I32).rearrange("p (g b t w) -> p g b t w", t=PACK, b=P // RUN, g=kpasses * groups),
+                dst[:].bitcast(I32).rearrange("p (g t b w) -> p g b t w", t=PACK, b=P // RUN, w=words),
+                src[:].bitcast(I32).rearrange("p (g b t w) -> p g b t w", t=PACK, b=P // RUN, w=words),
             )
+
+        deal(w1_wp[0], w1_w[0], 4)
+        deal(w1_sp, w1_s, 2)
         side_b(1, 0)
         side_b(1, 1)
         for a in range(kpasses):
             for j in range(halves):
                 nc.vector.tensor_copy(v_w[a][j][:], tab_w[a][:].bitcast(U32).indirect(picks(idx, j)))
+        deal(w1_wp[1], w1_w[1], 4)
         turned = psum_out.tile([P, P], F32, name="acc")
         nc.tensor.transpose(turned[:], emis_rows[:], ident[:])
         nc.scalar.activation(emis2[:], turned[:, 0 : groups * PACK], ACT.Square)
@@ -211,120 +229,155 @@ def tile_list_asteroid_band_fluxes_kernel(
         h_c = [held([P, S], U32, "h_c%d" % g) for g in range(groups)]
         h_q = [held([P, S], U8, "h_q%d" % g) for g in range(groups)]
         roots = [held([P, PACK, HALF], F32, "root%d" % u) for u in range(3)]
+        mags = [[roots[0], roots[1]], [roots[2], roots[0]]]
 
-        def magnitudes(g, j, mag):
+        def product_a(g, j):
+            banks = []
             for t in range(PACK):
                 bank = psum_ab.tile([P, HALF], F32, name="bank")
                 for a in range(kpasses):
                     c0 = a * H + g * PASS + t * P
+                    w0 = a * PASS + t * P
                     s0 = a * S + j * HALF
                     nc.tensor.matmul_mx(
                         out=bank[:],
-                        lhsT=w1_wp[:, c0 : c0 + P].bitcast(FP4X4),
+                        lhsT=w1_wp[g][:, w0 : w0 + P].bitcast(FP4X4),
                         lhsT_scale=w1_sp[:, c0 : c0 + P],
                         rhs=v_w[a][j][:].bitcast(FP8X4),
                         rhs_scale=v_s[:, s0 : s0 + HALF],
                         start=(a == 0),
                         stop=(a == kpasses - 1),
                     )
-                gain = emis2[:, g * PACK + t : g * PACK + t + 1]
-                if (g, j, t) in MAGNITUDES_ON_VECTOR:
-                    twin = ring.tile([P, HALF], F32, name="twin", align_bytes=64)
-                    nc.vector.tensor_scalar(twin[:], bank[:], gain, -1.0, MULT, MULT)
-                    nc.vector.scalar_tensor_tensor(mag[:, t, :], bank[:], gain, twin[:], MULT, MAX)
-                else:
-                    nc.scalar.activation(mag[:, t, :], bank[:], ACT.Abs, scale=gain)
+                banks.append(bank)
+            return banks
 
-        def prepare_w3(g):
+        def magnitudes(g, j, banks, cols):
+            for t in range(PACK):
+                gain = emis2[:, g * PACK + t : g * PACK + t + 1]
+                nc.scalar.activation(mags[j][g][:, t, cols], banks[t][:, cols], ACT.Abs, scale=gain)
+
+        def root(g, j, cols):
+            part = mags[j][g][:, :, cols]
+            nc.scalar.activation(part, part, ACT.Sqrt)
+
+        def joint(g, j, cols):
+            part = damp[g][j][:, :, cols]
+            nc.vector.scalar_tensor_tensor(part, part, 1.0, mags[j][g][:, :, cols], ADD, MULT)
+
+        def joint_root(g, j, cols):
+            part = damp[g][j][:, :, cols]
+            nc.scalar.activation(part, part, ACT.Abs_reciprocal_sqrt, bias=TINY)
+
+        def prepare_w3(g, stage):
             for u in range(2):
                 nc.vector.tensor_copy(
-                    staged[g][:].rearrange("p (c i j) -> p c j i", i=4, j=PACK)[:, 64 * u : 64 * u + 64],
+                    stage[:].rearrange("p (c i j) -> p c j i", i=4, j=PACK)[:, 64 * u : 64 * u + 64],
                     w_raw[g][:].rearrange("p j (c i) -> p c j i", i=4)[:, 64 * u : 64 * u + 64],
                 )
             for u in range(2):
                 cols = slice(2 * u * P, (2 * u + 2) * P)
-                quantise(w3_c[g][:, cols], w3_q[g][:, cols], staged[g][:, cols.start * PACK : cols.stop * PACK])
+                quantise(w3_c[g][:, cols], w3_q[g][:, cols], stage[:, cols.start * PACK : cols.stop * PACK])
 
-        def flux_pass(acc, n0, entries, g):
+        def weave(g, j, cols):
+            nc.vector.tensor_tensor(
+                staged[g][:, cols.start * PACK : cols.stop * PACK].rearrange("p (c i t) -> p c t i", i=4, t=PACK),
+                mags[j][g][:, :, cols].rearrange("p t (c i) -> p c t i", i=4),
+                damp[g][j][:, :, cols].rearrange("p t (c i) -> p c t i", i=4),
+                MULT,
+            )
+
+        def pack(g, j, cols):
+            entries = slice(j * HALF + cols.start, j * HALF + cols.stop)
+            quantise(h_c[g][:, entries], h_q[g][:, entries], staged[g][:, cols.start * PACK : cols.stop * PACK])
+
+        def flux_pass(acc, n0, j, cols, g):
+            entries = slice(j * HALF + cols.start, j * HALF + cols.stop)
             tiles = acc.shape[1]
             for u in range(tiles):
-                cols = slice((n0 + u) * P, (n0 + u + 1) * P)
+                bands = slice((n0 + u) * P, (n0 + u + 1) * P)
                 nc.tensor.matmul_mx(
                     out=acc[:, u, :],
-                    lhsT=w3_c[g][:, cols].bitcast(FP8X4),
-                    lhsT_scale=w3_q[g][:, cols],
+                    lhsT=w3_c[g][:, bands].bitcast(FP8X4),
+                    lhsT_scale=w3_q[g][:, bands],
                     rhs=h_c[g][:, entries].bitcast(FP8X4),
                     rhs_scale=h_q[g][:, entries],
                     start=(g == 0 and u == 0),
                     stop=(g == groups - 1 and u == tiles - 1),
                 )
 
-        def open_fluxes(entries, width):
-            late = entries.start >= S - 2 * P
+        def open_sums(j, cols, tiles, pool, name):
             accs = []
-            for n0 in range(0, N // P, 2):
-                if late:
-                    acc = psum_ab.tile([P, 2, width], F32, name="bank")
-                else:
-                    acc = psum_out.tile([P, 2, width], F32, name="acc")
-                flux_pass(acc, n0, entries, 0)
-                accs.append(acc)
+            for n0 in range(0, N // P, tiles):
+                acc = pool.tile([P, tiles, cols.stop - cols.start], F32, name=name)
+                flux_pass(acc, n0, j, cols, 0)
+                accs.append((acc, n0, j, cols))
             return accs
 
-        def close_fluxes(accs, entries, width):
-            for n0 in range(0, N // P, 2):
-                acc = accs[n0 // 2]
-                flux_pass(acc, n0, entries, 1)
-                res = ring.tile([P, 2, width], F32, name="res", align_bytes=64, bufs=6)
-                rows = out[n0 * P : (n0 + 2) * P, entries].rearrange("(u p) j -> p u j", p=P)
-                if entries.stop > HALF and (n0 > 0 or entries.stop == S - P):
-                    nc.scalar.copy(res[:], acc[:])
-                else:
-                    nc.vector.tensor_copy(res[:], acc[:])
-                nc.sync.dma_start(rows, res[:])
+        def close_sums(accs):
+            for acc, n0, j, cols in accs:
+                flux_pass(acc, n0, j, cols, 1)
 
-        def weave(g, j, mag, first, width):
-            cols = slice(first, first + width)
-            entries = slice(j * HALF + first, j * HALF + first + width)
-            h_bf = staged[g][:, first * PACK : (first + width) * PACK]
-            accs = open_fluxes(entries, width) if g == groups - 1 else None
-            if (g, j) not in ONE_ROOT:
-                nc.scalar.activation(mag[:, :, cols], mag[:, :, cols], ACT.Sqrt)
-            nc.vector.tensor_tensor(
-                h_bf.rearrange("p (c i t) -> p c t i", i=4, t=PACK),
-                mag[:, :, cols].rearrange("p t (c i) -> p c t i", i=4),
-                damp[g][j][:, :, cols].rearrange("p t (c i) -> p c t i", i=4),
-                MULT,
-            )
-            return g, entries, width, h_bf, accs
+        def store(copy, acc, n0, j, cols):
+            tiles = acc.shape[1]
+            res = ring.tile([P, tiles, cols.stop - cols.start], F32, name="res", align_bytes=64, bufs=6)
+            copy(res[:], acc[:])
+            rows = out[n0 * P : (n0 + tiles) * P, j * HALF + cols.start : j * HALF + cols.stop]
+            nc.sync.dma_start(rows.rearrange("(u p) j -> p u j", p=P), res[:])
 
-        def finish(g, entries, width, h_bf, accs):
-            quantise(h_c[g][:, entries], h_q[g][:, entries], h_bf)
-            if g == groups - 1:
-                close_fluxes(accs, entries, width)
+        whole, left, right = slice(0, HALF), slice(0, 256), slice(256, HALF)
+        third, fourth = slice(256, 384), slice(384, HALF)
+        on_vector, on_scalar = nc.vector.tensor_copy, nc.scalar.copy
 
-        waiting = None
-        for j in range(halves):
-            for g in range(groups):
-                mag = roots[(j * groups + g) % len(roots)]
-                magnitudes(g, j, mag)
-                if (g, j) in ONE_ROOT:
-                    for first in range(0, HALF, 256):
-                        part = damp[g][j][:, :, first : first + 256]
-                        nc.vector.scalar_tensor_tensor(part, part, 1.0, mag[:, :, first : first + 256], ADD, MULT)
-                        nc.scalar.activation(part, part, ACT.Abs_reciprocal_sqrt, bias=TINY)
-                if (g, j) == (0, 0):
-                    prepare_w3(0)
-                    prepare_w3(1)
-                last = (g, j) == (groups - 1, halves - 1)
-                first = 0
-                for width in (256, 128, 128) if last else (256, 256):
-                    if waiting is not None and g == groups - 1 and first == 0:
-                        finish(*waiting)
-                        waiting = None
-                    woven = weave(g, j, mag, first, width)
-                    if waiting is not None:
-                        finish(*waiting)
-                    waiting = woven
-                    first = first + width
-        finish(*waiting)
+        banks = product_a(0, 0)
+        for cols in (left, right):
+            magnitudes(0, 0, banks, cols)
+            joint(0, 0, cols)
+        for cols in (left, right):
+            joint_root(0, 0, cols)
+            weave(0, 0, cols)
+        prepare_w3(0, staged[2])
+        for cols in (left, right):
+            pack(0, 0, cols)
+        prepare_w3(1, staged[1])
+
+        magnitudes(1, 0, product_a(1, 0), whole)
+        sums = [open_sums(0, cols, 2, psum_out, "acc") for cols in (left, right)]
+        for cols in (left, right):
+            root(1, 0, cols)
+            weave(1, 0, cols)
+        for u, cols in enumerate((left, right)):
+            pack(1, 0, cols)
+            close_sums(sums[u])
+        store(on_vector, *sums[0][0])
+        store(on_vector, *sums[0][1])
+        store(on_vector, *sums[1][0])
+
+        magnitudes(0, 1, product_a(0, 1), whole)
+        for cols in (left, right):
+            root(0, 1, cols)
+            weave(0, 1, cols)
+        store(on_scalar, *sums[1][1])
+        for cols in (left, right):
+            pack(0, 1, cols)
+
+        banks = product_a(1, 1)
+        sums_left = open_sums(1, left, 2, psum_out, "acc")
+        sums_third = open_sums(1, third, 4, psum_out, "acc")
+        for cols in (left, third, fourth):
+            magnitudes(1, 1, banks, cols)
+            root(1, 1, cols)
+        sums_fourth = open_sums(1, fourth, 2, psum_ab, "bank")
+        weave(1, 1, left)
+        weave(1, 1, third)
+        pack(1, 1, left)
+        close_sums(sums_left)
+        weave(1, 1, fourth)
+        pack(1, 1, third)
+        close_sums(sums_third)
+        pack(1, 1, fourth)
+        close_sums(sums_fourth)
+        store(on_vector, *sums_left[0])
+        store(on_scalar, *sums_left[1])
+        store(on_scalar, *sums_third[0])
+        store(on_vector, *sums_fourth[0])
+        store(on_scalar, *sums_fourth[1])

@@ -25,8 +25,8 @@ PASS = P * PACK
 HALF = 512
 RUN = 8
 QUADS = 4
-SQUARES_ON_VECTOR = {(1, 0, 0), (1, 0, 1)}
-ONE_ROOT = {(0, 0)}
+SQUARES_ON_VECTOR = {(1, 0, 0), (1, 0, 1), (1, 1, 0), (1, 1, 1)}
+ONE_ROOT = set()
 TINY = 1e-36
 FIRST_CASTS_ON_SCALAR = (1, 2)
 
@@ -41,8 +41,8 @@ def tile_list_asteroid_band_fluxes_kernel(
     with ExitStack() as ctx:
         keep = ctx.enter_context(tc.tile_pool(name="keep", bufs=1))
         ring = ctx.enter_context(tc.tile_pool(name="ring", bufs=2))
-        psum_ab = ctx.enter_context(tc.psum_pool(name="psum_ab", bufs=5))
-        psum_out = ctx.enter_context(tc.psum_pool(name="psum_out", bufs=3))
+        psum = ctx.enter_context(tc.psum_pool(name="psum", bufs=1))
+        bank_of = [psum.tile([P, HALF], F32, name="bank%d" % u) for u in range(8)]
 
         def held(shape, dtype, name):
             return keep.tile(shape, dtype, name=name, align_bytes=64)
@@ -67,8 +67,8 @@ def tile_list_asteroid_band_fluxes_kernel(
         nc.vector.memset(tab2_s[0 : P - 16, :].bitcast(I32), 0)
         nc.vector.memset(v2_s[:].bitcast(I32), 0)
         nc.gpsimd.memset(tab_s[0 : P - 32, :].bitcast(I32), 0)
-        nc.gpsimd.memset(w1_s[:].bitcast(I32), 0)
-        nc.gpsimd.memset(v_s[:].bitcast(I32), 0)
+        nc.vector.memset(w1_s[:].bitcast(I32), 0)
+        nc.vector.memset(v_s[:].bitcast(I32), 0)
         one = held([P, 1], F32, "one")
         warm = held([P, 1], F32, "warm")
         nc.gpsimd.memset(one[:], 1.0)
@@ -106,6 +106,9 @@ def tile_list_asteroid_band_fluxes_kernel(
         def load_tab(a):
             nc.sync.dma_start(tab_w[a][:], tab_words[a].rearrange("p t i -> p (t i)").bitcast(I32))
 
+        emis_runs = emis.rearrange("(g b t i) -> g t b i", g=groups, t=PACK, i=RUN)
+        for g in range(groups):
+            nc.sync.dma_start(emis_rows[g * PACK : (g + 1) * PACK, :].rearrange("t (b i) -> t b i", i=RUN), emis_runs[g])
         load_tab(0)
 
 
@@ -120,7 +123,7 @@ def tile_list_asteroid_band_fluxes_kernel(
         def quantise(codes, scales, values):
             nc.vector.quantize_mx(out=codes.bitcast(FP8X4), scales=scales, in_=values)
 
-        staged = [held([P, PASS * PACK], BF16, "staged%d" % u) for u in range(3)]
+        staged = [held([P, PASS * PACK], BF16, "staged%d" % u) for u in range(2)]
         first_bf = [held([P, PASS], BF16, "first_bf%d" % t) for t in range(PACK)]
         w2_c = [held([P, PASS], U32, "w2_c%d" % g) for g in range(groups)]
         w2_q = [held([P, PASS], U8, "w2_q%d" % g) for g in range(groups)]
@@ -145,9 +148,12 @@ def tile_list_asteroid_band_fluxes_kernel(
 
         damp = [[held([P, PACK, HALF], F32, "damp%d_%d" % (g, j)) for j in range(halves)] for g in range(groups)]
 
-        def product_b(g, j, t, pool, name):
+        turns = [0, 0]
+
+        def product_b(g, j, t, helped):
             cols = slice(t * P, (t + 1) * P)
-            bank = pool.tile([P, HALF], F32, name=name)
+            bank = bank_of[6 + turns[1] % 2] if helped else bank_of[(2, 2, 4, 5)[t] if j else t % 2] if g else bank_of[turns[0] % 6]
+            turns[helped] = turns[helped] + 1
             nc.tensor.matmul_mx(
                 out=bank[:],
                 lhsT=w2_c[g][:, cols].bitcast(FP8X4),
@@ -163,7 +169,7 @@ def tile_list_asteroid_band_fluxes_kernel(
             taken = []
             for t in range(PACK):
                 if (g, j, t) in SQUARES_ON_VECTOR:
-                    bank = product_b(g, j, t, psum_out, "acc")
+                    bank = product_b(g, j, t, 1)
                     twin = ring.tile([P, HALF], F32, name="twin", align_bytes=64)
                     nc.vector.tensor_copy(twin[:], bank[:])
                     taken.append((t, bank, twin))
@@ -173,7 +179,7 @@ def tile_list_asteroid_band_fluxes_kernel(
         def side_b(g, j):
             for t in range(PACK):
                 if (g, j, t) not in SQUARES_ON_VECTOR:
-                    bank = product_b(g, j, t, psum_ab, "bank")
+                    bank = product_b(g, j, t, 0)
                     nc.scalar.activation(damp[g][j][:, t, :], bank[:], ACT.Square)
             if (g, j) not in ONE_ROOT:
                 nc.scalar.activation(damp[g][j][:], damp[g][j][:], ACT.Abs_reciprocal_sqrt, bias=1.0)
@@ -184,9 +190,6 @@ def tile_list_asteroid_band_fluxes_kernel(
         for q in range(QUADS):
             src = v_rows[P - 32 + 8 * q : P - 24 + 8 * q, :]
             nc.sync.dma_start(v_s[32 * q : 32 * q + 4, :].bitcast(I32), src.bitcast(I32))
-        emis_runs = emis.rearrange("(g b t i) -> g t b i", g=groups, t=PACK, i=RUN)
-        for g in range(groups):
-            nc.sync.dma_start(emis_rows[g * PACK : (g + 1) * PACK, :].rearrange("t (b i) -> t b i", i=RUN), emis_runs[g])
         load_tab(1)
         load_w1(1)
 
@@ -216,26 +219,29 @@ def tile_list_asteroid_band_fluxes_kernel(
 
         deal(w1_wp[0], w1_w[0], 4)
         deal(w1_sp, w1_s, 2)
+        turned = bank_of[3]
+        nc.tensor.transpose(turned[:, 0:P], emis_rows[:], ident[:])
+        nc.scalar.activation(emis2[:], turned[:, 0 : groups * PACK], ACT.Square)
         side_b(1, 0)
         side_b(1, 1)
         for a in range(kpasses):
             for j in range(halves):
                 nc.vector.tensor_copy(v_w[a][j][:], tab_w[a][:].bitcast(U32).indirect(picks(idx, j)))
         deal(w1_wp[1], w1_w[1], 4)
-        turned = psum_out.tile([P, P], F32, name="acc")
-        nc.tensor.transpose(turned[:], emis_rows[:], ident[:])
-        nc.scalar.activation(emis2[:], turned[:, 0 : groups * PACK], ACT.Square)
 
         h_c = [held([P, S], U32, "h_c%d" % g) for g in range(groups)]
         h_q = [held([P, S], U8, "h_q%d" % g) for g in range(groups)]
-        roots = [held([P, PACK, HALF], F32, "root%d" % u) for u in range(3)]
-        mags = [[roots[0], roots[1]], [roots[2], roots[0]]]
+        roots = [held([P, PACK, HALF], F32, "root%d" % u) for u in range(2)]
+        mags = [[roots[0], roots[1]], [roots[1], roots[0]]]
 
         def product_a(g, j):
-            banks = []
-            for t in range(PACK):
-                bank = psum_ab.tile([P, HALF], F32, name="bank")
-                for a in range(kpasses):
+            banks = bank_of[PACK * g : PACK * (g + 1)]
+            steps = [(a, t) for a in range(kpasses) for t in range(PACK)]
+            if (g, j) != (0, 0):
+                steps = sorted(steps, key=lambda step: step[1])
+            for a, t in steps:
+                if True:
+                    bank = banks[t]
                     c0 = a * H + g * PASS + t * P
                     w0 = a * PASS + t * P
                     s0 = a * S + j * HALF
@@ -248,7 +254,6 @@ def tile_list_asteroid_band_fluxes_kernel(
                         start=(a == 0),
                         stop=(a == kpasses - 1),
                     )
-                banks.append(bank)
             return banks
 
         def magnitudes(g, j, banks, cols):
@@ -305,10 +310,11 @@ def tile_list_asteroid_band_fluxes_kernel(
                     stop=(g == groups - 1 and u == tiles - 1),
                 )
 
-        def open_sums(j, cols, tiles, pool, name):
+        def open_sums(j, cols, tiles, first):
             accs = []
+            width = cols.stop - cols.start
             for n0 in range(0, N // P, tiles):
-                acc = pool.tile([P, tiles, cols.stop - cols.start], F32, name=name)
+                acc = bank_of[first + n0 // tiles][:, 0 : tiles * width].rearrange("p (u j) -> p u j", u=tiles)
                 flux_pass(acc, n0, j, cols, 0)
                 accs.append((acc, n0, j, cols))
             return accs
@@ -317,31 +323,30 @@ def tile_list_asteroid_band_fluxes_kernel(
             for acc, n0, j, cols in accs:
                 flux_pass(acc, n0, j, cols, 1)
 
-        def store(copy, acc, n0, j, cols):
+        def store(copy, acc, n0, j, cols, res=None):
             tiles = acc.shape[1]
-            res = ring.tile([P, tiles, cols.stop - cols.start], F32, name="res", align_bytes=64, bufs=6)
-            copy(res[:], acc[:])
+            if res is None:
+                res = ring.tile([P, tiles, cols.stop - cols.start], F32, name="res", align_bytes=64, bufs=6)[:]
+            copy(res, acc)
             rows = out[n0 * P : (n0 + tiles) * P, j * HALF + cols.start : j * HALF + cols.stop]
-            nc.sync.dma_start(rows.rearrange("(u p) j -> p u j", p=P), res[:])
+            nc.sync.dma_start(rows.rearrange("(u p) j -> p u j", p=P), res)
 
         whole, left, right = slice(0, HALF), slice(0, 256), slice(256, HALF)
         third, fourth = slice(256, 384), slice(384, HALF)
         on_vector, on_scalar = nc.vector.tensor_copy, nc.scalar.copy
 
         banks = product_a(0, 0)
+        prepare_w3(0, staged[0])
         for cols in (left, right):
             magnitudes(0, 0, banks, cols)
-            joint(0, 0, cols)
-        for cols in (left, right):
-            joint_root(0, 0, cols)
+            root(0, 0, cols)
             weave(0, 0, cols)
-        prepare_w3(0, staged[2])
+        prepare_w3(1, staged[1])
         for cols in (left, right):
             pack(0, 0, cols)
-        prepare_w3(1, staged[1])
 
         magnitudes(1, 0, product_a(1, 0), whole)
-        sums = [open_sums(0, cols, 2, psum_out, "acc") for cols in (left, right)]
+        sums = [open_sums(0, left, 2, 4), open_sums(0, right, 2, 6)]
         for cols in (left, right):
             root(1, 0, cols)
             weave(1, 0, cols)
@@ -351,22 +356,24 @@ def tile_list_asteroid_band_fluxes_kernel(
         store(on_vector, *sums[0][0])
         store(on_vector, *sums[0][1])
         store(on_vector, *sums[1][0])
+        store(on_vector, *sums[1][1])
 
-        magnitudes(0, 1, product_a(0, 1), whole)
+        banks = product_a(0, 1)
+        for cols in (left, right):
+            magnitudes(0, 1, banks, cols)
         for cols in (left, right):
             root(0, 1, cols)
             weave(0, 1, cols)
-        store(on_scalar, *sums[1][1])
         for cols in (left, right):
             pack(0, 1, cols)
 
         banks = product_a(1, 1)
-        sums_left = open_sums(1, left, 2, psum_out, "acc")
-        sums_third = open_sums(1, third, 4, psum_out, "acc")
+        sums_left = open_sums(1, left, 2, 0)
+        sums_third = open_sums(1, third, 4, 2)
         for cols in (left, third, fourth):
             magnitudes(1, 1, banks, cols)
             root(1, 1, cols)
-        sums_fourth = open_sums(1, fourth, 2, psum_ab, "bank")
+        sums_fourth = open_sums(1, fourth, 2, 3)
         weave(1, 1, left)
         weave(1, 1, third)
         pack(1, 1, left)
@@ -376,8 +383,8 @@ def tile_list_asteroid_band_fluxes_kernel(
         close_sums(sums_third)
         pack(1, 1, fourth)
         close_sums(sums_fourth)
-        store(on_vector, *sums_left[0])
+        store(on_scalar, *sums_left[0])
         store(on_scalar, *sums_left[1])
-        store(on_scalar, *sums_third[0])
+        store(on_vector, *sums_third[0], damp[1][1][:, :, fourth])
         store(on_vector, *sums_fourth[0])
         store(on_scalar, *sums_fourth[1])

@@ -25,9 +25,9 @@ PASS = P * PACK
 HALF = 512
 RUN = 8
 QUADS = 4
-SQUARES_ON_VECTOR = {(1, 0, 0), (1, 0, 1), (1, 1, 0), (1, 1, 1)}
-ONE_ROOT = set()
-TINY = 1e-36
+SQUARES_ON_VECTOR = {(1, 1, 0), (1, 1, 1)}
+ONE_ROOT = {(0, 0), (1, 0)}
+TINY = 2.0**-80
 FIRST_CASTS_ON_SCALAR = (1, 2)
 
 
@@ -51,24 +51,24 @@ def tile_list_asteroid_band_fluxes_kernel(
         idx2 = keep.tile([P, S // 16], U16, name="idx2")
         tab2_s = held([P, T], U8, "tab2_s")
         tab_s = held([P, T], U8, "tab_s")
-        w1_s = held([P, kpasses * H], U8, "w1_s")
+        w1_rows = held([P, H], U8, "w1_rows")
+        joined = held([P, S + H], U8, "joined")
         v2_s = held([P, S], U8, "v2_s")
-        v_s = held([P, kpasses * S], U8, "v_s")
+        a_s = held([P, kpasses * (S + H)], U8, "a_s")
         v2_rows = held([P, S], U8, "v2_rows")
         v_rows = held([P, S], U8, "v_rows")
         tab2_w = held([P, T], U16, "tab2_w")
         tab_w = [held([P, T], I32, "tab_w%d" % a) for a in range(kpasses)]
         w1_w = [held([P, kpasses * PASS], U16, "w1_w%d" % g) for g in range(groups)]
         w_raw = [held([P, PACK, PASS], F32, "w_raw%d" % g) for g in range(groups)]
-        emis_rows = held([P, P], F32, "emis_rows")
+        emis_rows = held([P, groups * P], F32, "emis_rows")
         ident = held([P, P], F32, "ident")
         emis2 = held([P, groups * PACK], F32, "emis2")
 
         nc.vector.memset(tab2_s[0 : P - 16, :].bitcast(I32), 0)
         nc.vector.memset(v2_s[:].bitcast(I32), 0)
         nc.gpsimd.memset(tab_s[0 : P - 32, :].bitcast(I32), 0)
-        nc.vector.memset(w1_s[:].bitcast(I32), 0)
-        nc.vector.memset(v_s[:].bitcast(I32), 0)
+        nc.vector.memset(a_s[:].bitcast(I32), 0)
         one = held([P, 1], F32, "one")
         warm = held([P, 1], F32, "warm")
         nc.gpsimd.memset(one[:], 1.0)
@@ -89,11 +89,7 @@ def tile_list_asteroid_band_fluxes_kernel(
             src = v2_rows[P - 16 + 4 * q : P - 12 + 4 * q, :]
             nc.sync.dma_start(v2_s[32 * q : 32 * q + 4, :].bitcast(I32), src.bitcast(I32))
         nc.sync.dma_start(w_raw[1][:], w2_rows[:, :, PASS : 2 * PASS])
-        for q in range(QUADS):
-            nc.sync.dma_start(
-                w1_s[32 * q : 32 * q + 4, :].bitcast(I32).rearrange("p (a c) -> p a c", a=kpasses),
-                w1_scales[:, 4 * q : 4 * q + 4, :].bitcast(I32).rearrange("a r c -> r a c"),
-            )
+        nc.sync.dma_start(w1_rows[P - 32 : P, :].bitcast(I32), w1_scales.rearrange("a q c -> q a c").bitcast(I32))
 
         def load_w1(g):
             nc.sync.dma_start(
@@ -106,9 +102,9 @@ def tile_list_asteroid_band_fluxes_kernel(
         def load_tab(a):
             nc.sync.dma_start(tab_w[a][:], tab_words[a].rearrange("p t i -> p (t i)").bitcast(I32))
 
-        emis_runs = emis.rearrange("(g b t i) -> g t b i", g=groups, t=PACK, i=RUN)
-        for g in range(groups):
-            nc.sync.dma_start(emis_rows[g * PACK : (g + 1) * PACK, :].rearrange("t (b i) -> t b i", i=RUN), emis_runs[g])
+        nc.sync.dma_start(
+            emis_rows[0:PACK, :].rearrange("t (b i) -> t b i", i=RUN), emis.rearrange("(b t i) -> t b i", t=PACK, i=RUN)
+        )
         load_tab(0)
 
 
@@ -152,7 +148,7 @@ def tile_list_asteroid_band_fluxes_kernel(
 
         def product_b(g, j, t, helped):
             cols = slice(t * P, (t + 1) * P)
-            bank = bank_of[6 + turns[1] % 2] if helped else bank_of[(2, 2, 4, 5)[t] if j else t % 2] if g else bank_of[turns[0] % 6]
+            bank = bank_of[6 + turns[1] % 2] if helped else bank_of[t - 2 if j else 2 + t] if g else bank_of[turns[0] % 6]
             turns[helped] = turns[helped] + 1
             nc.tensor.matmul_mx(
                 out=bank[:],
@@ -186,10 +182,18 @@ def tile_list_asteroid_band_fluxes_kernel(
 
         side_b(0, 0)
         side_b(0, 1)
+        def deal(dst, src, words):
+            nc.vector.tensor_copy(
+                dst.bitcast(I32).rearrange("p (g t b w) -> p g b t w", t=PACK, b=P // RUN, w=words),
+                src.bitcast(I32).rearrange("p (g b t w) -> p g b t w", t=PACK, b=P // RUN, w=words),
+            )
+
         nc.vector.tensor_copy(v_rows[:], tab_s[:].indirect(idx[:]))
+        deal(joined[P - 32 : P, S : S + H], w1_rows[P - 32 : P, :], 2)
+        nc.vector.tensor_copy(joined[P - 32 : P, 0:S].bitcast(I32), v_rows[P - 32 : P, :].bitcast(I32))
         for q in range(QUADS):
-            src = v_rows[P - 32 + 8 * q : P - 24 + 8 * q, :]
-            nc.sync.dma_start(v_s[32 * q : 32 * q + 4, :].bitcast(I32), src.bitcast(I32))
+            src = joined[P - 32 + 8 * q : P - 24 + 8 * q, :]
+            nc.sync.dma_start(a_s[32 * q : 32 * q + 4, :].bitcast(I32), src.bitcast(I32))
         load_tab(1)
         load_w1(1)
 
@@ -209,48 +213,45 @@ def tile_list_asteroid_band_fluxes_kernel(
         for j in range(halves):
             squares_on_vector(1, j)
         w1_wp = [held([P, kpasses * PASS], U16, "w1_wp%d" % g) for g in range(groups)]
-        w1_sp = held([P, kpasses * H], U8, "w1_sp")
-
-        def deal(dst, src, words):
-            nc.vector.tensor_copy(
-                dst[:].bitcast(I32).rearrange("p (g t b w) -> p g b t w", t=PACK, b=P // RUN, w=words),
-                src[:].bitcast(I32).rearrange("p (g b t w) -> p g b t w", t=PACK, b=P // RUN, w=words),
-            )
-
-        deal(w1_wp[0], w1_w[0], 4)
-        deal(w1_sp, w1_s, 2)
+        deal(w1_wp[0][:], w1_w[0][:], 4)
         turned = bank_of[3]
-        nc.tensor.transpose(turned[:, 0:P], emis_rows[:], ident[:])
-        nc.scalar.activation(emis2[:], turned[:, 0 : groups * PACK], ACT.Square)
+        for g in range(groups):
+            nc.tensor.transpose(turned[:, g * P : (g + 1) * P], emis_rows[:, g * P : (g + 1) * P], ident[:])
+        nc.scalar.activation(
+            emis2[:].rearrange("p (g t) -> p g t", g=groups),
+            turned[:, 0 : groups * P].rearrange("p (g c) -> p g c", g=groups)[:, :, 0:PACK],
+            ACT.Square,
+        )
         side_b(1, 0)
         side_b(1, 1)
         for a in range(kpasses):
             for j in range(halves):
                 nc.vector.tensor_copy(v_w[a][j][:], tab_w[a][:].bitcast(U32).indirect(picks(idx, j)))
-        deal(w1_wp[1], w1_w[1], 4)
+        deal(w1_wp[1][:], w1_w[1][:], 4)
 
         h_c = [held([P, S], U32, "h_c%d" % g) for g in range(groups)]
         h_q = [held([P, S], U8, "h_q%d" % g) for g in range(groups)]
-        roots = [held([P, PACK, HALF], F32, "root%d" % u) for u in range(2)]
-        mags = [[roots[0], roots[1]], [roots[1], roots[0]]]
+        first_mags = [held([P, PACK, HALF], F32, "mag%d" % g) for g in range(groups)]
+        mags = [first_mags, [first_mags[0], damp[0][0]]]
+        w3_bf = [held([P, PASS * PACK], BF16, "w3_bf%d" % g) for g in range(groups)]
 
         def product_a(g, j):
-            banks = bank_of[PACK * g : PACK * (g + 1)]
+            banks = [bank_of[(2 + PACK * g + t) % 8] for t in range(PACK)]
             steps = [(a, t) for a in range(kpasses) for t in range(PACK)]
             if (g, j) != (0, 0):
                 steps = sorted(steps, key=lambda step: step[1])
             for a, t in steps:
                 if True:
                     bank = banks[t]
-                    c0 = a * H + g * PASS + t * P
+                    c0 = a * (S + H) + S + g * PASS + t * P
                     w0 = a * PASS + t * P
-                    s0 = a * S + j * HALF
+                    s0 = a * (S + H) + j * HALF
                     nc.tensor.matmul_mx(
                         out=bank[:],
                         lhsT=w1_wp[g][:, w0 : w0 + P].bitcast(FP4X4),
-                        lhsT_scale=w1_sp[:, c0 : c0 + P],
+                        lhsT_scale=a_s[:, c0 : c0 + P],
                         rhs=v_w[a][j][:].bitcast(FP8X4),
-                        rhs_scale=v_s[:, s0 : s0 + HALF],
+                        rhs_scale=a_s[:, s0 : s0 + HALF],
                         start=(a == 0),
                         stop=(a == kpasses - 1),
                     )
@@ -265,20 +266,22 @@ def tile_list_asteroid_band_fluxes_kernel(
             part = mags[j][g][:, :, cols]
             nc.scalar.activation(part, part, ACT.Sqrt)
 
-        def joint(g, j, cols):
-            part = damp[g][j][:, :, cols]
-            nc.vector.scalar_tensor_tensor(part, part, 1.0, mags[j][g][:, :, cols], ADD, MULT)
+        def joint(g, j, slots):
+            part = damp[g][j][:, slots, :]
+            nc.vector.scalar_tensor_tensor(part, part, 1.0, mags[j][g][:, slots, :], ADD, MULT)
 
         def joint_root(g, j, cols):
             part = damp[g][j][:, :, cols]
             nc.scalar.activation(part, part, ACT.Abs_reciprocal_sqrt, bias=TINY)
 
-        def prepare_w3(g, stage):
+        def round_w3(g, stage):
             for u in range(2):
                 nc.vector.tensor_copy(
                     stage[:].rearrange("p (c i j) -> p c j i", i=4, j=PACK)[:, 64 * u : 64 * u + 64],
                     w_raw[g][:].rearrange("p j (c i) -> p c j i", i=4)[:, 64 * u : 64 * u + 64],
                 )
+
+        def quantise_w3(g, stage):
             for u in range(2):
                 cols = slice(2 * u * P, (2 * u + 2) * P)
                 quantise(w3_c[g][:, cols], w3_q[g][:, cols], stage[:, cols.start * PACK : cols.stop * PACK])
@@ -335,45 +338,39 @@ def tile_list_asteroid_band_fluxes_kernel(
         third, fourth = slice(256, 384), slice(384, HALF)
         on_vector, on_scalar = nc.vector.tensor_copy, nc.scalar.copy
 
-        banks = product_a(0, 0)
-        prepare_w3(0, staged[0])
-        for cols in (left, right):
-            magnitudes(0, 0, banks, cols)
-            root(0, 0, cols)
-            weave(0, 0, cols)
-        prepare_w3(1, staged[1])
-        for cols in (left, right):
-            pack(0, 0, cols)
-
-        magnitudes(1, 0, product_a(1, 0), whole)
-        sums = [open_sums(0, left, 2, 4), open_sums(0, right, 2, 6)]
-        for cols in (left, right):
-            root(1, 0, cols)
-            weave(1, 0, cols)
-        for u, cols in enumerate((left, right)):
-            pack(1, 0, cols)
-            close_sums(sums[u])
-        store(on_vector, *sums[0][0])
-        store(on_vector, *sums[0][1])
-        store(on_vector, *sums[1][0])
-        store(on_vector, *sums[1][1])
-
-        banks = product_a(0, 1)
-        for cols in (left, right):
-            magnitudes(0, 1, banks, cols)
+        for g in range(groups):
+            magnitudes(g, 0, product_a(g, 0), whole)
+            for slots in (slice(0, 2), slice(2, 4)):
+                joint(g, 0, slots)
+        later = [product_a(g, 1) for g in range(groups)]
+        for g in range(groups):
+            for cols in (left, right):
+                joint_root(g, 0, cols)
+        for g in range(groups):
+            for cols in (left, right):
+                weave(g, 0, cols)
+            round_w3(g, w3_bf[g])
+            pack(g, 0, whole)
+            quantise_w3(g, w3_bf[g])
+        magnitudes(0, 1, later[0], whole)
+        sums = open_sums(0, whole, 1, 2)
+        close_sums(sums)
         for cols in (left, right):
             root(0, 1, cols)
-            weave(0, 1, cols)
+        magnitudes(1, 1, later[1], whole)
+        store(on_scalar, *sums[0])
+        store(on_scalar, *sums[1])
         for cols in (left, right):
-            pack(0, 1, cols)
+            weave(0, 1, cols)
+        store(on_vector, *sums[2])
+        pack(0, 1, whole)
+        store(on_vector, *sums[3])
 
-        banks = product_a(1, 1)
-        sums_left = open_sums(1, left, 2, 0)
-        sums_third = open_sums(1, third, 4, 2)
+        sums_left = open_sums(1, left, 2, 6)
+        sums_third = open_sums(1, third, 4, 0)
+        sums_fourth = open_sums(1, fourth, 2, 1)
         for cols in (left, third, fourth):
-            magnitudes(1, 1, banks, cols)
             root(1, 1, cols)
-        sums_fourth = open_sums(1, fourth, 2, 3)
         weave(1, 1, left)
         weave(1, 1, third)
         pack(1, 1, left)

@@ -25,8 +25,8 @@ PASS = P * PACK
 HALF = 512
 RUN = 8
 QUADS = 4
-SQUARES_ON_VECTOR = {(1, 1, 0), (1, 1, 1)}
-ONE_ROOT = {(0, 0), (1, 0)}
+SQUARES_ON_VECTOR = {(1, 0, 0), (1, 0, 1), (1, 1, 0), (1, 1, 1)}
+ONE_ROOT = set()
 TINY = 2.0**-80
 FIRST_CASTS_ON_SCALAR = (1, 2)
 
@@ -67,7 +67,8 @@ def tile_list_asteroid_band_fluxes_kernel(
 
         nc.vector.memset(tab2_s[0 : P - 16, :].bitcast(I32), 0)
         nc.vector.memset(v2_s[:].bitcast(I32), 0)
-        nc.gpsimd.memset(tab_s[0 : P - 32, :].bitcast(I32), 0)
+        nc.gpsimd.memset(tab_s[:].bitcast(I32), 0)
+        nc.gpsimd.memset(w1_rows[:].bitcast(I32), 0)
         nc.vector.memset(a_s[:].bitcast(I32), 0)
         one = held([P, 1], F32, "one")
         warm = held([P, 1], F32, "warm")
@@ -83,13 +84,13 @@ def tile_list_asteroid_band_fluxes_kernel(
         nc.sync.dma_start(tab2_w[:].bitcast(I32), tab2_words[0].bitcast(I32))
         nc.sync.dma_start(w_raw[0][:], w2_rows[:, :, 0:PASS])
         nc.sync.dma_start(idx[:], offs)
-        nc.sync.dma_start(tab_s[P - 32 : P, :].bitcast(I32), tab_scales.rearrange("a q t -> q a t").bitcast(I32))
+        nc.sync.dma_start(tab_s[32:96:2, :].bitcast(I32), tab_scales.rearrange("a q t -> q a t").bitcast(I32))
         nc.vector.tensor_copy(v2_rows[:], tab2_s[:].indirect(idx2[:]))
         for q in range(QUADS):
             src = v2_rows[P - 16 + 4 * q : P - 12 + 4 * q, :]
             nc.sync.dma_start(v2_s[32 * q : 32 * q + 4, :].bitcast(I32), src.bitcast(I32))
         nc.sync.dma_start(w_raw[1][:], w2_rows[:, :, PASS : 2 * PASS])
-        nc.sync.dma_start(w1_rows[P - 32 : P, :].bitcast(I32), w1_scales.rearrange("a q c -> q a c").bitcast(I32))
+        nc.sync.dma_start(w1_rows[32:96:2, :].bitcast(I32), w1_scales.rearrange("a q c -> q a c").bitcast(I32))
 
         def load_w1(g):
             nc.sync.dma_start(
@@ -148,7 +149,7 @@ def tile_list_asteroid_band_fluxes_kernel(
 
         def product_b(g, j, t, helped):
             cols = slice(t * P, (t + 1) * P)
-            bank = bank_of[6 + turns[1] % 2] if helped else bank_of[t - 2 if j else 2 + t] if g else bank_of[turns[0] % 6]
+            bank = bank_of[6 + turns[1] % 2] if helped else bank_of[(2, 2, 4, 5)[t] if j else t % 2] if g else bank_of[turns[0] % 6]
             turns[helped] = turns[helped] + 1
             nc.tensor.matmul_mx(
                 out=bank[:],
@@ -184,17 +185,26 @@ def tile_list_asteroid_band_fluxes_kernel(
         side_b(0, 1)
         def deal(dst, src, words):
             nc.vector.tensor_copy(
-                dst.bitcast(I32).rearrange("p (g t b w) -> p g b t w", t=PACK, b=P // RUN, w=words),
+                dst.bitcast(I32).rearrange("p g (t b w) -> p g b t w", t=PACK, w=words),
                 src.bitcast(I32).rearrange("p (g b t w) -> p g b t w", t=PACK, b=P // RUN, w=words),
             )
 
         nc.vector.tensor_copy(v_rows[:], tab_s[:].indirect(idx[:]))
-        deal(joined[P - 32 : P, S : S + H], w1_rows[P - 32 : P, :], 2)
-        nc.vector.tensor_copy(joined[P - 32 : P, 0:S].bitcast(I32), v_rows[P - 32 : P, :].bitcast(I32))
-        for q in range(QUADS):
-            src = joined[P - 32 + 8 * q : P - 24 + 8 * q, :]
-            nc.sync.dma_start(a_s[32 * q : 32 * q + 4, :].bitcast(I32), src.bitcast(I32))
+        pairs = joined[:].rearrange("p (u c) -> p u c", u=2)
+        deal(pairs[:, :, HALF : HALF + PASS], w1_rows[:], 2)
+        nc.vector.tensor_copy(pairs[:, :, 0:HALF].bitcast(I32), v_rows[:].rearrange("p (u c) -> p u c", u=2).bitcast(I32))
+        width = HALF + PASS
+
+        def spread(u, a0, a1):
+            for q in range(QUADS):
+                first = 32 + 16 * q + 2 * a0
+                src = pairs[first : 48 + 16 * q : 4 // (a1 - a0), u, :]
+                dst = a_s[32 * q : 32 * q + 4, (kpasses * u + a0) * width : (kpasses * u + a1) * width]
+                nc.sync.dma_start(dst.bitcast(I32), src.bitcast(I32))
+
+        spread(0, 0, 1)
         load_tab(1)
+        spread(0, 1, 2)
         load_w1(1)
 
         for u in range(2):
@@ -209,11 +219,13 @@ def tile_list_asteroid_band_fluxes_kernel(
             rows = w3[g * PASS : (g + 1) * PASS, :].rearrange("(b t i) n -> t b i n", t=PACK, i=RUN)
             for t in range(PACK):
                 nc.sync.dma_start(w_raw[g][:, t, :], rows[t])
+            if g == 0:
+                spread(1, 0, 2)
 
         for j in range(halves):
             squares_on_vector(1, j)
         w1_wp = [held([P, kpasses * PASS], U16, "w1_wp%d" % g) for g in range(groups)]
-        deal(w1_wp[0][:], w1_w[0][:], 4)
+        deal(w1_wp[0][:].rearrange("p (a c) -> p a c", a=kpasses), w1_w[0][:], 4)
         turned = bank_of[3]
         for g in range(groups):
             nc.tensor.transpose(turned[:, g * P : (g + 1) * P], emis_rows[:, g * P : (g + 1) * P], ident[:])
@@ -227,25 +239,24 @@ def tile_list_asteroid_band_fluxes_kernel(
         for a in range(kpasses):
             for j in range(halves):
                 nc.vector.tensor_copy(v_w[a][j][:], tab_w[a][:].bitcast(U32).indirect(picks(idx, j)))
-        deal(w1_wp[1][:], w1_w[1][:], 4)
+        deal(w1_wp[1][:].rearrange("p (a c) -> p a c", a=kpasses), w1_w[1][:], 4)
 
         h_c = [held([P, S], U32, "h_c%d" % g) for g in range(groups)]
         h_q = [held([P, S], U8, "h_q%d" % g) for g in range(groups)]
-        first_mags = [held([P, PACK, HALF], F32, "mag%d" % g) for g in range(groups)]
-        mags = [first_mags, [first_mags[0], damp[0][0]]]
-        w3_bf = [held([P, PASS * PACK], BF16, "w3_bf%d" % g) for g in range(groups)]
+        roots = [held([P, PACK, HALF], F32, "root%d" % u) for u in range(2)]
+        mags = [[roots[0], roots[1]], [roots[1], roots[0]]]
 
         def product_a(g, j):
-            banks = [bank_of[(2 + PACK * g + t) % 8] for t in range(PACK)]
+            banks = bank_of[PACK * g : PACK * (g + 1)]
             steps = [(a, t) for a in range(kpasses) for t in range(PACK)]
             if (g, j) != (0, 0):
                 steps = sorted(steps, key=lambda step: step[1])
             for a, t in steps:
                 if True:
                     bank = banks[t]
-                    c0 = a * (S + H) + S + g * PASS + t * P
+                    c0 = (kpasses * g + a) * width + HALF + t * P
                     w0 = a * PASS + t * P
-                    s0 = a * (S + H) + j * HALF
+                    s0 = (kpasses * j + a) * width
                     nc.tensor.matmul_mx(
                         out=bank[:],
                         lhsT=w1_wp[g][:, w0 : w0 + P].bitcast(FP4X4),
@@ -338,39 +349,47 @@ def tile_list_asteroid_band_fluxes_kernel(
         third, fourth = slice(256, 384), slice(384, HALF)
         on_vector, on_scalar = nc.vector.tensor_copy, nc.scalar.copy
 
-        for g in range(groups):
-            magnitudes(g, 0, product_a(g, 0), whole)
-            for slots in (slice(0, 2), slice(2, 4)):
-                joint(g, 0, slots)
-        later = [product_a(g, 1) for g in range(groups)]
-        for g in range(groups):
-            for cols in (left, right):
-                joint_root(g, 0, cols)
-        for g in range(groups):
-            for cols in (left, right):
-                weave(g, 0, cols)
-            round_w3(g, w3_bf[g])
-            pack(g, 0, whole)
-            quantise_w3(g, w3_bf[g])
-        magnitudes(0, 1, later[0], whole)
-        sums = open_sums(0, whole, 1, 2)
-        close_sums(sums)
+        banks = product_a(0, 0)
+        round_w3(0, staged[0])
+        quantise_w3(0, staged[0])
+        for cols in (left, right):
+            magnitudes(0, 0, banks, cols)
+            root(0, 0, cols)
+            weave(0, 0, cols)
+        round_w3(1, staged[1])
+        quantise_w3(1, staged[1])
+        for cols in (left, right):
+            pack(0, 0, cols)
+
+        magnitudes(1, 0, product_a(1, 0), whole)
+        sums = [open_sums(0, left, 2, 4), open_sums(0, right, 2, 6)]
+        for cols in (left, right):
+            root(1, 0, cols)
+            weave(1, 0, cols)
+        for u, cols in enumerate((left, right)):
+            pack(1, 0, cols)
+            close_sums(sums[u])
+        store(on_vector, *sums[0][0])
+        store(on_vector, *sums[0][1])
+        store(on_vector, *sums[1][0])
+        store(on_vector, *sums[1][1])
+
+        banks = product_a(0, 1)
+        for cols in (left, right):
+            magnitudes(0, 1, banks, cols)
         for cols in (left, right):
             root(0, 1, cols)
-        magnitudes(1, 1, later[1], whole)
-        store(on_scalar, *sums[0])
-        store(on_scalar, *sums[1])
-        for cols in (left, right):
             weave(0, 1, cols)
-        store(on_vector, *sums[2])
-        pack(0, 1, whole)
-        store(on_vector, *sums[3])
+        for cols in (left, right):
+            pack(0, 1, cols)
 
-        sums_left = open_sums(1, left, 2, 6)
-        sums_third = open_sums(1, third, 4, 0)
-        sums_fourth = open_sums(1, fourth, 2, 1)
+        banks = product_a(1, 1)
+        sums_left = open_sums(1, left, 2, 0)
+        sums_third = open_sums(1, third, 4, 2)
         for cols in (left, third, fourth):
+            magnitudes(1, 1, banks, cols)
             root(1, 1, cols)
+        sums_fourth = open_sums(1, fourth, 2, 3)
         weave(1, 1, left)
         weave(1, 1, third)
         pack(1, 1, left)

@@ -26,8 +26,7 @@ HALF = 512
 RUN = 8
 QUADS = 4
 SQUARES_ON_VECTOR = {(1, 0, 0), (1, 0, 1), (1, 1, 0), (1, 1, 1)}
-ONE_ROOT = set()
-TINY = 2.0**-80
+CHUNK = 128
 FIRST_CASTS_ON_SCALAR = (1, 2)
 
 
@@ -59,11 +58,12 @@ def tile_list_asteroid_band_fluxes_kernel(
         v_rows = held([P, S], U8, "v_rows")
         tab2_w = held([P, T], U16, "tab2_w")
         tab_w = [held([P, T], I32, "tab_w%d" % a) for a in range(kpasses)]
-        w1_w = [held([P, kpasses * PASS], U16, "w1_w%d" % g) for g in range(groups)]
+        w1_w = held([P, kpasses * H], U16, "w1_w")
         w_raw = [held([P, PACK, PASS], F32, "w_raw%d" % g) for g in range(groups)]
         emis_rows = held([P, groups * P], F32, "emis_rows")
         ident = held([P, P], F32, "ident")
-        emis2 = held([P, groups * PACK], F32, "emis2")
+        inverse = held([P, groups * PACK], F32, "inverse")
+        inverse2 = held([P, groups * PACK], F32, "inverse2")
 
         nc.vector.memset(tab2_s[0 : P - 16, :].bitcast(I32), 0)
         nc.vector.memset(v2_s[:].bitcast(I32), 0)
@@ -92,13 +92,9 @@ def tile_list_asteroid_band_fluxes_kernel(
         nc.sync.dma_start(w_raw[1][:], w2_rows[:, :, PASS : 2 * PASS])
         nc.sync.dma_start(w1_rows[32:96:2, :].bitcast(I32), w1_scales.rearrange("a q c -> q a c").bitcast(I32))
 
-        def load_w1(g):
-            nc.sync.dma_start(
-                w1_w[g][:].bitcast(I32).rearrange("p (a c) -> p a c", a=kpasses),
-                w1_words.bitcast(I32).rearrange("a p (g c) -> g p a c", g=groups)[g],
-            )
-
-        load_w1(0)
+        nc.sync.dma_start(
+            w1_w[:].bitcast(I32).rearrange("p (a c) -> p a c", a=kpasses), w1_words.bitcast(I32).rearrange("a p c -> p a c")
+        )
 
         def load_tab(a):
             nc.sync.dma_start(tab_w[a][:], tab_words[a].rearrange("p t i -> p (t i)").bitcast(I32))
@@ -145,6 +141,15 @@ def tile_list_asteroid_band_fluxes_kernel(
 
         damp = [[held([P, PACK, HALF], F32, "damp%d_%d" % (g, j)) for j in range(halves)] for g in range(groups)]
 
+        turned = bank_of[7]
+        for g in range(groups):
+            nc.tensor.transpose(turned[:, g * P : (g + 1) * P], emis_rows[:, g * P : (g + 1) * P], ident[:])
+        nc.vector.reciprocal(
+            inverse[:].rearrange("p (g t) -> p g t", g=groups),
+            turned[:, 0 : groups * P].rearrange("p (g c) -> p g c", g=groups)[:, :, 0:PACK],
+        )
+        nc.vector.tensor_tensor(inverse2[:], inverse[:], inverse[:], MULT)
+
         turns = [0, 0]
 
         def product_b(g, j, t, helped):
@@ -178,8 +183,10 @@ def tile_list_asteroid_band_fluxes_kernel(
                 if (g, j, t) not in SQUARES_ON_VECTOR:
                     bank = product_b(g, j, t, 0)
                     nc.scalar.activation(damp[g][j][:, t, :], bank[:], ACT.Square)
-            if (g, j) not in ONE_ROOT:
-                nc.scalar.activation(damp[g][j][:], damp[g][j][:], ACT.Abs_reciprocal_sqrt, bias=1.0)
+            for t in range(PACK):
+                unit = inverse2[:, g * PACK + t : g * PACK + t + 1]
+                part = damp[g][j][:, t, :]
+                nc.scalar.activation(part, part, ACT.Abs_reciprocal_sqrt, bias=unit, scale=unit)
 
         side_b(0, 0)
         side_b(0, 1)
@@ -190,22 +197,12 @@ def tile_list_asteroid_band_fluxes_kernel(
             )
 
         nc.vector.tensor_copy(v_rows[:], tab_s[:].indirect(idx[:]))
-        pairs = joined[:].rearrange("p (u c) -> p u c", u=2)
-        deal(pairs[:, :, HALF : HALF + PASS], w1_rows[:], 2)
-        nc.vector.tensor_copy(pairs[:, :, 0:HALF].bitcast(I32), v_rows[:].rearrange("p (u c) -> p u c", u=2).bitcast(I32))
-        width = HALF + PASS
-
-        def spread(u, a0, a1):
-            for q in range(QUADS):
-                first = 32 + 16 * q + 2 * a0
-                src = pairs[first : 48 + 16 * q : 4 // (a1 - a0), u, :]
-                dst = a_s[32 * q : 32 * q + 4, (kpasses * u + a0) * width : (kpasses * u + a1) * width]
-                nc.sync.dma_start(dst.bitcast(I32), src.bitcast(I32))
-
-        spread(0, 0, 1)
+        deal(joined[:, S : S + H].rearrange("p (g c) -> p g c", g=groups), w1_rows[:], 2)
+        nc.vector.tensor_copy(joined[:, 0:S].bitcast(I32), v_rows[:].bitcast(I32))
+        for q in range(QUADS):
+            src = joined[32 + 16 * q : 48 + 16 * q : 2, :]
+            nc.sync.dma_start(a_s[32 * q : 32 * q + 4, :].bitcast(I32), src.bitcast(I32))
         load_tab(1)
-        spread(0, 1, 2)
-        load_w1(1)
 
         for u in range(2):
             nc.vector.tensor_copy(
@@ -219,98 +216,60 @@ def tile_list_asteroid_band_fluxes_kernel(
             rows = w3[g * PASS : (g + 1) * PASS, :].rearrange("(b t i) n -> t b i n", t=PACK, i=RUN)
             for t in range(PACK):
                 nc.sync.dma_start(w_raw[g][:, t, :], rows[t])
-            if g == 0:
-                spread(1, 0, 2)
 
         for j in range(halves):
             squares_on_vector(1, j)
-        w1_wp = [held([P, kpasses * PASS], U16, "w1_wp%d" % g) for g in range(groups)]
-        deal(w1_wp[0][:].rearrange("p (a c) -> p a c", a=kpasses), w1_w[0][:], 4)
-        turned = bank_of[3]
-        for g in range(groups):
-            nc.tensor.transpose(turned[:, g * P : (g + 1) * P], emis_rows[:, g * P : (g + 1) * P], ident[:])
-        nc.scalar.activation(
-            emis2[:].rearrange("p (g t) -> p g t", g=groups),
-            turned[:, 0 : groups * P].rearrange("p (g c) -> p g c", g=groups)[:, :, 0:PACK],
-            ACT.Square,
-        )
+        w1_wp = held([P, kpasses * H], U16, "w1_wp")
+        deal(w1_wp[:].rearrange("p (u c) -> p u c", c=PASS), w1_w[:], 4)
         side_b(1, 0)
         side_b(1, 1)
-        for a in range(kpasses):
-            for j in range(halves):
-                nc.vector.tensor_copy(v_w[a][j][:], tab_w[a][:].bitcast(U32).indirect(picks(idx, j)))
-        deal(w1_wp[1][:].rearrange("p (a c) -> p a c", a=kpasses), w1_w[1][:], 4)
+        def gather_words(a, j):
+            nc.vector.tensor_copy(v_w[a][j][:], tab_w[a][:].bitcast(U32).indirect(picks(idx, j)))
 
-        h_c = [held([P, S], U32, "h_c%d" % g) for g in range(groups)]
-        h_q = [held([P, S], U8, "h_q%d" % g) for g in range(groups)]
-        roots = [held([P, PACK, HALF], F32, "root%d" % u) for u in range(2)]
-        mags = [[roots[0], roots[1]], [roots[1], roots[0]]]
+        gather_words(0, 0)
+        gather_words(0, 1)
+        gather_words(1, 0)
+        gather_words(1, 1)
 
-        def product_a(g, j):
-            banks = bank_of[PACK * g : PACK * (g + 1)]
-            steps = [(a, t) for a in range(kpasses) for t in range(PACK)]
-            if (g, j) != (0, 0):
-                steps = sorted(steps, key=lambda step: step[1])
-            for a, t in steps:
-                if True:
-                    bank = banks[t]
-                    c0 = (kpasses * g + a) * width + HALF + t * P
-                    w0 = a * PASS + t * P
-                    s0 = (kpasses * j + a) * width
-                    nc.tensor.matmul_mx(
-                        out=bank[:],
-                        lhsT=w1_wp[g][:, w0 : w0 + P].bitcast(FP4X4),
-                        lhsT_scale=a_s[:, c0 : c0 + P],
-                        rhs=v_w[a][j][:].bitcast(FP8X4),
-                        rhs_scale=a_s[:, s0 : s0 + HALF],
-                        start=(a == 0),
-                        stop=(a == kpasses - 1),
-                    )
-            return banks
+        chunks = S // CHUNK
+        per_half = HALF // CHUNK
+        last = chunks - 1
 
-        def magnitudes(g, j, banks, cols):
+        def bank_a(g, c):
+            return bank_of[4 + c % 2] if g else bank_of[c % 4]
+
+        def pass_a(g, c, a):
+            j, first = c // per_half, (c % per_half) * CHUNK
             for t in range(PACK):
-                gain = emis2[:, g * PACK + t : g * PACK + t + 1]
-                nc.scalar.activation(mags[j][g][:, t, cols], banks[t][:, cols], ACT.Abs, scale=gain)
-
-        def root(g, j, cols):
-            part = mags[j][g][:, :, cols]
-            nc.scalar.activation(part, part, ACT.Sqrt)
-
-        def joint(g, j, slots):
-            part = damp[g][j][:, slots, :]
-            nc.vector.scalar_tensor_tensor(part, part, 1.0, mags[j][g][:, slots, :], ADD, MULT)
-
-        def joint_root(g, j, cols):
-            part = damp[g][j][:, :, cols]
-            nc.scalar.activation(part, part, ACT.Abs_reciprocal_sqrt, bias=TINY)
-
-        def round_w3(g, stage):
-            for u in range(2):
-                nc.vector.tensor_copy(
-                    stage[:].rearrange("p (c i j) -> p c j i", i=4, j=PACK)[:, 64 * u : 64 * u + 64],
-                    w_raw[g][:].rearrange("p j (c i) -> p c j i", i=4)[:, 64 * u : 64 * u + 64],
+                c0 = a * (S + H) + S + g * PASS + t * P
+                w0 = a * H + g * PASS + t * P
+                s0 = a * (S + H) + c * CHUNK
+                nc.tensor.matmul_mx(
+                    out=bank_a(g, c)[:, t * CHUNK : (t + 1) * CHUNK],
+                    lhsT=w1_wp[:, w0 : w0 + P].bitcast(FP4X4),
+                    lhsT_scale=a_s[:, c0 : c0 + P],
+                    rhs=v_w[a][j][:, first : first + CHUNK].bitcast(FP8X4),
+                    rhs_scale=a_s[:, s0 : s0 + CHUNK],
+                    start=(a == 0 and t == 0),
+                    stop=(a == kpasses - 1 and t == PACK - 1),
                 )
 
-        def quantise_w3(g, stage):
-            for u in range(2):
-                cols = slice(2 * u * P, (2 * u + 2) * P)
-                quantise(w3_c[g][:, cols], w3_q[g][:, cols], stage[:, cols.start * PACK : cols.stop * PACK])
+        def round_w3(g, stage):
+            nc.vector.tensor_copy(
+                stage[:].rearrange("p (c i j) -> p c j i", i=4, j=PACK),
+                w_raw[g][:].rearrange("p j (c i) -> p c j i", i=4),
+            )
 
-        def weave(g, j, cols):
+        def weave(g, c, root, h_bf):
+            first = (c % per_half) * CHUNK
             nc.vector.tensor_tensor(
-                staged[g][:, cols.start * PACK : cols.stop * PACK].rearrange("p (c i t) -> p c t i", i=4, t=PACK),
-                mags[j][g][:, :, cols].rearrange("p t (c i) -> p c t i", i=4),
-                damp[g][j][:, :, cols].rearrange("p t (c i) -> p c t i", i=4),
+                h_bf[:, g, :].rearrange("p (c i t) -> p c t i", i=4, t=PACK),
+                root[:, g, :].rearrange("p (t c i) -> p c t i", i=4, t=PACK),
+                damp[g][c // per_half][:, :, first : first + CHUNK].rearrange("p t (c i) -> p c t i", i=4),
                 MULT,
             )
 
-        def pack(g, j, cols):
-            entries = slice(j * HALF + cols.start, j * HALF + cols.stop)
-            quantise(h_c[g][:, entries], h_q[g][:, entries], staged[g][:, cols.start * PACK : cols.stop * PACK])
-
-        def flux_pass(acc, n0, j, cols, g):
-            entries = slice(j * HALF + cols.start, j * HALF + cols.stop)
+        def flux(acc, n0, g, h_c, h_q):
             tiles = acc.shape[1]
             for u in range(tiles):
                 bands = slice((n0 + u) * P, (n0 + u + 1) * P)
@@ -318,89 +277,65 @@ def tile_list_asteroid_band_fluxes_kernel(
                     out=acc[:, u, :],
                     lhsT=w3_c[g][:, bands].bitcast(FP8X4),
                     lhsT_scale=w3_q[g][:, bands],
-                    rhs=h_c[g][:, entries].bitcast(FP8X4),
-                    rhs_scale=h_q[g][:, entries],
+                    rhs=h_c[:, g, :].bitcast(FP8X4),
+                    rhs_scale=h_q[:, g, :],
                     start=(g == 0 and u == 0),
                     stop=(g == groups - 1 and u == tiles - 1),
                 )
 
-        def open_sums(j, cols, tiles, first):
-            accs = []
-            width = cols.stop - cols.start
-            for n0 in range(0, N // P, tiles):
-                acc = bank_of[first + n0 // tiles][:, 0 : tiles * width].rearrange("p (u j) -> p u j", u=tiles)
-                flux_pass(acc, n0, j, cols, 0)
-                accs.append((acc, n0, j, cols))
-            return accs
+        def sums_in(bank, tiles):
+            return bank[:, 0 : tiles * CHUNK].rearrange("p (u j) -> p u j", u=tiles)
 
-        def close_sums(accs):
-            for acc, n0, j, cols in accs:
-                flux_pass(acc, n0, j, cols, 1)
-
-        def store(copy, acc, n0, j, cols, res=None):
+        def store(copy, acc, n0, c):
             tiles = acc.shape[1]
-            if res is None:
-                res = ring.tile([P, tiles, cols.stop - cols.start], F32, name="res", align_bytes=64, bufs=6)[:]
-            copy(res, acc)
-            rows = out[n0 * P : (n0 + tiles) * P, j * HALF + cols.start : j * HALF + cols.stop]
-            nc.sync.dma_start(rows.rearrange("(u p) j -> p u j", p=P), res)
+            res = ring.tile([P, tiles, CHUNK], F32, name="res", align_bytes=64, bufs=4)
+            copy(res[:], acc)
+            rows = out[n0 * P : (n0 + tiles) * P, c * CHUNK : (c + 1) * CHUNK]
+            nc.sync.dma_start(rows.rearrange("(u p) j -> p u j", p=P), res[:])
 
-        whole, left, right = slice(0, HALF), slice(0, 256), slice(256, HALF)
-        third, fourth = slice(256, 384), slice(384, HALF)
-        on_vector, on_scalar = nc.vector.tensor_copy, nc.scalar.copy
-
-        banks = product_a(0, 0)
-        round_w3(0, staged[0])
-        quantise_w3(0, staged[0])
-        for cols in (left, right):
-            magnitudes(0, 0, banks, cols)
-            root(0, 0, cols)
-            weave(0, 0, cols)
-        round_w3(1, staged[1])
-        quantise_w3(1, staged[1])
-        for cols in (left, right):
-            pack(0, 0, cols)
-
-        magnitudes(1, 0, product_a(1, 0), whole)
-        sums = [open_sums(0, left, 2, 4), open_sums(0, right, 2, 6)]
-        for cols in (left, right):
-            root(1, 0, cols)
-            weave(1, 0, cols)
-        for u, cols in enumerate((left, right)):
-            pack(1, 0, cols)
-            close_sums(sums[u])
-        store(on_vector, *sums[0][0])
-        store(on_vector, *sums[0][1])
-        store(on_vector, *sums[1][0])
-        store(on_vector, *sums[1][1])
-
-        banks = product_a(0, 1)
-        for cols in (left, right):
-            magnitudes(0, 1, banks, cols)
-        for cols in (left, right):
-            root(0, 1, cols)
-            weave(0, 1, cols)
-        for cols in (left, right):
-            pack(0, 1, cols)
-
-        banks = product_a(1, 1)
-        sums_left = open_sums(1, left, 2, 0)
-        sums_third = open_sums(1, third, 4, 2)
-        for cols in (left, third, fourth):
-            magnitudes(1, 1, banks, cols)
-            root(1, 1, cols)
-        sums_fourth = open_sums(1, fourth, 2, 3)
-        weave(1, 1, left)
-        weave(1, 1, third)
-        pack(1, 1, left)
-        close_sums(sums_left)
-        weave(1, 1, fourth)
-        pack(1, 1, third)
-        close_sums(sums_third)
-        pack(1, 1, fourth)
-        close_sums(sums_fourth)
-        store(on_scalar, *sums_left[0])
-        store(on_scalar, *sums_left[1])
-        store(on_vector, *sums_third[0], damp[1][1][:, :, fourth])
-        store(on_vector, *sums_fourth[0])
-        store(on_scalar, *sums_fourth[1])
+        early = [(g, c) for c in range(per_half) for g in range(groups) if g == 0 or c < 2]
+        for g, c in early:
+            pass_a(g, c, 0)
+        for g in range(groups):
+            round_w3(g, staged[g])
+        for g in range(groups):
+            quantise(w3_c[g][:], w3_q[g][:], staged[g][:])
+        waiting = []
+        for c in range(chunks):
+            root = ring.tile([P, groups, PACK * CHUNK], F32, name="root", align_bytes=64, bufs=3)
+            h_bf = ring.tile([P, groups, PACK * CHUNK], BF16, name="h_bf", align_bytes=64, bufs=2)
+            h_c = ring.tile([P, groups, CHUNK], U32, name="h_c", align_bytes=64, bufs=4)
+            h_q = ring.tile([P, groups, CHUNK], U8, name="h_q", align_bytes=64, bufs=4)
+            for g in range(groups):
+                if (g, c) not in early:
+                    pass_a(g, c, 0)
+                pass_a(g, c, 1)
+                nc.scalar.activation(root[:, g, :], bank_a(g, c)[:], ACT.Abs)
+                if c == last:
+                    nc.scalar.activation(root[:, g, :], root[:, g, :], ACT.Sqrt)
+            if c < last:
+                nc.scalar.activation(root[:], root[:], ACT.Sqrt)
+                for g in range(groups):
+                    weave(g, c, root, h_bf)
+                if 0 < c < last - 1:
+                    store(nc.vector.tensor_copy, *waiting.pop())
+                quantise(
+                    h_c[:].rearrange("p g c -> p (g c)"),
+                    h_q[:].rearrange("p g c -> p (g c)"),
+                    h_bf[:].rearrange("p g c -> p (g c)"),
+                )
+                acc = sums_in(bank_of[6 + c % 2], N // P)
+                for g in range(groups):
+                    flux(acc, 0, g, h_c, h_q)
+                waiting.append((acc, 0, c))
+            else:
+                accs = [(sums_in(bank_of[2], 2), 0), (sums_in(bank_of[3], 2), 2)]
+                for g in range(groups):
+                    weave(g, c, root, h_bf)
+                    quantise(h_c[:, g, :], h_q[:, g, :], h_bf[:, g, :])
+                    for acc, n0 in accs:
+                        flux(acc, n0, g, h_c, h_q)
+                for held_back in waiting:
+                    store(nc.scalar.copy, *held_back)
+                store(nc.vector.tensor_copy, *accs[0], c)
+                store(nc.scalar.copy, *accs[1], c)

@@ -25,8 +25,10 @@ PASS = P * PACK
 HALF = 512
 RUN = 8
 QUADS = 4
-SQUARES_ON_VECTOR = {(1, 0, 0), (1, 0, 1), (1, 1, 0), (1, 1, 1)}
+SQUARES_ON_VECTOR = {(1, 0, 0), (1, 0, 1)}
 CHUNK = 128
+SIGNED = 2
+TINY = 2.0**-80
 FIRST_CASTS_ON_SCALAR = (1, 2)
 
 
@@ -154,7 +156,7 @@ def tile_list_asteroid_band_fluxes_kernel(
 
         def product_b(g, j, t, helped):
             cols = slice(t * P, (t + 1) * P)
-            bank = bank_of[6 + turns[1] % 2] if helped else bank_of[(2, 2, 4, 5)[t] if j else t % 2] if g else bank_of[turns[0] % 6]
+            bank = bank_of[6 + turns[1] % 2] if helped else bank_of[(2, 3, 4, 5)[t] if j else t % 2] if g else bank_of[turns[0] % 6]
             turns[helped] = turns[helped] + 1
             nc.tensor.matmul_mx(
                 out=bank[:],
@@ -178,18 +180,24 @@ def tile_list_asteroid_band_fluxes_kernel(
             for t, bank, twin in taken:
                 nc.vector.tensor_tensor(damp[g][j][:, t, :], bank[:], twin[:], MULT)
 
-        def side_b(g, j):
+        def squares_on_scalar(g, j):
             for t in range(PACK):
                 if (g, j, t) not in SQUARES_ON_VECTOR:
                     bank = product_b(g, j, t, 0)
                     nc.scalar.activation(damp[g][j][:, t, :], bank[:], ACT.Square)
+
+        def damping(g, j):
+            first = SIGNED * CHUNK if j == 0 else 0
             for t in range(PACK):
                 unit = inverse2[:, g * PACK + t : g * PACK + t + 1]
-                part = damp[g][j][:, t, :]
+                part = damp[g][j][:, t, first:HALF]
                 nc.scalar.activation(part, part, ACT.Abs_reciprocal_sqrt, bias=unit, scale=unit)
 
-        side_b(0, 0)
-        side_b(0, 1)
+        for j in range(halves):
+            squares_on_scalar(0, j)
+        for j in range(halves):
+            damping(0, j)
+
         def deal(dst, src, words):
             nc.vector.tensor_copy(
                 dst.bitcast(I32).rearrange("p g (t b w) -> p g b t w", t=PACK, w=words),
@@ -221,8 +229,11 @@ def tile_list_asteroid_band_fluxes_kernel(
             squares_on_vector(1, j)
         w1_wp = held([P, kpasses * H], U16, "w1_wp")
         deal(w1_wp[:].rearrange("p (u c) -> p u c", c=PASS), w1_w[:], 4)
-        side_b(1, 0)
-        side_b(1, 1)
+        for j in range(halves):
+            squares_on_scalar(1, j)
+        for j in range(halves):
+            damping(1, j)
+
         def gather_words(a, j):
             nc.vector.tensor_copy(v_w[a][j][:], tab_w[a][:].bitcast(U32).indirect(picks(idx, j)))
 
@@ -236,7 +247,7 @@ def tile_list_asteroid_band_fluxes_kernel(
         last = chunks - 1
 
         def bank_a(g, c):
-            return bank_of[4 + c % 2] if g else bank_of[c % 4]
+            return bank_of[groups * c + g] if c < SIGNED else bank_of[4 + groups * (c % 2) + g]
 
         def pass_a(g, c, a):
             j, first = c // per_half, (c % per_half) * CHUNK
@@ -255,16 +266,22 @@ def tile_list_asteroid_band_fluxes_kernel(
                 )
 
         def round_w3(g, stage):
-            nc.vector.tensor_copy(
-                stage[:].rearrange("p (c i j) -> p c j i", i=4, j=PACK),
-                w_raw[g][:].rearrange("p j (c i) -> p c j i", i=4),
-            )
+            for u in range(4):
+                cols = slice(u * P, (u + 1) * P)
+                nc.gpsimd.tensor_scalar(
+                    stage[:].rearrange("p (c j) -> p c j", j=PACK)[:, cols],
+                    w_raw[g][:].rearrange("p j c -> p c j")[:, cols],
+                    1.0,
+                    0.0,
+                    MULT,
+                    ADD,
+                )
 
         def weave(g, c, root, h_bf):
             first = (c % per_half) * CHUNK
             nc.vector.tensor_tensor(
                 h_bf[:, g, :].rearrange("p (c i t) -> p c t i", i=4, t=PACK),
-                root[:, g, :].rearrange("p (t c i) -> p c t i", i=4, t=PACK),
+                root.rearrange("p (t c i) -> p c t i", i=4, t=PACK),
                 damp[g][c // per_half][:, :, first : first + CHUNK].rearrange("p t (c i) -> p c t i", i=4),
                 MULT,
             )
@@ -293,49 +310,112 @@ def tile_list_asteroid_band_fluxes_kernel(
             rows = out[n0 * P : (n0 + tiles) * P, c * CHUNK : (c + 1) * CHUNK]
             nc.sync.dma_start(rows.rearrange("(u p) j -> p u j", p=P), res[:])
 
-        early = [(g, c) for c in range(per_half) for g in range(groups) if g == 0 or c < 2]
-        for g, c in early:
-            pass_a(g, c, 0)
-        for g in range(groups):
-            round_w3(g, staged[g])
-        for g in range(groups):
-            quantise(w3_c[g][:], w3_q[g][:], staged[g][:])
-        waiting = []
-        for c in range(chunks):
-            root = ring.tile([P, groups, PACK * CHUNK], F32, name="root", align_bytes=64, bufs=3)
-            h_bf = ring.tile([P, groups, PACK * CHUNK], BF16, name="h_bf", align_bytes=64, bufs=2)
+        def pack(h_bf):
             h_c = ring.tile([P, groups, CHUNK], U32, name="h_c", align_bytes=64, bufs=4)
             h_q = ring.tile([P, groups, CHUNK], U8, name="h_q", align_bytes=64, bufs=4)
+            quantise(
+                h_c[:].rearrange("p g c -> p (g c)"),
+                h_q[:].rearrange("p g c -> p (g c)"),
+                h_bf.rearrange("p g c -> p (g c)"),
+            )
+            return h_c, h_q
+
+        def staging(c):
+            return staged[c // 2 % 2][:].rearrange("p (u g c) -> p u g c", u=2, g=groups)[:, c % 2]
+
+        for c in range(per_half):
             for g in range(groups):
-                if (g, c) not in early:
+                pass_a(g, c, 0)
+        for c in range(SIGNED):
+            for g in range(groups):
+                pass_a(g, c, 1)
+        for g in range(groups):
+            round_w3(g, staged[g])
+
+        width = SIGNED * CHUNK
+        joint = held([P, PACK, groups, width], F32, "joint")
+        spare = joint[:].rearrange("p (u t) g c -> p u (t g c)", u=2)
+        mags = [held([P, groups * PACK * CHUNK], F32, "mag%d" % u) for u in range(2)]
+
+        def magnitudes(c, into):
+            for g in range(groups):
+                if c >= per_half:
                     pass_a(g, c, 0)
                 pass_a(g, c, 1)
-                nc.scalar.activation(root[:, g, :], bank_a(g, c)[:], ACT.Abs)
-                if c == last:
-                    nc.scalar.activation(root[:, g, :], root[:, g, :], ACT.Sqrt)
-            if c < last:
-                nc.scalar.activation(root[:], root[:], ACT.Sqrt)
-                for g in range(groups):
-                    weave(g, c, root, h_bf)
-                if 0 < c < last - 1:
-                    store(nc.vector.tensor_copy, *waiting.pop())
-                quantise(
-                    h_c[:].rearrange("p g c -> p (g c)"),
-                    h_q[:].rearrange("p g c -> p (g c)"),
-                    h_bf[:].rearrange("p g c -> p (g c)"),
+                nc.scalar.activation(into[:, g * HALF : (g + 1) * HALF], bank_a(g, c)[:], ACT.Abs)
+
+        magnitudes(SIGNED, mags[0][:])
+        for g in range(groups):
+            for c in range(SIGNED):
+                cols = slice(c * CHUNK, (c + 1) * CHUNK)
+                nc.vector.scalar_tensor_tensor(
+                    joint[:, :, g, cols],
+                    damp[g][0][:, :, cols],
+                    1.0,
+                    bank_a(g, c)[:].rearrange("p (t c) -> p t c", t=PACK),
+                    ADD,
+                    MULT,
                 )
-                acc = sums_in(bank_of[6 + c % 2], N // P)
-                for g in range(groups):
-                    flux(acc, 0, g, h_c, h_q)
-                waiting.append((acc, 0, c))
+            for t in range(PACK):
+                unit = inverse2[:, g * PACK + t : g * PACK + t + 1]
+                nc.scalar.activation(
+                    damp[g][0][:, t, 0:width], joint[:, t, g, :], ACT.Abs_reciprocal_sqrt, bias=TINY, scale=unit
+                )
+        magnitudes(SIGNED + 1, mags[1][:])
+        signed = [held([P, groups, PACK * CHUNK], BF16, "signed%d" % c) for c in range(SIGNED)]
+        mirror = [held([P, groups * PACK * CHUNK], BF16, "mirror%d" % c) for c in range(SIGNED)]
+        for g in range(groups):
+            for c in range(SIGNED):
+                weave(g, c, bank_a(g, c)[:], signed[c])
+        for c in range(SIGNED):
+            flat = signed[c][:].rearrange("p g c -> p (g c)")
+            nc.vector.tensor_scalar(mirror[c][:], flat, -1.0, None, MULT)
+        for c in range(SIGNED):
+            flat = signed[c][:].rearrange("p g c -> p (g c)")
+            nc.vector.tensor_tensor(flat, flat, mirror[c][:], MAX)
+        packed = [pack(signed[c][:]) for c in range(SIGNED)]
+        for g in range(groups):
+            quantise(w3_c[g][:], w3_q[g][:], staged[g][:])
+        sums = {}
+
+        def open_sums(c, h_c, h_q):
+            sums[c] = sums_in(bank_of[c % 4], N // P)
+            for g in range(groups):
+                flux(sums[c], 0, g, h_c, h_q)
+
+        for c in range(SIGNED):
+            open_sums(c, *packed[c])
+
+        for c in range(SIGNED, chunks):
+            u = c % 2
+            if c < SIGNED + 2:
+                root = spare[:, 1 - u, :]
+                nc.scalar.activation(root, mags[u][:], ACT.Sqrt)
             else:
-                accs = [(sums_in(bank_of[2], 2), 0), (sums_in(bank_of[3], 2), 2)]
+                root = mags[u][:] if c < SIGNED + 4 else spare[:, 1 - u, :]
+                magnitudes(c, root)
+                if c < last:
+                    nc.scalar.activation(root, root, ACT.Sqrt)
+                else:
+                    for g in range(groups):
+                        part = root[:, g * HALF : (g + 1) * HALF]
+                        nc.scalar.activation(part, part, ACT.Sqrt)
+            h_bf = staging(c)
+            if c < last:
                 for g in range(groups):
-                    weave(g, c, root, h_bf)
+                    weave(g, c, root[:, g * HALF : (g + 1) * HALF], h_bf)
+                for done in {SIGNED: (0,), SIGNED + 1: (1, 2)}.get(c, (c - 1,)):
+                    store(nc.vector.tensor_copy, sums[done], 0, done)
+                open_sums(c, *pack(h_bf))
+            else:
+                h_c = ring.tile([P, groups, CHUNK], U32, name="h_c", align_bytes=64, bufs=4)
+                h_q = ring.tile([P, groups, CHUNK], U8, name="h_q", align_bytes=64, bufs=4)
+                accs = [(sums_in(bank_of[4], 2), 0), (sums_in(bank_of[5], 2), 2)]
+                for g in range(groups):
+                    weave(g, c, root[:, g * HALF : (g + 1) * HALF], h_bf)
                     quantise(h_c[:, g, :], h_q[:, g, :], h_bf[:, g, :])
                     for acc, n0 in accs:
                         flux(acc, n0, g, h_c, h_q)
-                for held_back in waiting:
-                    store(nc.scalar.copy, *held_back)
+                store(nc.scalar.copy, sums[c - 1], 0, c - 1)
                 store(nc.vector.tensor_copy, *accs[0], c)
                 store(nc.scalar.copy, *accs[1], c)

@@ -28,6 +28,7 @@ QUADS = 4
 SQUARES_ON_VECTOR = {(1, 0, 0), (1, 0, 1)}
 CHUNK = 128
 SIGNED = 2
+COPIES_ON_SCALAR = (0, 1, 2)
 TINY = 2.0**-80
 FIRST_CASTS_ON_SCALAR = (1, 2)
 
@@ -266,16 +267,10 @@ def tile_list_asteroid_band_fluxes_kernel(
                 )
 
         def round_w3(g, stage):
-            for u in range(4):
-                cols = slice(u * P, (u + 1) * P)
-                nc.gpsimd.tensor_scalar(
-                    stage[:].rearrange("p (c j) -> p c j", j=PACK)[:, cols],
-                    w_raw[g][:].rearrange("p j c -> p c j")[:, cols],
-                    1.0,
-                    0.0,
-                    MULT,
-                    ADD,
-                )
+            nc.vector.tensor_copy(
+                stage[:].rearrange("p (c i j) -> p c j i", i=4, j=PACK),
+                w_raw[g][:].rearrange("p j (c i) -> p c j i", i=4),
+            )
 
         def weave(g, c, root, h_bf):
             first = (c % per_half) * CHUNK
@@ -329,9 +324,6 @@ def tile_list_asteroid_band_fluxes_kernel(
         for c in range(SIGNED):
             for g in range(groups):
                 pass_a(g, c, 1)
-        for g in range(groups):
-            round_w3(g, staged[g])
-
         width = SIGNED * CHUNK
         joint = held([P, PACK, groups, width], F32, "joint")
         spare = joint[:].rearrange("p (u t) g c -> p u (t g c)", u=2)
@@ -362,6 +354,7 @@ def tile_list_asteroid_band_fluxes_kernel(
                     damp[g][0][:, t, 0:width], joint[:, t, g, :], ACT.Abs_reciprocal_sqrt, bias=TINY, scale=unit
                 )
         magnitudes(SIGNED + 1, mags[1][:])
+        round_w3(0, staged[0])
         signed = [held([P, groups, PACK * CHUNK], BF16, "signed%d" % c) for c in range(SIGNED)]
         mirror = [held([P, groups * PACK * CHUNK], BF16, "mirror%d" % c) for c in range(SIGNED)]
         for g in range(groups):
@@ -373,6 +366,7 @@ def tile_list_asteroid_band_fluxes_kernel(
         for c in range(SIGNED):
             flat = signed[c][:].rearrange("p g c -> p (g c)")
             nc.vector.tensor_tensor(flat, flat, mirror[c][:], MAX)
+        round_w3(1, staged[1])
         packed = [pack(signed[c][:]) for c in range(SIGNED)]
         for g in range(groups):
             quantise(w3_c[g][:], w3_q[g][:], staged[g][:])
@@ -400,12 +394,14 @@ def tile_list_asteroid_band_fluxes_kernel(
                     for g in range(groups):
                         part = root[:, g * HALF : (g + 1) * HALF]
                         nc.scalar.activation(part, part, ACT.Sqrt)
+            if c - 4 in COPIES_ON_SCALAR:
+                store(nc.scalar.copy, sums[c - 4], 0, c - 4)
             h_bf = staging(c)
             if c < last:
                 for g in range(groups):
                     weave(g, c, root[:, g * HALF : (g + 1) * HALF], h_bf)
-                for done in {SIGNED: (0,), SIGNED + 1: (1, 2)}.get(c, (c - 1,)):
-                    store(nc.vector.tensor_copy, sums[done], 0, done)
+                if c - 1 not in COPIES_ON_SCALAR:
+                    store(nc.vector.tensor_copy, sums[c - 1], 0, c - 1)
                 open_sums(c, *pack(h_bf))
             else:
                 h_c = ring.tile([P, groups, CHUNK], U32, name="h_c", align_bytes=64, bufs=4)

@@ -89,9 +89,8 @@ def tile_list_asteroid_band_fluxes_kernel(
         nc.sync.dma_start(idx[:], offs)
         nc.sync.dma_start(tab_s[32:96:2, :].bitcast(I32), tab_scales.rearrange("a q t -> q a t").bitcast(I32))
         nc.vector.tensor_copy(v2_rows[:], tab2_s[:].indirect(idx2[:]))
-        for q in range(QUADS):
-            src = v2_rows[P - 16 + 4 * q : P - 12 + 4 * q, :]
-            nc.sync.dma_start(v2_s[32 * q : 32 * q + 4, :].bitcast(I32), src.bitcast(I32))
+        for r in range(QUADS):
+            nc.sync.dma_start(v2_s[r:P:32, :].bitcast(I32), v2_rows[P - 16 + r : P : 4, :].bitcast(I32))
         nc.sync.dma_start(w_raw[1][:], w2_rows[:, :, PASS : 2 * PASS])
         nc.sync.dma_start(w1_rows[32:96:2, :].bitcast(I32), w1_scales.rearrange("a q c -> q a c").bitcast(I32))
 
@@ -208,10 +207,15 @@ def tile_list_asteroid_band_fluxes_kernel(
         nc.vector.tensor_copy(v_rows[:], tab_s[:].indirect(idx[:]))
         deal(joined[:, S : S + H].rearrange("p (g c) -> p g c", g=groups), w1_rows[:], 2)
         nc.vector.tensor_copy(joined[:, 0:S].bitcast(I32), v_rows[:].bitcast(I32))
-        for q in range(QUADS):
-            src = joined[32 + 16 * q : 48 + 16 * q : 2, :]
-            nc.sync.dma_start(a_s[32 * q : 32 * q + 4, :].bitcast(I32), src.bitcast(I32))
+
+        def spread_a(a):
+            for r in range(QUADS):
+                src = joined[32 + 2 * a + 4 * r : 96 : 16, :]
+                nc.sync.dma_start(a_s[r:P:32, a * (S + H) : (a + 1) * (S + H)].bitcast(I32), src.bitcast(I32))
+
+        spread_a(0)
         load_tab(1)
+        spread_a(1)
 
         for u in range(2):
             nc.vector.tensor_copy(

@@ -28,9 +28,9 @@ QUADS = 4
 SQUARES_ON_VECTOR = {(1, 0, 0), (1, 0, 1)}
 CHUNK = 128
 SIGNED = 2
-COPIES_ON_SCALAR = (0, 1, 2)
+COPIES_ON_SCALAR = (0, 1, 2, 6)
 TINY = 2.0**-80
-FIRST_CASTS_ON_SCALAR = (1, 2)
+FIRST_CASTS_ON_SCALAR = (1, 2, 3)
 
 
 def tile_list_asteroid_band_fluxes_kernel(
@@ -63,7 +63,8 @@ def tile_list_asteroid_band_fluxes_kernel(
         tab_w = [held([P, T], I32, "tab_w%d" % a) for a in range(kpasses)]
         w1_w = held([P, kpasses * H], U16, "w1_w")
         w_raw = [held([P, PACK, PASS], F32, "w_raw%d" % g) for g in range(groups)]
-        emis_rows = held([P, groups * P], F32, "emis_rows")
+        emis_raw = held([groups, PASS], F32, "emis_raw")
+        emis_rows = held([P, PASS], F32, "emis_rows")
         ident = held([P, P], F32, "ident")
         inverse = held([P, groups * PACK], F32, "inverse")
         inverse2 = held([P, groups * PACK], F32, "inverse2")
@@ -76,6 +77,7 @@ def tile_list_asteroid_band_fluxes_kernel(
         one = held([P, 1], F32, "one")
         warm = held([P, 1], F32, "warm")
         nc.gpsimd.memset(one[:], 1.0)
+        nc.scalar.dma_start(emis_raw[:], emis.rearrange("(g c) -> g c", g=groups))
         nc.scalar.activation(warm[:], one[:], ACT.Abs_reciprocal_sqrt)
 
         nc.gpsimd.memset(emis_rows[:], 0.0)
@@ -101,9 +103,6 @@ def tile_list_asteroid_band_fluxes_kernel(
         def load_tab(a):
             nc.sync.dma_start(tab_w[a][:], tab_words[a].rearrange("p t i -> p (t i)").bitcast(I32))
 
-        nc.sync.dma_start(
-            emis_rows[0:PACK, :].rearrange("t (b i) -> t b i", i=RUN), emis.rearrange("(b t i) -> t b i", t=PACK, i=RUN)
-        )
         load_tab(0)
 
 
@@ -144,11 +143,15 @@ def tile_list_asteroid_band_fluxes_kernel(
         damp = [[held([P, PACK, HALF], F32, "damp%d_%d" % (g, j)) for j in range(halves)] for g in range(groups)]
 
         turned = bank_of[7]
-        for g in range(groups):
-            nc.tensor.transpose(turned[:, g * P : (g + 1) * P], emis_rows[:, g * P : (g + 1) * P], ident[:])
+        nc.scalar.copy(
+            emis_rows[0:groups, :].rearrange("g (t b i) -> g t b i", t=PACK, i=RUN),
+            emis_raw[:].rearrange("g (b t i) -> g t b i", t=PACK, i=RUN),
+        )
+        for t in range(PACK):
+            nc.tensor.transpose(turned[:, t * P : (t + 1) * P], emis_rows[:, t * P : (t + 1) * P], ident[:])
         nc.vector.reciprocal(
-            inverse[:].rearrange("p (g t) -> p g t", g=groups),
-            turned[:, 0 : groups * P].rearrange("p (g c) -> p g c", g=groups)[:, :, 0:PACK],
+            inverse[:].rearrange("p (g t) -> p t g", g=groups),
+            turned[:].rearrange("p (t c) -> p t c", t=PACK)[:, :, 0:groups],
         )
         nc.vector.tensor_tensor(inverse2[:], inverse[:], inverse[:], MULT)
 
@@ -302,12 +305,12 @@ def tile_list_asteroid_band_fluxes_kernel(
         def sums_in(bank, tiles):
             return bank[:, 0 : tiles * CHUNK].rearrange("p (u j) -> p u j", u=tiles)
 
-        def store(copy, acc, n0, c):
+        def store(copy, acc, n0, c, queue=nc.sync):
             tiles = acc.shape[1]
             res = ring.tile([P, tiles, CHUNK], F32, name="res", align_bytes=64, bufs=4)
             copy(res[:], acc)
             rows = out[n0 * P : (n0 + tiles) * P, c * CHUNK : (c + 1) * CHUNK]
-            nc.sync.dma_start(rows.rearrange("(u p) j -> p u j", p=P), res[:])
+            queue.dma_start(rows.rearrange("(u p) j -> p u j", p=P), res[:])
 
         def pack(h_bf):
             h_c = ring.tile([P, groups, CHUNK], U32, name="h_c", align_bytes=64, bufs=4)
@@ -416,6 +419,7 @@ def tile_list_asteroid_band_fluxes_kernel(
                     quantise(h_c[:, g, :], h_q[:, g, :], h_bf[:, g, :])
                     for acc, n0 in accs:
                         flux(acc, n0, g, h_c, h_q)
-                store(nc.scalar.copy, sums[c - 1], 0, c - 1)
+                for done in (c - 1,):
+                    store(nc.scalar.copy, sums[done], 0, done)
                 store(nc.vector.tensor_copy, *accs[0], c)
-                store(nc.scalar.copy, *accs[1], c)
+                store(nc.scalar.copy, *accs[1], c, nc.scalar)

@@ -25,10 +25,10 @@ PASS = P * PACK
 HALF = 512
 RUN = 8
 QUADS = 4
-SQUARES_ON_VECTOR = {(1, 0, 0), (1, 0, 1)}
+SQUARES_ON_VECTOR = {(1, 0, 0), (1, 0, 1), (1, 1, 0)}
 CHUNK = 128
 SIGNED = 2
-COPIES_ON_SCALAR = (0, 1, 2, 6)
+COPIES_ON_SCALAR = (0, 1, 4, 5, 6)
 TINY = 2.0**-80
 FIRST_CASTS_ON_SCALAR = (1, 2, 3)
 
@@ -328,23 +328,26 @@ def tile_list_asteroid_band_fluxes_kernel(
         for c in range(per_half):
             for g in range(groups):
                 pass_a(g, c, 0)
-        for c in range(SIGNED):
-            for g in range(groups):
-                pass_a(g, c, 1)
+        for g, c in ((0, 2), (1, 2), (0, 0), (0, 1), (0, 3), (1, 0), (1, 3), (1, 1)):
+            pass_a(g, c, 1)
         width = SIGNED * CHUNK
         joint = held([P, PACK, groups, width], F32, "joint")
         spare = joint[:].rearrange("p (u t) g c -> p u (t g c)", u=2)
         mags = [held([P, groups * PACK * CHUNK], F32, "mag%d" % u) for u in range(2)]
 
+        def magnitude(g, c, into):
+            nc.scalar.activation(into[:, g * HALF : (g + 1) * HALF], bank_a(g, c)[:], ACT.Abs)
+
         def magnitudes(c, into):
             for g in range(groups):
-                if c >= per_half:
-                    pass_a(g, c, 0)
-                pass_a(g, c, 1)
-                nc.scalar.activation(into[:, g * HALF : (g + 1) * HALF], bank_a(g, c)[:], ACT.Abs)
+                for a in range(kpasses):
+                    pass_a(g, c, a)
+                magnitude(g, c, into)
 
-        magnitudes(SIGNED, mags[0][:])
         for g in range(groups):
+            magnitude(g, SIGNED, mags[0][:])
+        for g in range(groups):
+            magnitude(g, SIGNED + 1, mags[1][:])
             for c in range(SIGNED):
                 cols = slice(c * CHUNK, (c + 1) * CHUNK)
                 nc.vector.scalar_tensor_tensor(
@@ -360,7 +363,6 @@ def tile_list_asteroid_band_fluxes_kernel(
                 nc.scalar.activation(
                     damp[g][0][:, t, 0:width], joint[:, t, g, :], ACT.Abs_reciprocal_sqrt, bias=TINY, scale=unit
                 )
-        magnitudes(SIGNED + 1, mags[1][:])
         round_w3(0, staged[0])
         signed = [held([P, groups, PACK * CHUNK], BF16, "signed%d" % c) for c in range(SIGNED)]
         mirror = [held([P, groups * PACK * CHUNK], BF16, "mirror%d" % c) for c in range(SIGNED)]
@@ -387,7 +389,7 @@ def tile_list_asteroid_band_fluxes_kernel(
         for c in range(SIGNED):
             open_sums(c, *packed[c])
 
-        for c in range(SIGNED, chunks):
+        def roots_of(c):
             u = c % 2
             if c < SIGNED + 2:
                 root = spare[:, 1 - u, :]
@@ -401,8 +403,15 @@ def tile_list_asteroid_band_fluxes_kernel(
                     for g in range(groups):
                         part = root[:, g * HALF : (g + 1) * HALF]
                         nc.scalar.activation(part, part, ACT.Sqrt)
-            if c - 4 in COPIES_ON_SCALAR:
-                store(nc.scalar.copy, sums[c - 4], 0, c - 4)
+            if c - 5 in range(SIGNED):
+                store(nc.scalar.copy, sums[c - 5], 0, c - 5)
+            return root
+
+        ahead = roots_of(SIGNED)
+        for c in range(SIGNED, chunks):
+            root = ahead
+            if c < last:
+                ahead = roots_of(c + 1)
             h_bf = staging(c)
             if c < last:
                 for g in range(groups):
@@ -419,7 +428,7 @@ def tile_list_asteroid_band_fluxes_kernel(
                     quantise(h_c[:, g, :], h_q[:, g, :], h_bf[:, g, :])
                     for acc, n0 in accs:
                         flux(acc, n0, g, h_c, h_q)
-                for done in (c - 1,):
+                for done in (c - 3, c - 2, c - 1):
                     store(nc.scalar.copy, sums[done], 0, done)
                 store(nc.vector.tensor_copy, *accs[0], c)
                 store(nc.scalar.copy, *accs[1], c, nc.scalar)

@@ -28,7 +28,8 @@ QUADS = 4
 SQUARES_ON_VECTOR = {(1, 0, 0), (1, 0, 1), (1, 1, 0)}
 CHUNK = 128
 SIGNED = 2
-COPIES_ON_SCALAR = (0, 1, 4, 5, 6)
+COPIES_ON_VECTOR = (2, 4)
+COPIES_BEHIND_ROOT = {5: (0,), 6: (1, 3)}
 TINY = 2.0**-80
 FIRST_CASTS_ON_SCALAR = (1, 2, 3)
 
@@ -159,7 +160,7 @@ def tile_list_asteroid_band_fluxes_kernel(
 
         def product_b(g, j, t, helped):
             cols = slice(t * P, (t + 1) * P)
-            bank = bank_of[6 + turns[1] % 2] if helped else bank_of[(2, 3, 4, 5)[t] if j else t % 2] if g else bank_of[turns[0] % 6]
+            bank = bank_of[(6, 7, 2)[turns[1]]] if helped else bank_of[(2, 3, 4, 5)[t] if j else t % 2] if g else bank_of[turns[0] % 6]
             turns[helped] = turns[helped] + 1
             nc.tensor.matmul_mx(
                 out=bank[:],
@@ -172,16 +173,14 @@ def tile_list_asteroid_band_fluxes_kernel(
             )
             return bank
 
-        def squares_on_vector(g, j):
-            taken = []
-            for t in range(PACK):
-                if (g, j, t) in SQUARES_ON_VECTOR:
-                    bank = product_b(g, j, t, 1)
-                    twin = ring.tile([P, HALF], F32, name="twin", align_bytes=64)
-                    nc.vector.tensor_copy(twin[:], bank[:])
-                    taken.append((t, bank, twin))
-            for t, bank, twin in taken:
-                nc.vector.tensor_tensor(damp[g][j][:, t, :], bank[:], twin[:], MULT)
+        def take(g, j, t):
+            bank = product_b(g, j, t, 1)
+            twin = ring.tile([P, HALF], F32, name="twin", align_bytes=64, bufs=3)
+            nc.vector.tensor_copy(twin[:], bank[:])
+            return damp[g][j][:, t, :], bank, twin
+
+        def square(into, bank, twin):
+            nc.vector.tensor_tensor(into, bank[:], twin[:], MULT)
 
         def squares_on_scalar(g, j):
             for t in range(PACK):
@@ -198,8 +197,6 @@ def tile_list_asteroid_band_fluxes_kernel(
 
         for j in range(halves):
             squares_on_scalar(0, j)
-        for j in range(halves):
-            damping(0, j)
 
         def deal(dst, src, words):
             nc.vector.tensor_copy(
@@ -233,19 +230,20 @@ def tile_list_asteroid_band_fluxes_kernel(
             for t in range(PACK):
                 nc.sync.dma_start(w_raw[g][:, t, :], rows[t])
 
-        for j in range(halves):
-            squares_on_vector(1, j)
-        w1_wp = held([P, kpasses * H], U16, "w1_wp")
-        deal(w1_wp[:].rearrange("p (u c) -> p u c", c=PASS), w1_w[:], 4)
-        for j in range(halves):
-            squares_on_scalar(1, j)
-        for j in range(halves):
-            damping(1, j)
-
         def gather_words(a, j):
             nc.vector.tensor_copy(v_w[a][j][:], tab_w[a][:].bitcast(U32).indirect(picks(idx, j)))
 
+        w1_wp = held([P, kpasses * H], U16, "w1_wp")
+        deal(w1_wp[:].rearrange("p (u c) -> p u c", c=PASS), w1_w[:], 4)
+        taken = [take(*place) for place in sorted(SQUARES_ON_VECTOR)]
+        for j in range(halves):
+            squares_on_scalar(1, j)
         gather_words(0, 0)
+        for held_bank in taken:
+            square(*held_bank)
+        for g in range(groups):
+            for j in range(halves):
+                damping(g, j)
         gather_words(0, 1)
         gather_words(1, 0)
         gather_words(1, 1)
@@ -325,9 +323,8 @@ def tile_list_asteroid_band_fluxes_kernel(
         def staging(c):
             return staged[c // 2 % 2][:].rearrange("p (u g c) -> p u g c", u=2, g=groups)[:, c % 2]
 
-        for c in range(per_half):
-            for g in range(groups):
-                pass_a(g, c, 0)
+        for g, c in ((0, 0), (1, 0), (1, 1), (0, 2), (1, 2), (0, 3), (1, 3), (0, 1)):
+            pass_a(g, c, 0)
         for g, c in ((0, 2), (1, 2), (0, 0), (0, 1), (0, 3), (1, 0), (1, 3), (1, 1)):
             pass_a(g, c, 1)
         width = SIGNED * CHUNK
@@ -403,8 +400,8 @@ def tile_list_asteroid_band_fluxes_kernel(
                     for g in range(groups):
                         part = root[:, g * HALF : (g + 1) * HALF]
                         nc.scalar.activation(part, part, ACT.Sqrt)
-            if c - 5 in range(SIGNED):
-                store(nc.scalar.copy, sums[c - 5], 0, c - 5)
+            for done in COPIES_BEHIND_ROOT.get(c, ()):
+                store(nc.scalar.copy, sums[done], 0, done)
             return root
 
         ahead = roots_of(SIGNED)
@@ -416,7 +413,7 @@ def tile_list_asteroid_band_fluxes_kernel(
             if c < last:
                 for g in range(groups):
                     weave(g, c, root[:, g * HALF : (g + 1) * HALF], h_bf)
-                if c - 1 not in COPIES_ON_SCALAR:
+                if c - 1 in COPIES_ON_VECTOR:
                     store(nc.vector.tensor_copy, sums[c - 1], 0, c - 1)
                 open_sums(c, *pack(h_bf))
             else:
@@ -428,7 +425,7 @@ def tile_list_asteroid_band_fluxes_kernel(
                     quantise(h_c[:, g, :], h_q[:, g, :], h_bf[:, g, :])
                     for acc, n0 in accs:
                         flux(acc, n0, g, h_c, h_q)
-                for done in (c - 3, c - 2, c - 1):
+                for done in (c - 2, c - 1):
                     store(nc.scalar.copy, sums[done], 0, done)
                 store(nc.vector.tensor_copy, *accs[0], c)
                 store(nc.scalar.copy, *accs[1], c, nc.scalar)

@@ -394,12 +394,9 @@ def tile_list_asteroid_band_fluxes_kernel(
             else:
                 root = mags[u][:] if c < SIGNED + 4 else spare[:, 1 - u, :]
                 magnitudes(c, root)
-                if c < last:
-                    nc.scalar.activation(root, root, ACT.Sqrt)
-                else:
-                    for g in range(groups):
-                        part = root[:, g * HALF : (g + 1) * HALF]
-                        nc.scalar.activation(part, part, ACT.Sqrt)
+                for g in range(groups):
+                    part = root[:, g * HALF : (g + 1) * HALF]
+                    nc.scalar.activation(part, part, ACT.Sqrt)
             for done in COPIES_BEHIND_ROOT.get(c, ()):
                 store(nc.scalar.copy, sums[done], 0, done)
             return root
@@ -410,18 +407,20 @@ def tile_list_asteroid_band_fluxes_kernel(
             if c < last:
                 ahead = roots_of(c + 1)
             h_bf = staging(c)
+            weave(0, c, root[:, 0:HALF], h_bf)
+            if c > SIGNED:
+                open_sums(c - 1, *pack(staging(c - 1)))
             if c < last:
-                for g in range(groups):
-                    weave(g, c, root[:, g * HALF : (g + 1) * HALF], h_bf)
-                if c - 1 in COPIES_ON_VECTOR:
-                    store(nc.vector.tensor_copy, sums[c - 1], 0, c - 1)
-                open_sums(c, *pack(h_bf))
+                weave(1, c, root[:, HALF : 2 * HALF], h_bf)
+                if c - 2 in COPIES_ON_VECTOR:
+                    store(nc.vector.tensor_copy, sums[c - 2], 0, c - 2)
             else:
                 h_c = ring.tile([P, groups, CHUNK], U32, name="h_c", align_bytes=64, bufs=4)
                 h_q = ring.tile([P, groups, CHUNK], U8, name="h_q", align_bytes=64, bufs=4)
                 accs = [(sums_in(bank_of[4], 2), 0), (sums_in(bank_of[5], 2), 2)]
                 for g in range(groups):
-                    weave(g, c, root[:, g * HALF : (g + 1) * HALF], h_bf)
+                    if g:
+                        weave(g, c, root[:, g * HALF : (g + 1) * HALF], h_bf)
                     quantise(h_c[:, g, :], h_q[:, g, :], h_bf[:, g, :])
                     for acc, n0 in accs:
                         flux(acc, n0, g, h_c, h_q)

@@ -277,12 +277,12 @@ def tile_list_asteroid_band_fluxes_kernel(
                 w_raw[g][:].rearrange("p j (c i) -> p c j i", i=4),
             )
 
-        def weave(g, c, root, h_bf):
+        def weave(g, c, root, h_bf, cols=slice(0, CHUNK)):
             first = (c % per_half) * CHUNK
             nc.vector.tensor_tensor(
-                h_bf[:, g, :].rearrange("p (c i t) -> p c t i", i=4, t=PACK),
-                root.rearrange("p (t c i) -> p c t i", i=4, t=PACK),
-                damp[g][c // per_half][:, :, first : first + CHUNK].rearrange("p t (c i) -> p c t i", i=4),
+                h_bf[:, g, cols.start * PACK : cols.stop * PACK].rearrange("p (c i t) -> p c t i", i=4, t=PACK),
+                root.rearrange("p (t c) -> p t c", t=PACK)[:, :, cols].rearrange("p t (c i) -> p c t i", i=4),
+                damp[g][c // per_half][:, :, first + cols.start : first + cols.stop].rearrange("p t (c i) -> p c t i", i=4),
                 MULT,
             )
 
@@ -321,7 +321,7 @@ def tile_list_asteroid_band_fluxes_kernel(
             return h_c, h_q
 
         def staging(c):
-            return staged[c // 2 % 2][:].rearrange("p (u g c) -> p u g c", u=2, g=groups)[:, c % 2]
+            return staged[c % 2][:].rearrange("p (u g c) -> p u g c", u=2, g=groups)[:, c // 2 % 2]
 
         for g, c in ((0, 0), (1, 0), (1, 1), (0, 2), (1, 2), (0, 3), (1, 3), (0, 1)):
             pass_a(g, c, 0)
@@ -386,6 +386,10 @@ def tile_list_asteroid_band_fluxes_kernel(
         for c in range(SIGNED):
             open_sums(c, *packed[c])
 
+        def pieces(g, c):
+            cuts = 2 if (g, c) == (groups - 1, last) else 1
+            return [slice(u * CHUNK // cuts, (u + 1) * CHUNK // cuts) for u in range(cuts)]
+
         def roots_of(c):
             u = c % 2
             if c < SIGNED + 2:
@@ -395,8 +399,9 @@ def tile_list_asteroid_band_fluxes_kernel(
                 root = mags[u][:] if c < SIGNED + 4 else spare[:, 1 - u, :]
                 magnitudes(c, root)
                 for g in range(groups):
-                    part = root[:, g * HALF : (g + 1) * HALF]
-                    nc.scalar.activation(part, part, ACT.Sqrt)
+                    for cols in pieces(g, c):
+                        part = root[:, g * HALF : (g + 1) * HALF].rearrange("p (t c) -> p t c", t=PACK)[:, :, cols]
+                        nc.scalar.activation(part, part, ACT.Sqrt)
             for done in COPIES_BEHIND_ROOT.get(c, ()):
                 store(nc.scalar.copy, sums[done], 0, done)
             return root
@@ -408,20 +413,25 @@ def tile_list_asteroid_band_fluxes_kernel(
                 ahead = roots_of(c + 1)
             h_bf = staging(c)
             weave(0, c, root[:, 0:HALF], h_bf)
-            if c > SIGNED:
+            if SIGNED < c < last:
                 open_sums(c - 1, *pack(staging(c - 1)))
             if c < last:
                 weave(1, c, root[:, HALF : 2 * HALF], h_bf)
                 if c - 2 in COPIES_ON_VECTOR:
                     store(nc.vector.tensor_copy, sums[c - 2], 0, c - 2)
+                if c == last - 1:
+                    open_sums(c, *pack(h_bf))
             else:
                 h_c = ring.tile([P, groups, CHUNK], U32, name="h_c", align_bytes=64, bufs=4)
                 h_q = ring.tile([P, groups, CHUNK], U8, name="h_q", align_bytes=64, bufs=4)
                 accs = [(sums_in(bank_of[4], 2), 0), (sums_in(bank_of[5], 2), 2)]
+                left, right = pieces(1, c)
+                weave(1, c, root[:, HALF : 2 * HALF], h_bf, left)
+                quantise(h_c[:, 0, :], h_q[:, 0, :], h_bf[:, 0, :])
+                weave(1, c, root[:, HALF : 2 * HALF], h_bf, right)
+                for cols in (left, right):
+                    quantise(h_c[:, 1, cols], h_q[:, 1, cols], h_bf[:, 1, cols.start * PACK : cols.stop * PACK])
                 for g in range(groups):
-                    if g:
-                        weave(g, c, root[:, g * HALF : (g + 1) * HALF], h_bf)
-                    quantise(h_c[:, g, :], h_q[:, g, :], h_bf[:, g, :])
                     for acc, n0 in accs:
                         flux(acc, n0, g, h_c, h_q)
                 for done in (c - 2, c - 1):

@@ -25,13 +25,14 @@ PASS = P * PACK
 HALF = 512
 RUN = 8
 QUADS = 4
-SQUARES_ON_VECTOR = {(1, 0, 0), (1, 0, 1), (1, 1, 0)}
 CHUNK = 128
-SIGNED = 2
+SIGNED = 3
+SQUARES_ON_VECTOR = ((1, 0, 0), (1, 0, 1))
+FIRST_CASTS_ON_SCALAR = (1,)
+W3_PIECES = 4
 COPIES_ON_VECTOR = (2, 4)
 COPIES_BEHIND_ROOT = {5: (0,), 6: (1, 3)}
 TINY = 2.0**-80
-FIRST_CASTS_ON_SCALAR = (1, 2, 3)
 
 
 def tile_list_asteroid_band_fluxes_kernel(
@@ -41,46 +42,57 @@ def tile_list_asteroid_band_fluxes_kernel(
     halves = S // HALF
     groups = H // PASS
     kpasses = K // PASS
+    chunks = S // CHUNK
+    last = chunks - 1
+    wide = SIGNED * CHUNK
     with ExitStack() as ctx:
         keep = ctx.enter_context(tc.tile_pool(name="keep", bufs=1))
         ring = ctx.enter_context(tc.tile_pool(name="ring", bufs=2))
+        laid = ctx.enter_context(tc.tile_pool(name="laid", bufs=1))
         psum = ctx.enter_context(tc.psum_pool(name="psum", bufs=1))
-        bank_of = [psum.tile([P, HALF], F32, name="bank%d" % u) for u in range(8)]
+        banks = [psum.tile([P, HALF], F32, name="bank%d" % u) for u in range(8)]
 
         def held(shape, dtype, name):
             return keep.tile(shape, dtype, name=name, align_bytes=64)
 
+        def quantise(codes, scales, values):
+            nc.vector.quantize_mx(out=codes.bitcast(FP8X4), scales=scales, in_=values)
+
         idx = keep.tile([P, S // 16], U16, name="idx")
         idx2 = keep.tile([P, S // 16], U16, name="idx2")
+
+        def picks(offsets, first, count):
+            return offsets[:, first // 16 : (first + count) // 16]
+
         tab2_s = held([P, T], U8, "tab2_s")
         tab_s = held([P, T], U8, "tab_s")
         w1_rows = held([P, H], U8, "w1_rows")
+        v2_rows = held([P, S], U8, "v2_rows")
+        v_rows = held([P, S], U8, "v_rows")
         joined = held([P, S + H], U8, "joined")
         v2_s = held([P, S], U8, "v2_s")
         a_s = held([P, kpasses * (S + H)], U8, "a_s")
-        v2_rows = held([P, S], U8, "v2_rows")
-        v_rows = held([P, S], U8, "v_rows")
         tab2_w = held([P, T], U16, "tab2_w")
         tab_w = [held([P, T], I32, "tab_w%d" % a) for a in range(kpasses)]
         w1_w = held([P, kpasses * H], U16, "w1_w")
+        w1_wp = held([P, kpasses * H], U16, "w1_wp")
         w_raw = [held([P, PACK, PASS], F32, "w_raw%d" % g) for g in range(groups)]
         emis_raw = held([groups, PASS], F32, "emis_raw")
         emis_rows = held([P, PASS], F32, "emis_rows")
         ident = held([P, P], F32, "ident")
         inverse = held([P, groups * PACK], F32, "inverse")
         inverse2 = held([P, groups * PACK], F32, "inverse2")
+        one = held([P, 1], F32, "one")
+        warm = held([P, 1], F32, "warm")
 
         nc.vector.memset(tab2_s[0 : P - 16, :].bitcast(I32), 0)
         nc.vector.memset(v2_s[:].bitcast(I32), 0)
         nc.gpsimd.memset(tab_s[:].bitcast(I32), 0)
         nc.gpsimd.memset(w1_rows[:].bitcast(I32), 0)
         nc.vector.memset(a_s[:].bitcast(I32), 0)
-        one = held([P, 1], F32, "one")
-        warm = held([P, 1], F32, "warm")
         nc.gpsimd.memset(one[:], 1.0)
         nc.scalar.dma_start(emis_raw[:], emis.rearrange("(g c) -> g c", g=groups))
         nc.scalar.activation(warm[:], one[:], ACT.Abs_reciprocal_sqrt)
-
         nc.gpsimd.memset(emis_rows[:], 0.0)
         make_identity(nc, ident[:])
 
@@ -96,7 +108,6 @@ def tile_list_asteroid_band_fluxes_kernel(
             nc.sync.dma_start(v2_s[r:P:32, :].bitcast(I32), v2_rows[P - 16 + r : P : 4, :].bitcast(I32))
         nc.sync.dma_start(w_raw[1][:], w2_rows[:, :, PASS : 2 * PASS])
         nc.sync.dma_start(w1_rows[32:96:2, :].bitcast(I32), w1_scales.rearrange("a q c -> q a c").bitcast(I32))
-
         nc.sync.dma_start(
             w1_w[:].bitcast(I32).rearrange("p (a c) -> p a c", a=kpasses), w1_words.bitcast(I32).rearrange("a p c -> p a c")
         )
@@ -106,44 +117,26 @@ def tile_list_asteroid_band_fluxes_kernel(
 
         load_tab(0)
 
-
-        def picks(offsets, j):
-            return offsets[:, j * (HALF // 16) : (j + 1) * (HALF // 16)]
-
         v2_w = [held([P, HALF], U16, "v2_w%d" % j) for j in range(halves)]
-        v_w = [[held([P, HALF], U32, "v_w%d_%d" % (a, j)) for j in range(halves)] for a in range(kpasses)]
         for j in range(halves):
-            nc.vector.tensor_copy(v2_w[j][:], tab2_w[:].indirect(picks(idx2, j)))
+            nc.vector.tensor_copy(v2_w[j][:], tab2_w[:].indirect(picks(idx2, j * HALF, HALF)))
 
-        def quantise(codes, scales, values):
-            nc.vector.quantize_mx(out=codes.bitcast(FP8X4), scales=scales, in_=values)
-
-        staged = [held([P, PASS * PACK], BF16, "staged%d" % u) for u in range(2)]
         first_bf = [held([P, PASS], BF16, "first_bf%d" % t) for t in range(PACK)]
+        second_bf = held([P, PASS * PACK], BF16, "second_bf")
         w2_c = [held([P, PASS], U32, "w2_c%d" % g) for g in range(groups)]
         w2_q = [held([P, PASS], U8, "w2_q%d" % g) for g in range(groups)]
-        w3_c = [held([P, N], U32, "w3_c%d" % g) for g in range(groups)]
-        w3_q = [held([P, N], U8, "w3_q%d" % g) for g in range(groups)]
-
-        def round_first(t):
+        for t in range(PACK):
             copy = nc.scalar.copy if t in FIRST_CASTS_ON_SCALAR else nc.vector.tensor_copy
             copy(
                 first_bf[t][:].rearrange("p (b i j) -> p b j i", i=RUN, j=PACK),
                 w_raw[0][:].rearrange("p j (b t i) -> p t b j i", t=PACK, i=RUN)[:, t],
             )
+            if t > 0:
+                cols = slice((t - 1) * P, t * P)
+                quantise(w2_c[0][:, cols], w2_q[0][:, cols], first_bf[t - 1][:])
+        quantise(w2_c[0][:, PASS - P : PASS], w2_q[0][:, PASS - P : PASS], first_bf[PACK - 1][:])
 
-        def quantise_first(t):
-            cols = slice(t * P, (t + 1) * P)
-            quantise(w2_c[0][:, cols], w2_q[0][:, cols], first_bf[t][:])
-
-        for t in range(PACK):
-            round_first(t)
-        for t in range(PACK):
-            quantise_first(t)
-
-        damp = [[held([P, PACK, HALF], F32, "damp%d_%d" % (g, j)) for j in range(halves)] for g in range(groups)]
-
-        turned = bank_of[7]
+        turned = banks[7]
         nc.scalar.copy(
             emis_rows[0:groups, :].rearrange("g (t b i) -> g t b i", t=PACK, i=RUN),
             emis_raw[:].rearrange("g (b t i) -> g t b i", t=PACK, i=RUN),
@@ -156,12 +149,13 @@ def tile_list_asteroid_band_fluxes_kernel(
         )
         nc.vector.tensor_tensor(inverse2[:], inverse[:], inverse[:], MULT)
 
-        turns = [0, 0]
+        def unit(g, t):
+            return inverse2[:, g * PACK + t : g * PACK + t + 1]
 
-        def product_b(g, j, t, helped):
+        damp = [held([P, PACK, S], F32, "damp%d" % g) for g in range(groups)]
+
+        def product_b(g, j, t, bank):
             cols = slice(t * P, (t + 1) * P)
-            bank = bank_of[(6, 7, 2)[turns[1]]] if helped else bank_of[(2, 3, 4, 5)[t] if j else t % 2] if g else bank_of[turns[0] % 6]
-            turns[helped] = turns[helped] + 1
             nc.tensor.matmul_mx(
                 out=bank[:],
                 lhsT=w2_c[g][:, cols].bitcast(FP8X4),
@@ -171,32 +165,19 @@ def tile_list_asteroid_band_fluxes_kernel(
                 start=True,
                 stop=True,
             )
-            return bank
 
-        def take(g, j, t):
-            bank = product_b(g, j, t, 1)
-            twin = ring.tile([P, HALF], F32, name="twin", align_bytes=64, bufs=3)
-            nc.vector.tensor_copy(twin[:], bank[:])
-            return damp[g][j][:, t, :], bank, twin
+        turn = [0]
 
-        def square(into, bank, twin):
-            nc.vector.tensor_tensor(into, bank[:], twin[:], MULT)
+        def squares_on_scalar(g):
+            for j in range(halves):
+                for t in range(PACK):
+                    if (g, j, t) not in SQUARES_ON_VECTOR:
+                        bank = banks[turn[0] % 6]
+                        turn[0] = turn[0] + 1
+                        product_b(g, j, t, bank)
+                        nc.scalar.activation(damp[g][:, t, j * HALF : (j + 1) * HALF], bank[:], ACT.Square)
 
-        def squares_on_scalar(g, j):
-            for t in range(PACK):
-                if (g, j, t) not in SQUARES_ON_VECTOR:
-                    bank = product_b(g, j, t, 0)
-                    nc.scalar.activation(damp[g][j][:, t, :], bank[:], ACT.Square)
-
-        def damping(g, j):
-            first = SIGNED * CHUNK if j == 0 else 0
-            for t in range(PACK):
-                unit = inverse2[:, g * PACK + t : g * PACK + t + 1]
-                part = damp[g][j][:, t, first:HALF]
-                nc.scalar.activation(part, part, ACT.Abs_reciprocal_sqrt, bias=unit, scale=unit)
-
-        for j in range(halves):
-            squares_on_scalar(0, j)
+        squares_on_scalar(0)
 
         def deal(dst, src, words):
             nc.vector.tensor_copy(
@@ -219,44 +200,44 @@ def tile_list_asteroid_band_fluxes_kernel(
 
         for u in range(2):
             nc.vector.tensor_copy(
-                staged[1][:].rearrange("p (t b i j) -> p b t j i", t=PACK, i=RUN, j=PACK)[:, :, 2 * u : 2 * u + 2],
+                second_bf[:].rearrange("p (t b i j) -> p b t j i", t=PACK, i=RUN, j=PACK)[:, :, 2 * u : 2 * u + 2],
                 w_raw[1][:].rearrange("p j (b t i) -> p b t j i", t=PACK, i=RUN)[:, :, 2 * u : 2 * u + 2],
             )
         for u in range(2):
             cols = slice(2 * u * P, (2 * u + 2) * P)
-            quantise(w2_c[1][:, cols], w2_q[1][:, cols], staged[1][:, cols.start * PACK : cols.stop * PACK])
+            quantise(w2_c[1][:, cols], w2_q[1][:, cols], second_bf[:, cols.start * PACK : cols.stop * PACK])
         for g in range(groups):
             rows = w3[g * PASS : (g + 1) * PASS, :].rearrange("(b t i) n -> t b i n", t=PACK, i=RUN)
             for t in range(PACK):
                 nc.sync.dma_start(w_raw[g][:, t, :], rows[t])
 
-        def gather_words(a, j):
-            nc.vector.tensor_copy(v_w[a][j][:], tab_w[a][:].bitcast(U32).indirect(picks(idx, j)))
-
-        w1_wp = held([P, kpasses * H], U16, "w1_wp")
         deal(w1_wp[:].rearrange("p (u c) -> p u c", c=PASS), w1_w[:], 4)
-        taken = [take(*place) for place in sorted(SQUARES_ON_VECTOR)]
-        for j in range(halves):
-            squares_on_scalar(1, j)
-        gather_words(0, 0)
-        for held_bank in taken:
-            square(*held_bank)
+        for u, (g, j, t) in enumerate(SQUARES_ON_VECTOR):
+            bank = banks[6 + u % 2]
+            product_b(g, j, t, bank)
+            twin = ring.tile([P, HALF], F32, name="twin", align_bytes=64, bufs=2)
+            nc.vector.tensor_copy(twin[:], bank[:])
+            nc.vector.tensor_tensor(damp[g][:, t, j * HALF : (j + 1) * HALF], bank[:], twin[:], MULT)
+        squares_on_scalar(1)
         for g in range(groups):
-            for j in range(halves):
-                damping(g, j)
-        gather_words(0, 1)
-        gather_words(1, 0)
-        gather_words(1, 1)
+            for t in range(PACK):
+                part = damp[g][:, t, wide:S]
+                nc.scalar.activation(part, part, ACT.Abs_reciprocal_sqrt, bias=unit(g, t), scale=unit(g, t))
 
-        chunks = S // CHUNK
-        per_half = HALF // CHUNK
-        last = chunks - 1
+        spans = [((0, HALF), (HALF, HALF)), ((0, HALF // 2), (HALF // 2, HALF // 2), (HALF, HALF))]
+        words_of = {}
+        for a in range(kpasses):
+            for first, count in spans[a]:
+                picked = held([P, count], U32, "v_w%d_%d" % (a, first))
+                nc.vector.tensor_copy(picked[:], tab_w[a][:].bitcast(U32).indirect(picks(idx, first, count)))
+                for c in range(first // CHUNK, (first + count) // CHUNK):
+                    words_of[a, c] = picked[:, c * CHUNK - first : (c + 1) * CHUNK - first]
 
         def bank_a(g, c):
-            return bank_of[groups * c + g] if c < SIGNED else bank_of[4 + groups * (c % 2) + g]
+            pair = c if c <= SIGNED else 3 - c % 2
+            return banks[groups * pair + g]
 
         def pass_a(g, c, a):
-            j, first = c // per_half, (c % per_half) * CHUNK
             for t in range(PACK):
                 c0 = a * (S + H) + S + g * PASS + t * P
                 w0 = a * H + g * PASS + t * P
@@ -265,26 +246,84 @@ def tile_list_asteroid_band_fluxes_kernel(
                     out=bank_a(g, c)[:, t * CHUNK : (t + 1) * CHUNK],
                     lhsT=w1_wp[:, w0 : w0 + P].bitcast(FP4X4),
                     lhsT_scale=a_s[:, c0 : c0 + P],
-                    rhs=v_w[a][j][:, first : first + CHUNK].bitcast(FP8X4),
+                    rhs=words_of[a, c].bitcast(FP8X4),
                     rhs_scale=a_s[:, s0 : s0 + CHUNK],
                     start=(a == 0 and t == 0),
                     stop=(a == kpasses - 1 and t == PACK - 1),
                 )
 
-        def round_w3(g, stage):
-            nc.vector.tensor_copy(
-                stage[:].rearrange("p (c i j) -> p c j i", i=4, j=PACK),
-                w_raw[g][:].rearrange("p j (c i) -> p c j i", i=4),
-            )
+        free_order = [7, 6] + [(turn[0] + u) % 6 for u in range(6)]
+        for u in free_order:
+            pass_a(u % groups, u // groups, 0)
 
-        def weave(g, c, root, h_bf, cols=slice(0, CHUNK)):
-            first = (c % per_half) * CHUNK
-            nc.vector.tensor_tensor(
-                h_bf[:, g, cols.start * PACK : cols.stop * PACK].rearrange("p (c i t) -> p c t i", i=4, t=PACK),
-                root.rearrange("p (t c) -> p t c", t=PACK)[:, :, cols].rearrange("p t (c i) -> p c t i", i=4),
-                damp[g][c // per_half][:, :, first + cols.start : first + cols.stop].rearrange("p t (c i) -> p c t i", i=4),
+        roots = [laid.tile([P, PACK, wide], F32, name="roots%d" % g, offset=g * PACK * wide * 4) for g in range(groups)]
+        joint = held([P, PACK, groups, wide], F32, "joint")
+        flat_joint = joint[:].rearrange("p t g c -> p (t g c)")
+        spare = [flat_joint[:, PACK * groups * wide - 2 * HALF :], flat_joint[:, 0 : 2 * HALF]]
+        mags = [held([P, groups * HALF], F32, "mag%d" % u) for u in range(2)]
+
+        def magnitude(g, c, into):
+            nc.scalar.activation(into[:, g * HALF : (g + 1) * HALF], bank_a(g, c)[:], ACT.Abs)
+
+        def join(g, c):
+            cols = slice(c * CHUNK, (c + 1) * CHUNK)
+            nc.vector.scalar_tensor_tensor(
+                joint[:, :, g, cols],
+                damp[g][:, :, cols],
+                1.0,
+                bank_a(g, c)[:].rearrange("p (t c) -> p t c", t=PACK),
+                ADD,
                 MULT,
             )
+
+        def joint_roots(g, cols):
+            for t in range(PACK):
+                nc.scalar.activation(
+                    roots[g][:, t, cols], joint[:, t, g, cols], ACT.Abs_reciprocal_sqrt, bias=TINY, scale=unit(g, t)
+                )
+
+        for g, c in ((0, 0), (0, 1), (0, 3), (0, 2), (1, 3), (1, 0), (1, 1), (1, 2)):
+            pass_a(g, c, 1)
+        for g in range(groups):
+            magnitude(g, SIGNED, mags[0][:])
+        for g in range(groups):
+            for c in range(SIGNED):
+                join(g, c)
+            joint_roots(g, slice(0, wide - CHUNK))
+            joint_roots(g, slice(wide - CHUNK, wide))
+        for g in range(groups):
+            for a in range(kpasses):
+                pass_a(g, SIGNED + 1, a)
+            magnitude(g, SIGNED + 1, mags[1][:])
+
+        w3_bf = [held([P, N * PACK], BF16, "w3_bf%d" % g) for g in range(groups)]
+        w3_c = [held([P, N], U32, "w3_c%d" % g) for g in range(groups)]
+        w3_q = [
+            laid.tile([P, N], U8, name="w3_q%d" % g, align_bytes=64, offset=PACK * wide * 4 + g * N) for g in range(groups)
+        ]
+        piece = N // W3_PIECES
+        for g in range(groups):
+            for u in range(W3_PIECES):
+                nc.gpsimd.tensor_scalar(
+                    w3_bf[g][:, u * piece * PACK : (u + 1) * piece * PACK].rearrange("p (c j) -> p c j", j=PACK),
+                    w_raw[g][:, :, u * piece : (u + 1) * piece].rearrange("p j c -> p c j"),
+                    1.0,
+                    0.0,
+                    MULT,
+                    ADD,
+                )
+
+        def weave(g, c, root, h_bf, cols=slice(0, CHUNK)):
+            first = c * CHUNK
+            return (
+                h_bf[:, g, cols.start * PACK : cols.stop * PACK].rearrange("p (c i t) -> p c t i", i=4, t=PACK),
+                root.rearrange("p (t c) -> p t c", t=PACK)[:, :, cols].rearrange("p t (c i) -> p c t i", i=4),
+                (roots if c < SIGNED else damp)[g][:, :, first + cols.start : first + cols.stop].rearrange("p t (c i) -> p c t i", i=4),
+            )
+
+        def multiply(g, c, root, h_bf, cols=slice(0, CHUNK)):
+            into, left, right = weave(g, c, root, h_bf, cols)
+            nc.vector.tensor_tensor(into, right, left, MULT)
 
         def flux(acc, n0, g, h_c, h_q):
             tiles = acc.shape[1]
@@ -310,9 +349,13 @@ def tile_list_asteroid_band_fluxes_kernel(
             rows = out[n0 * P : (n0 + tiles) * P, c * CHUNK : (c + 1) * CHUNK]
             queue.dma_start(rows.rearrange("(u p) j -> p u j", p=P), res[:])
 
-        def pack(h_bf):
+        def packed_tiles():
             h_c = ring.tile([P, groups, CHUNK], U32, name="h_c", align_bytes=64, bufs=4)
             h_q = ring.tile([P, groups, CHUNK], U8, name="h_q", align_bytes=64, bufs=4)
+            return h_c, h_q
+
+        def pack(h_bf):
+            h_c, h_q = packed_tiles()
             quantise(
                 h_c[:].rearrange("p g c -> p (g c)"),
                 h_q[:].rearrange("p g c -> p (g c)"),
@@ -320,84 +363,46 @@ def tile_list_asteroid_band_fluxes_kernel(
             )
             return h_c, h_q
 
-        def staging(c):
-            return staged[c % 2][:].rearrange("p (u g c) -> p u g c", u=2, g=groups)[:, c // 2 % 2]
+        sums = {}
 
-        for g, c in ((0, 0), (1, 0), (1, 1), (0, 2), (1, 2), (0, 3), (1, 3), (0, 1)):
-            pass_a(g, c, 0)
-        for g, c in ((0, 2), (1, 2), (0, 0), (0, 1), (0, 3), (1, 0), (1, 3), (1, 1)):
-            pass_a(g, c, 1)
-        width = SIGNED * CHUNK
-        joint = held([P, PACK, groups, width], F32, "joint")
-        spare = joint[:].rearrange("p (u t) g c -> p u (t g c)", u=2)
-        mags = [held([P, groups * PACK * CHUNK], F32, "mag%d" % u) for u in range(2)]
-
-        def magnitude(g, c, into):
-            nc.scalar.activation(into[:, g * HALF : (g + 1) * HALF], bank_a(g, c)[:], ACT.Abs)
-
-        def magnitudes(c, into):
+        def open_sums(c, h_c, h_q):
+            sums[c] = sums_in(banks[c % 4], N // P)
             for g in range(groups):
-                for a in range(kpasses):
-                    pass_a(g, c, a)
-                magnitude(g, c, into)
+                flux(sums[c], 0, g, h_c, h_q)
 
-        for g in range(groups):
-            magnitude(g, SIGNED, mags[0][:])
-        for g in range(groups):
-            magnitude(g, SIGNED + 1, mags[1][:])
-            for c in range(SIGNED):
-                cols = slice(c * CHUNK, (c + 1) * CHUNK)
-                nc.vector.scalar_tensor_tensor(
-                    joint[:, :, g, cols],
-                    damp[g][0][:, :, cols],
-                    1.0,
-                    bank_a(g, c)[:].rearrange("p (t c) -> p t c", t=PACK),
-                    ADD,
-                    MULT,
-                )
-            for t in range(PACK):
-                unit = inverse2[:, g * PACK + t : g * PACK + t + 1]
-                nc.scalar.activation(
-                    damp[g][0][:, t, 0:width], joint[:, t, g, :], ACT.Abs_reciprocal_sqrt, bias=TINY, scale=unit
-                )
-        round_w3(0, staged[0])
         signed = [held([P, groups, PACK * CHUNK], BF16, "signed%d" % c) for c in range(SIGNED)]
         mirror = [held([P, groups * PACK * CHUNK], BF16, "mirror%d" % c) for c in range(SIGNED)]
         for g in range(groups):
             for c in range(SIGNED):
-                weave(g, c, bank_a(g, c)[:], signed[c])
+                multiply(g, c, bank_a(g, c)[:], signed[c])
+        flats = [signed[c][:].rearrange("p g c -> p (g c)") for c in range(SIGNED)]
         for c in range(SIGNED):
-            flat = signed[c][:].rearrange("p g c -> p (g c)")
-            nc.vector.tensor_scalar(mirror[c][:], flat, -1.0, None, MULT)
-        for c in range(SIGNED):
-            flat = signed[c][:].rearrange("p g c -> p (g c)")
-            nc.vector.tensor_tensor(flat, flat, mirror[c][:], MAX)
-        round_w3(1, staged[1])
-        packed = [pack(signed[c][:]) for c in range(SIGNED)]
-        for g in range(groups):
-            quantise(w3_c[g][:], w3_q[g][:], staged[g][:])
-        sums = {}
-
-        def open_sums(c, h_c, h_q):
-            sums[c] = sums_in(bank_of[c % 4], N // P)
-            for g in range(groups):
-                flux(sums[c], 0, g, h_c, h_q)
-
-        for c in range(SIGNED):
-            open_sums(c, *packed[c])
+            nc.vector.tensor_scalar(mirror[c][:], flats[c], -1.0, None, MULT)
+        nc.vector.tensor_tensor(flats[0], flats[0], mirror[0][:], MAX)
+        quantise(w3_c[0][:], w3_q[0][:], w3_bf[0][:])
+        packed = [pack(signed[0][:])]
+        quantise(w3_c[1][:], w3_q[1][:], w3_bf[1][:])
+        open_sums(0, *packed[0])
+        for c in range(1, SIGNED):
+            nc.vector.tensor_tensor(flats[c], flats[c], mirror[c][:], MAX)
+        for c in range(1, SIGNED):
+            open_sums(c, *pack(signed[c][:]))
 
         def pieces(g, c):
             cuts = 2 if (g, c) == (groups - 1, last) else 1
             return [slice(u * CHUNK // cuts, (u + 1) * CHUNK // cuts) for u in range(cuts)]
 
         def roots_of(c):
-            u = c % 2
+            u = (c - SIGNED) % 2
             if c < SIGNED + 2:
-                root = spare[:, 1 - u, :]
+                root = spare[u]
                 nc.scalar.activation(root, mags[u][:], ACT.Sqrt)
             else:
-                root = mags[u][:] if c < SIGNED + 4 else spare[:, 1 - u, :]
-                magnitudes(c, root)
+                root = mags[u][:] if c < SIGNED + 4 else spare[u]
+                for g in range(groups):
+                    for a in range(kpasses):
+                        pass_a(g, c, a)
+                    magnitude(g, c, root)
                 for g in range(groups):
                     for cols in pieces(g, c):
                         part = root[:, g * HALF : (g + 1) * HALF].rearrange("p (t c) -> p t c", t=PACK)[:, :, cols]
@@ -406,29 +411,29 @@ def tile_list_asteroid_band_fluxes_kernel(
                 store(nc.scalar.copy, sums[done], 0, done)
             return root
 
+        staged = [held([P, groups, PACK * CHUNK], BF16, "staged%d" % u) for u in range(3)]
         ahead = roots_of(SIGNED)
         for c in range(SIGNED, chunks):
             root = ahead
             if c < last:
                 ahead = roots_of(c + 1)
-            h_bf = staging(c)
-            weave(0, c, root[:, 0:HALF], h_bf)
+            h_bf = staged[c % 3][:]
+            multiply(0, c, root[:, 0:HALF], h_bf)
             if SIGNED < c < last:
-                open_sums(c - 1, *pack(staging(c - 1)))
+                open_sums(c - 1, *pack(staged[(c - 1) % 3][:]))
             if c < last:
-                weave(1, c, root[:, HALF : 2 * HALF], h_bf)
+                multiply(1, c, root[:, HALF : 2 * HALF], h_bf)
                 if c - 2 in COPIES_ON_VECTOR:
                     store(nc.vector.tensor_copy, sums[c - 2], 0, c - 2)
                 if c == last - 1:
                     open_sums(c, *pack(h_bf))
             else:
-                h_c = ring.tile([P, groups, CHUNK], U32, name="h_c", align_bytes=64, bufs=4)
-                h_q = ring.tile([P, groups, CHUNK], U8, name="h_q", align_bytes=64, bufs=4)
-                accs = [(sums_in(bank_of[4], 2), 0), (sums_in(bank_of[5], 2), 2)]
+                h_c, h_q = packed_tiles()
+                accs = [(sums_in(banks[6], 2), 0), (sums_in(banks[7], 2), 2)]
                 left, right = pieces(1, c)
-                weave(1, c, root[:, HALF : 2 * HALF], h_bf, left)
+                multiply(1, c, root[:, HALF : 2 * HALF], h_bf, left)
                 quantise(h_c[:, 0, :], h_q[:, 0, :], h_bf[:, 0, :])
-                weave(1, c, root[:, HALF : 2 * HALF], h_bf, right)
+                multiply(1, c, root[:, HALF : 2 * HALF], h_bf, right)
                 for cols in (left, right):
                     quantise(h_c[:, 1, cols], h_q[:, 1, cols], h_bf[:, 1, cols.start * PACK : cols.stop * PACK])
                 for g in range(groups):

@@ -29,9 +29,9 @@ CHUNK = 128
 SIGNED = 3
 SQUARES_ON_VECTOR = ((1, 0, 0), (1, 0, 1))
 FIRST_CASTS_ON_SCALAR = (1,)
-W3_PIECES = 4
-COPIES_ON_VECTOR = (2, 4)
-COPIES_BEHIND_ROOT = {5: (0,), 6: (1, 3)}
+COPIES_ON_VECTOR = ()
+COPIES_BEHIND_ROOT = {6: (0, 1), 7: (3,)}
+COPIES_BEHIND_MAGNITUDES = {7: (2,)}
 TINY = 2.0**-80
 
 
@@ -64,14 +64,14 @@ def tile_list_asteroid_band_fluxes_kernel(
         def picks(offsets, first, count):
             return offsets[:, first // 16 : (first + count) // 16]
 
-        tab2_s = held([P, T], U8, "tab2_s")
-        tab_s = held([P, T], U8, "tab_s")
+        tab2_s = laid.tile([P, T], U8, name="tab2_s", align_bytes=64, offset=groups * PACK * wide * 4)
+        tab_s = laid.tile([P, T], U8, name="tab_s", align_bytes=64, offset=groups * PACK * wide * 4 + T)
         w1_rows = held([P, H], U8, "w1_rows")
         v2_rows = held([P, S], U8, "v2_rows")
         v_rows = held([P, S], U8, "v_rows")
         joined = held([P, S + H], U8, "joined")
-        v2_s = held([P, S], U8, "v2_s")
-        a_s = held([P, kpasses * (S + H)], U8, "a_s")
+        v2_s = laid.tile([P, S], U8, name="v2_s", align_bytes=64, offset=groups * PACK * wide * 4)
+        a_s = laid.tile([P, kpasses * (S + H)], U8, name="a_s", align_bytes=64, offset=groups * PACK * wide * 4 + T)
         tab2_w = held([P, T], U16, "tab2_w")
         tab_w = [held([P, T], I32, "tab_w%d" % a) for a in range(kpasses)]
         w1_w = held([P, kpasses * H], U16, "w1_w")
@@ -85,11 +85,9 @@ def tile_list_asteroid_band_fluxes_kernel(
         one = held([P, 1], F32, "one")
         warm = held([P, 1], F32, "warm")
 
+        nc.vector.memset(w1_rows[:].bitcast(I32), 0)
+        nc.vector.memset(tab_s[:].bitcast(I32), 0)
         nc.vector.memset(tab2_s[0 : P - 16, :].bitcast(I32), 0)
-        nc.vector.memset(v2_s[:].bitcast(I32), 0)
-        nc.gpsimd.memset(tab_s[:].bitcast(I32), 0)
-        nc.gpsimd.memset(w1_rows[:].bitcast(I32), 0)
-        nc.vector.memset(a_s[:].bitcast(I32), 0)
         nc.gpsimd.memset(one[:], 1.0)
         nc.scalar.dma_start(emis_raw[:], emis.rearrange("(g c) -> g c", g=groups))
         nc.scalar.activation(warm[:], one[:], ACT.Abs_reciprocal_sqrt)
@@ -99,18 +97,18 @@ def tile_list_asteroid_band_fluxes_kernel(
         w2_rows = w2.rearrange("(p j) r -> p j r", j=PACK)
         nc.sync.dma_start(idx2[:], offs2)
         nc.sync.dma_start(tab2_s[P - 16 : P, :].bitcast(I32), tab2_scales[0].bitcast(I32))
-        nc.sync.dma_start(tab2_w[:].bitcast(I32), tab2_words[0].bitcast(I32))
-        nc.sync.dma_start(w_raw[0][:], w2_rows[:, :, 0:PASS])
         nc.sync.dma_start(idx[:], offs)
+        nc.sync.dma_start(tab2_w[:].bitcast(I32), tab2_words[0].bitcast(I32))
+        nc.sync.dma_start(w1_rows[32:96:2, :].bitcast(I32), w1_scales.rearrange("a q c -> q a c").bitcast(I32))
+        nc.sync.dma_start(w_raw[0][:], w2_rows[:, :, 0:PASS])
         nc.sync.dma_start(tab_s[32:96:2, :].bitcast(I32), tab_scales.rearrange("a q t -> q a t").bitcast(I32))
+        nc.sync.dma_start(
+            w1_w[:].bitcast(I32).rearrange("p (a c) -> p a c", a=kpasses), w1_words.bitcast(I32).rearrange("a p c -> p a c")
+        )
         nc.vector.tensor_copy(v2_rows[:], tab2_s[:].indirect(idx2[:]))
         for r in range(QUADS):
             nc.sync.dma_start(v2_s[r:P:32, :].bitcast(I32), v2_rows[P - 16 + r : P : 4, :].bitcast(I32))
         nc.sync.dma_start(w_raw[1][:], w2_rows[:, :, PASS : 2 * PASS])
-        nc.sync.dma_start(w1_rows[32:96:2, :].bitcast(I32), w1_scales.rearrange("a q c -> q a c").bitcast(I32))
-        nc.sync.dma_start(
-            w1_w[:].bitcast(I32).rearrange("p (a c) -> p a c", a=kpasses), w1_words.bitcast(I32).rearrange("a p c -> p a c")
-        )
 
         def load_tab(a):
             nc.sync.dma_start(tab_w[a][:], tab_words[a].rearrange("p t i -> p (t i)").bitcast(I32))
@@ -289,8 +287,7 @@ def tile_list_asteroid_band_fluxes_kernel(
         for g in range(groups):
             for c in range(SIGNED):
                 join(g, c)
-            joint_roots(g, slice(0, wide - CHUNK))
-            joint_roots(g, slice(wide - CHUNK, wide))
+            joint_roots(g, slice(0, wide))
         for g in range(groups):
             for a in range(kpasses):
                 pass_a(g, SIGNED + 1, a)
@@ -301,17 +298,14 @@ def tile_list_asteroid_band_fluxes_kernel(
         w3_q = [
             laid.tile([P, N], U8, name="w3_q%d" % g, align_bytes=64, offset=PACK * wide * 4 + g * N) for g in range(groups)
         ]
-        piece = N // W3_PIECES
-        for g in range(groups):
-            for u in range(W3_PIECES):
-                nc.gpsimd.tensor_scalar(
-                    w3_bf[g][:, u * piece * PACK : (u + 1) * piece * PACK].rearrange("p (c j) -> p c j", j=PACK),
-                    w_raw[g][:, :, u * piece : (u + 1) * piece].rearrange("p j c -> p c j"),
-                    1.0,
-                    0.0,
-                    MULT,
-                    ADD,
-                )
+
+        def round_w3(g):
+            nc.vector.tensor_copy(
+                w3_bf[g][:].rearrange("p (c i j) -> p c j i", i=4, j=PACK),
+                w_raw[g][:].rearrange("p j (c i) -> p c j i", i=4),
+            )
+
+        round_w3(0)
 
         def weave(g, c, root, h_bf, cols=slice(0, CHUNK)):
             first = c * CHUNK
@@ -344,7 +338,7 @@ def tile_list_asteroid_band_fluxes_kernel(
 
         def store(copy, acc, n0, c, queue=nc.sync):
             tiles = acc.shape[1]
-            res = ring.tile([P, tiles, CHUNK], F32, name="res", align_bytes=64, bufs=4)
+            res = ring.tile([P, tiles, CHUNK], F32, name="res", align_bytes=64, bufs=9)
             copy(res[:], acc)
             rows = out[n0 * P : (n0 + tiles) * P, c * CHUNK : (c + 1) * CHUNK]
             queue.dma_start(rows.rearrange("(u p) j -> p u j", p=P), res[:])
@@ -380,6 +374,7 @@ def tile_list_asteroid_band_fluxes_kernel(
             nc.vector.tensor_scalar(mirror[c][:], flats[c], -1.0, None, MULT)
         nc.vector.tensor_tensor(flats[0], flats[0], mirror[0][:], MAX)
         quantise(w3_c[0][:], w3_q[0][:], w3_bf[0][:])
+        round_w3(1)
         packed = [pack(signed[0][:])]
         quantise(w3_c[1][:], w3_q[1][:], w3_bf[1][:])
         open_sums(0, *packed[0])
@@ -403,6 +398,8 @@ def tile_list_asteroid_band_fluxes_kernel(
                     for a in range(kpasses):
                         pass_a(g, c, a)
                     magnitude(g, c, root)
+                for done in COPIES_BEHIND_MAGNITUDES.get(c, ()):
+                    store(nc.scalar.copy, sums[done], 0, done)
                 for g in range(groups):
                     for cols in pieces(g, c):
                         part = root[:, g * HALF : (g + 1) * HALF].rearrange("p (t c) -> p t c", t=PACK)[:, :, cols]
@@ -439,7 +436,7 @@ def tile_list_asteroid_band_fluxes_kernel(
                 for g in range(groups):
                     for acc, n0 in accs:
                         flux(acc, n0, g, h_c, h_q)
-                for done in (c - 2, c - 1):
+                for done in (c - 3, c - 2, c - 1):
                     store(nc.scalar.copy, sums[done], 0, done)
                 store(nc.vector.tensor_copy, *accs[0], c)
                 store(nc.scalar.copy, *accs[1], c, nc.scalar)

@@ -30,8 +30,8 @@ SIGNED = 3
 SQUARES_ON_VECTOR = ((1, 0, 0), (1, 0, 1))
 FIRST_CASTS_ON_SCALAR = (1,)
 COPIES_ON_VECTOR = ()
-COPIES_BEHIND_ROOT = {6: (0, 1), 7: (3,)}
-COPIES_BEHIND_MAGNITUDES = {7: (2,)}
+COPIES_BEHIND_ROOT = {6: (1, 2)}
+COPIES_BEHIND_MAGNITUDES = {6: (0,), 7: (3,)}
 TINY = 2.0**-80
 
 
@@ -232,7 +232,7 @@ def tile_list_asteroid_band_fluxes_kernel(
                     words_of[a, c] = picked[:, c * CHUNK - first : (c + 1) * CHUNK - first]
 
         def bank_a(g, c):
-            pair = c if c <= SIGNED else 3 - c % 2
+            pair = c if c <= SIGNED else 2 if c == last - 1 else 3
             return banks[groups * pair + g]
 
         def pass_a(g, c, a):
@@ -295,9 +295,7 @@ def tile_list_asteroid_band_fluxes_kernel(
 
         w3_bf = [held([P, N * PACK], BF16, "w3_bf%d" % g) for g in range(groups)]
         w3_c = [held([P, N], U32, "w3_c%d" % g) for g in range(groups)]
-        w3_q = [
-            laid.tile([P, N], U8, name="w3_q%d" % g, align_bytes=64, offset=PACK * wide * 4 + g * N) for g in range(groups)
-        ]
+        w3_q = [held([P, N], U8, "w3_q%d" % g) for g in range(groups)]
 
         def round_w3(g):
             nc.vector.tensor_copy(
@@ -366,22 +364,33 @@ def tile_list_asteroid_band_fluxes_kernel(
 
         signed = [held([P, groups, PACK * CHUNK], BF16, "signed%d" % c) for c in range(SIGNED)]
         mirror = [held([P, groups * PACK * CHUNK], BF16, "mirror%d" % c) for c in range(SIGNED)]
-        for g in range(groups):
-            for c in range(SIGNED):
-                multiply(g, c, bank_a(g, c)[:], signed[c])
         flats = [signed[c][:].rearrange("p g c -> p (g c)") for c in range(SIGNED)]
-        for c in range(SIGNED):
+
+        def signed_product(g, c):
+            multiply(g, c, bank_a(g, c)[:], signed[c])
+
+        def negate(c):
             nc.vector.tensor_scalar(mirror[c][:], flats[c], -1.0, None, MULT)
-        nc.vector.tensor_tensor(flats[0], flats[0], mirror[0][:], MAX)
-        quantise(w3_c[0][:], w3_q[0][:], w3_bf[0][:])
-        round_w3(1)
-        packed = [pack(signed[0][:])]
-        quantise(w3_c[1][:], w3_q[1][:], w3_bf[1][:])
-        open_sums(0, *packed[0])
-        for c in range(1, SIGNED):
+
+        def unsign(c):
             nc.vector.tensor_tensor(flats[c], flats[c], mirror[c][:], MAX)
-        for c in range(1, SIGNED):
-            open_sums(c, *pack(signed[c][:]))
+
+        for g, c in ((0, 0), (0, 1), (1, 0)):
+            signed_product(g, c)
+        round_w3(1)
+        negate(0)
+        quantise(w3_c[0][:], w3_q[0][:], w3_bf[0][:])
+        unsign(0)
+        quantise(w3_c[1][:], w3_q[1][:], w3_bf[1][:])
+        open_sums(0, *pack(signed[0][:]))
+        for g, c in ((1, 1), (0, 2)):
+            signed_product(g, c)
+        negate(1)
+        signed_product(1, 2)
+        unsign(1)
+        negate(2)
+        open_sums(1, *pack(signed[1][:]))
+        unsign(2)
 
         def pieces(g, c):
             cuts = 2 if (g, c) == (groups - 1, last) else 1
@@ -404,6 +413,8 @@ def tile_list_asteroid_band_fluxes_kernel(
                     for cols in pieces(g, c):
                         part = root[:, g * HALF : (g + 1) * HALF].rearrange("p (t c) -> p t c", t=PACK)[:, :, cols]
                         nc.scalar.activation(part, part, ACT.Sqrt)
+                        if (g, c, cols.start) == (groups - 1, last, 0):
+                            store(nc.scalar.copy, sums[c - 3], 0, c - 3)
             for done in COPIES_BEHIND_ROOT.get(c, ()):
                 store(nc.scalar.copy, sums[done], 0, done)
             return root
@@ -416,8 +427,8 @@ def tile_list_asteroid_band_fluxes_kernel(
                 ahead = roots_of(c + 1)
             h_bf = staged[c % 3][:]
             multiply(0, c, root[:, 0:HALF], h_bf)
-            if SIGNED < c < last:
-                open_sums(c - 1, *pack(staged[(c - 1) % 3][:]))
+            if c < last:
+                open_sums(c - 1, *pack(staged[(c - 1) % 3][:] if c > SIGNED else signed[c - 1][:]))
             if c < last:
                 multiply(1, c, root[:, HALF : 2 * HALF], h_bf)
                 if c - 2 in COPIES_ON_VECTOR:
@@ -426,7 +437,7 @@ def tile_list_asteroid_band_fluxes_kernel(
                     open_sums(c, *pack(h_bf))
             else:
                 h_c, h_q = packed_tiles()
-                accs = [(sums_in(banks[6], 2), 0), (sums_in(banks[7], 2), 2)]
+                accs = [(sums_in(banks[4], 2), 0), (sums_in(banks[5], 2), 2)]
                 left, right = pieces(1, c)
                 multiply(1, c, root[:, HALF : 2 * HALF], h_bf, left)
                 quantise(h_c[:, 0, :], h_q[:, 0, :], h_bf[:, 0, :])
@@ -436,7 +447,7 @@ def tile_list_asteroid_band_fluxes_kernel(
                 for g in range(groups):
                     for acc, n0 in accs:
                         flux(acc, n0, g, h_c, h_q)
-                for done in (c - 3, c - 2, c - 1):
+                for done in (c - 2, c - 1):
                     store(nc.scalar.copy, sums[done], 0, done)
                 store(nc.vector.tensor_copy, *accs[0], c)
                 store(nc.scalar.copy, *accs[1], c, nc.scalar)

@@ -26,12 +26,12 @@ HALF = 512
 RUN = 8
 QUADS = 4
 CHUNK = 128
-SIGNED = 3
-SQUARES_ON_VECTOR = ((1, 0, 0), (1, 0, 1))
+SIGNED = 2
+EARLY = 4
+SQUARES_ON_VECTOR = ((1, 0, 0), (1, 0, 1), (1, 1, 0))
 FIRST_CASTS_ON_SCALAR = (1,)
-COPIES_ON_VECTOR = ()
-COPIES_BEHIND_ROOT = {6: (1, 2)}
-COPIES_BEHIND_MAGNITUDES = {6: (0,), 7: (3,)}
+COPIES_ON_VECTOR = (2, 4)
+COPIES_BEHIND_ROOT = {5: (0,), 6: (1, 3)}
 TINY = 2.0**-80
 
 
@@ -86,12 +86,13 @@ def tile_list_asteroid_band_fluxes_kernel(
         warm = held([P, 1], F32, "warm")
 
         nc.vector.memset(w1_rows[:].bitcast(I32), 0)
-        nc.vector.memset(tab_s[:].bitcast(I32), 0)
         nc.vector.memset(tab2_s[0 : P - 16, :].bitcast(I32), 0)
+        nc.vector.memset(tab_s[:, 0 : T // 2].bitcast(I32), 0)
         nc.gpsimd.memset(one[:], 1.0)
+        nc.gpsimd.memset(tab_s[:, T // 2 : T].bitcast(I32), 0)
         nc.scalar.dma_start(emis_raw[:], emis.rearrange("(g c) -> g c", g=groups))
         nc.scalar.activation(warm[:], one[:], ACT.Abs_reciprocal_sqrt)
-        nc.gpsimd.memset(emis_rows[:], 0.0)
+        nc.scalar.activation(emis_rows[:], one[:].to_broadcast([P, PASS]), ACT.Copy, scale=0.0)
         make_identity(nc, ident[:])
 
         w2_rows = w2.rearrange("(p j) r -> p j r", j=PACK)
@@ -102,13 +103,16 @@ def tile_list_asteroid_band_fluxes_kernel(
         nc.sync.dma_start(w1_rows[32:96:2, :].bitcast(I32), w1_scales.rearrange("a q c -> q a c").bitcast(I32))
         nc.sync.dma_start(w_raw[0][:], w2_rows[:, :, 0:PASS])
         nc.sync.dma_start(tab_s[32:96:2, :].bitcast(I32), tab_scales.rearrange("a q t -> q a t").bitcast(I32))
-        nc.sync.dma_start(
-            w1_w[:].bitcast(I32).rearrange("p (a c) -> p a c", a=kpasses), w1_words.bitcast(I32).rearrange("a p c -> p a c")
-        )
+
+        def load_w1(a):
+            nc.sync.dma_start(w1_w[:, a * H : (a + 1) * H].bitcast(I32), w1_words[a].bitcast(I32))
+
+        load_w1(0)
         nc.vector.tensor_copy(v2_rows[:], tab2_s[:].indirect(idx2[:]))
         for r in range(QUADS):
             nc.sync.dma_start(v2_s[r:P:32, :].bitcast(I32), v2_rows[P - 16 + r : P : 4, :].bitcast(I32))
         nc.sync.dma_start(w_raw[1][:], w2_rows[:, :, PASS : 2 * PASS])
+        load_w1(1)
 
         def load_tab(a):
             nc.sync.dma_start(tab_w[a][:], tab_words[a].rearrange("p t i -> p (t i)").bitcast(I32))
@@ -170,7 +174,7 @@ def tile_list_asteroid_band_fluxes_kernel(
             for j in range(halves):
                 for t in range(PACK):
                     if (g, j, t) not in SQUARES_ON_VECTOR:
-                        bank = banks[turn[0] % 6]
+                        bank = banks[turn[0] % 5]
                         turn[0] = turn[0] + 1
                         product_b(g, j, t, bank)
                         nc.scalar.activation(damp[g][:, t, j * HALF : (j + 1) * HALF], bank[:], ACT.Square)
@@ -210,29 +214,37 @@ def tile_list_asteroid_band_fluxes_kernel(
                 nc.sync.dma_start(w_raw[g][:, t, :], rows[t])
 
         deal(w1_wp[:].rearrange("p (u c) -> p u c", c=PASS), w1_w[:], 4)
+        spans = [((0, HALF), (HALF, HALF)), ((HALF // 2, HALF // 2), (0, HALF // 2), (HALF, HALF))]
+        words_of = {}
+
+        def gather_words(a, first, count):
+            picked = held([P, count], U32, "v_w%d_%d" % (a, first))
+            nc.vector.tensor_copy(picked[:], tab_w[a][:].bitcast(U32).indirect(picks(idx, first, count)))
+            for c in range(first // CHUNK, (first + count) // CHUNK):
+                words_of[a, c] = picked[:, c * CHUNK - first : (c + 1) * CHUNK - first]
+
+        twins = []
         for u, (g, j, t) in enumerate(SQUARES_ON_VECTOR):
-            bank = banks[6 + u % 2]
-            product_b(g, j, t, bank)
-            twin = ring.tile([P, HALF], F32, name="twin", align_bytes=64, bufs=2)
-            nc.vector.tensor_copy(twin[:], bank[:])
-            nc.vector.tensor_tensor(damp[g][:, t, j * HALF : (j + 1) * HALF], bank[:], twin[:], MULT)
+            product_b(g, j, t, banks[5 + u])
+            twins.append(held([P, HALF], F32, "twin%d" % u))
+            nc.vector.tensor_copy(twins[u][:], banks[5 + u][:])
         squares_on_scalar(1)
-        for g in range(groups):
-            for t in range(PACK):
+        gather_words(0, *spans[0][0])
+        for u, (g, j, t) in enumerate(SQUARES_ON_VECTOR):
+            nc.vector.tensor_tensor(damp[g][:, t, j * HALF : (j + 1) * HALF], banks[5 + u][:], twins[u][:], MULT)
+
+        def damping(places):
+            for g, t in places:
                 part = damp[g][:, t, wide:S]
                 nc.scalar.activation(part, part, ACT.Abs_reciprocal_sqrt, bias=unit(g, t), scale=unit(g, t))
 
-        spans = [((0, HALF), (HALF, HALF)), ((0, HALF // 2), (HALF // 2, HALF // 2), (HALF, HALF))]
-        words_of = {}
-        for a in range(kpasses):
-            for first, count in spans[a]:
-                picked = held([P, count], U32, "v_w%d_%d" % (a, first))
-                nc.vector.tensor_copy(picked[:], tab_w[a][:].bitcast(U32).indirect(picks(idx, first, count)))
-                for c in range(first // CHUNK, (first + count) // CHUNK):
-                    words_of[a, c] = picked[:, c * CHUNK - first : (c + 1) * CHUNK - first]
+        damping([(g, t) for g in range(groups) for t in range(PACK)])
+        gather_words(0, *spans[0][1])
+        for span in spans[1]:
+            gather_words(1, *span)
 
         def bank_a(g, c):
-            pair = c if c <= SIGNED else 2 if c == last - 1 else 3
+            pair = c if c < EARLY else 2 + c % 2
             return banks[groups * pair + g]
 
         def pass_a(g, c, a):
@@ -250,7 +262,7 @@ def tile_list_asteroid_band_fluxes_kernel(
                     stop=(a == kpasses - 1 and t == PACK - 1),
                 )
 
-        free_order = [7, 6] + [(turn[0] + u) % 6 for u in range(6)]
+        free_order = [(turn[0] + u) % 5 for u in range(5)] + [5, 6, 7]
         for u in free_order:
             pass_a(u % groups, u // groups, 0)
 
@@ -280,18 +292,16 @@ def tile_list_asteroid_band_fluxes_kernel(
                     roots[g][:, t, cols], joint[:, t, g, cols], ACT.Abs_reciprocal_sqrt, bias=TINY, scale=unit(g, t)
                 )
 
-        for g, c in ((0, 0), (0, 1), (0, 3), (0, 2), (1, 3), (1, 0), (1, 1), (1, 2)):
+        for g, c in ((0, 2), (1, 2), (0, 0), (0, 1), (0, 3), (1, 0), (1, 1), (1, 3)):
             pass_a(g, c, 1)
         for g in range(groups):
             magnitude(g, SIGNED, mags[0][:])
+        magnitude(0, SIGNED + 1, mags[1][:])
         for g in range(groups):
             for c in range(SIGNED):
                 join(g, c)
             joint_roots(g, slice(0, wide))
-        for g in range(groups):
-            for a in range(kpasses):
-                pass_a(g, SIGNED + 1, a)
-            magnitude(g, SIGNED + 1, mags[1][:])
+        magnitude(1, SIGNED + 1, mags[1][:])
 
         w3_bf = [held([P, N * PACK], BF16, "w3_bf%d" % g) for g in range(groups)]
         w3_c = [held([P, N], U32, "w3_c%d" % g) for g in range(groups)]
@@ -362,35 +372,22 @@ def tile_list_asteroid_band_fluxes_kernel(
             for g in range(groups):
                 flux(sums[c], 0, g, h_c, h_q)
 
-        signed = [held([P, groups, PACK * CHUNK], BF16, "signed%d" % c) for c in range(SIGNED)]
-        mirror = [held([P, groups * PACK * CHUNK], BF16, "mirror%d" % c) for c in range(SIGNED)]
-        flats = [signed[c][:].rearrange("p g c -> p (g c)") for c in range(SIGNED)]
-
-        def signed_product(g, c):
-            multiply(g, c, bank_a(g, c)[:], signed[c])
-
-        def negate(c):
-            nc.vector.tensor_scalar(mirror[c][:], flats[c], -1.0, None, MULT)
-
-        def unsign(c):
-            nc.vector.tensor_tensor(flats[c], flats[c], mirror[c][:], MAX)
-
-        for g, c in ((0, 0), (0, 1), (1, 0)):
-            signed_product(g, c)
-        round_w3(1)
-        negate(0)
+        signed = held([P, SIGNED, groups, PACK * CHUNK], BF16, "signed")
+        mirror = held([P, SIGNED * groups * PACK * CHUNK], BF16, "mirror")
+        flat = signed[:].rearrange("p c g x -> p (c g x)")
+        signed_c = held([P, SIGNED, groups, CHUNK], U32, "signed_c")
+        signed_q = held([P, SIGNED, groups, CHUNK], U8, "signed_q")
+        for g in range(groups):
+            for c in range(SIGNED):
+                multiply(g, c, bank_a(g, c)[:], signed[:, c])
         quantise(w3_c[0][:], w3_q[0][:], w3_bf[0][:])
-        unsign(0)
+        nc.vector.tensor_scalar(mirror[:], flat, -1.0, None, MULT)
+        round_w3(1)
+        nc.vector.tensor_tensor(flat, flat, mirror[:], MAX)
         quantise(w3_c[1][:], w3_q[1][:], w3_bf[1][:])
-        open_sums(0, *pack(signed[0][:]))
-        for g, c in ((1, 1), (0, 2)):
-            signed_product(g, c)
-        negate(1)
-        signed_product(1, 2)
-        unsign(1)
-        negate(2)
-        open_sums(1, *pack(signed[1][:]))
-        unsign(2)
+        quantise(signed_c[:].rearrange("p c g x -> p (c g x)"), signed_q[:].rearrange("p c g x -> p (c g x)"), flat)
+        for c in range(SIGNED):
+            open_sums(c, signed_c[:, c], signed_q[:, c])
 
         def pieces(g, c):
             cuts = 2 if (g, c) == (groups - 1, last) else 1
@@ -407,14 +404,10 @@ def tile_list_asteroid_band_fluxes_kernel(
                     for a in range(kpasses):
                         pass_a(g, c, a)
                     magnitude(g, c, root)
-                for done in COPIES_BEHIND_MAGNITUDES.get(c, ()):
-                    store(nc.scalar.copy, sums[done], 0, done)
                 for g in range(groups):
                     for cols in pieces(g, c):
                         part = root[:, g * HALF : (g + 1) * HALF].rearrange("p (t c) -> p t c", t=PACK)[:, :, cols]
                         nc.scalar.activation(part, part, ACT.Sqrt)
-                        if (g, c, cols.start) == (groups - 1, last, 0):
-                            store(nc.scalar.copy, sums[c - 3], 0, c - 3)
             for done in COPIES_BEHIND_ROOT.get(c, ()):
                 store(nc.scalar.copy, sums[done], 0, done)
             return root
@@ -427,8 +420,8 @@ def tile_list_asteroid_band_fluxes_kernel(
                 ahead = roots_of(c + 1)
             h_bf = staged[c % 3][:]
             multiply(0, c, root[:, 0:HALF], h_bf)
-            if c < last:
-                open_sums(c - 1, *pack(staged[(c - 1) % 3][:] if c > SIGNED else signed[c - 1][:]))
+            if SIGNED < c < last:
+                open_sums(c - 1, *pack(staged[(c - 1) % 3][:]))
             if c < last:
                 multiply(1, c, root[:, HALF : 2 * HALF], h_bf)
                 if c - 2 in COPIES_ON_VECTOR:

@@ -74,7 +74,8 @@ def tile_list_asteroid_band_fluxes_kernel(
         a_s = laid.tile([P, kpasses * (S + H)], U8, name="a_s", align_bytes=64, offset=groups * PACK * wide * 4 + T)
         tab2_w = held([P, T], U16, "tab2_w")
         tab_w = [held([P, T], I32, "tab_w%d" % a) for a in range(kpasses)]
-        w1_w = held([P, kpasses * H], U16, "w1_w")
+        w1_place = groups * PACK * wide * 4 + 2 * T
+        w1_w = laid.tile([P, kpasses * H], U16, name="w1_w", align_bytes=64, offset=w1_place)
         w1_wp = held([P, kpasses * H], U16, "w1_wp")
         w_raw = [held([P, PACK, PASS], F32, "w_raw%d" % g) for g in range(groups)]
         emis_raw = held([groups, PASS], F32, "emis_raw")
@@ -112,12 +113,12 @@ def tile_list_asteroid_band_fluxes_kernel(
         for r in range(QUADS):
             nc.sync.dma_start(v2_s[r:P:32, :].bitcast(I32), v2_rows[P - 16 + r : P : 4, :].bitcast(I32))
         nc.sync.dma_start(w_raw[1][:], w2_rows[:, :, PASS : 2 * PASS])
-        load_w1(1)
 
         def load_tab(a):
             nc.sync.dma_start(tab_w[a][:], tab_words[a].rearrange("p t i -> p (t i)").bitcast(I32))
 
         load_tab(0)
+        load_w1(1)
 
         v2_w = [held([P, HALF], U16, "v2_w%d" % j) for j in range(halves)]
         for j in range(halves):
@@ -213,7 +214,12 @@ def tile_list_asteroid_band_fluxes_kernel(
             for t in range(PACK):
                 nc.sync.dma_start(w_raw[g][:, t, :], rows[t])
 
-        deal(w1_wp[:].rearrange("p (u c) -> p u c", c=PASS), w1_w[:], 4)
+
+        def deal_w1(a):
+            cols = slice(a * H, (a + 1) * H)
+            deal(w1_wp[:, cols].rearrange("p (u c) -> p u c", c=PASS), w1_w[:, cols], 4)
+
+        deal_w1(0)
         spans = [((0, HALF), (HALF, HALF)), ((HALF // 2, HALF // 2), (0, HALF // 2), (HALF, HALF))]
         words_of = {}
 
@@ -223,15 +229,27 @@ def tile_list_asteroid_band_fluxes_kernel(
             for c in range(first // CHUNK, (first + count) // CHUNK):
                 words_of[a, c] = picked[:, c * CHUNK - first : (c + 1) * CHUNK - first]
 
-        twins = []
-        for u, (g, j, t) in enumerate(SQUARES_ON_VECTOR):
-            product_b(g, j, t, banks[5 + u])
-            twins.append(held([P, HALF], F32, "twin%d" % u))
+        twins = [held([P, HALF], F32, "twin0")] + [
+            laid.tile([P, HALF], F32, name="twin%d" % (u + 1), align_bytes=64, offset=w1_place + u * HALF * 4) for u in range(2)
+        ]
+
+        def take(u):
             nc.vector.tensor_copy(twins[u][:], banks[5 + u][:])
-        squares_on_scalar(1)
-        gather_words(0, *spans[0][0])
-        for u, (g, j, t) in enumerate(SQUARES_ON_VECTOR):
+
+        def square(u):
+            g, j, t = SQUARES_ON_VECTOR[u]
             nc.vector.tensor_tensor(damp[g][:, t, j * HALF : (j + 1) * HALF], banks[5 + u][:], twins[u][:], MULT)
+
+        for u, place in enumerate(SQUARES_ON_VECTOR):
+            product_b(*place, banks[5 + u])
+        take(0)
+        squares_on_scalar(1)
+        square(0)
+        gather_words(0, *spans[0][0])
+        deal_w1(1)
+        for step in (take, square):
+            for u in (1, 2):
+                step(u)
 
         def damping(places):
             for g, t in places:

@@ -28,9 +28,10 @@ QUADS = 4
 CHUNK = 128
 SIGNED = 2
 EARLY = 4
-SQUARES_ON_VECTOR = ((1, 0, 0), (1, 0, 1), (1, 1, 0))
+SQUARES_ON_VECTOR = ((1, 0, 0), (1, 0, 1), (1, 1, 0), (1, 1, 1))
 FIRST_CASTS_ON_SCALAR = (1,)
-COPIES_ON_VECTOR = (2, 4)
+COPIES_ON_VECTOR = (4,)
+SHARED_COPY = 2
 COPIES_BEHIND_ROOT = {5: (0,), 6: (1, 3)}
 TINY = 2.0**-80
 
@@ -175,7 +176,7 @@ def tile_list_asteroid_band_fluxes_kernel(
             for j in range(halves):
                 for t in range(PACK):
                     if (g, j, t) not in SQUARES_ON_VECTOR:
-                        bank = banks[turn[0] % 5]
+                        bank = banks[turn[0] % 4]
                         turn[0] = turn[0] + 1
                         product_b(g, j, t, bank)
                         nc.scalar.activation(damp[g][:, t, j * HALF : (j + 1) * HALF], bank[:], ACT.Square)
@@ -229,26 +230,28 @@ def tile_list_asteroid_band_fluxes_kernel(
             for c in range(first // CHUNK, (first + count) // CHUNK):
                 words_of[a, c] = picked[:, c * CHUNK - first : (c + 1) * CHUNK - first]
 
-        twins = [held([P, HALF], F32, "twin0")] + [
-            laid.tile([P, HALF], F32, name="twin%d" % (u + 1), align_bytes=64, offset=w1_place + u * HALF * 4) for u in range(2)
+        twins = [held([P, HALF], F32, "twin%d" % u) for u in range(2)] + [
+            laid.tile([P, HALF], F32, name="twin%d" % (u + 2), align_bytes=64, offset=w1_place + u * HALF * 4) for u in range(2)
         ]
 
         def take(u):
-            nc.vector.tensor_copy(twins[u][:], banks[5 + u][:])
+            nc.vector.tensor_copy(twins[u][:], banks[4 + u][:])
 
         def square(u):
             g, j, t = SQUARES_ON_VECTOR[u]
-            nc.vector.tensor_tensor(damp[g][:, t, j * HALF : (j + 1) * HALF], banks[5 + u][:], twins[u][:], MULT)
+            nc.vector.tensor_tensor(damp[g][:, t, j * HALF : (j + 1) * HALF], banks[4 + u][:], twins[u][:], MULT)
 
         for u, place in enumerate(SQUARES_ON_VECTOR):
-            product_b(*place, banks[5 + u])
-        take(0)
+            product_b(*place, banks[4 + u])
+        for u in (0, 1):
+            take(u)
         squares_on_scalar(1)
-        square(0)
+        for u in (0, 1):
+            square(u)
         gather_words(0, *spans[0][0])
         deal_w1(1)
         for step in (take, square):
-            for u in (1, 2):
+            for u in (2, 3):
                 step(u)
 
         def damping(places):
@@ -280,7 +283,7 @@ def tile_list_asteroid_band_fluxes_kernel(
                     stop=(a == kpasses - 1 and t == PACK - 1),
                 )
 
-        free_order = [(turn[0] + u) % 5 for u in range(5)] + [5, 6, 7]
+        free_order = [(turn[0] + u) % 4 for u in range(4)] + [4, 5, 6, 7]
         for u in free_order:
             pass_a(u % groups, u // groups, 0)
 
@@ -364,7 +367,7 @@ def tile_list_asteroid_band_fluxes_kernel(
 
         def store(copy, acc, n0, c, queue=nc.sync):
             tiles = acc.shape[1]
-            res = ring.tile([P, tiles, CHUNK], F32, name="res", align_bytes=64, bufs=9)
+            res = ring.tile([P, tiles, CHUNK], F32, name="res", align_bytes=64, bufs=10)
             copy(res[:], acc)
             rows = out[n0 * P : (n0 + tiles) * P, c * CHUNK : (c + 1) * CHUNK]
             queue.dma_start(rows.rearrange("(u p) j -> p u j", p=P), res[:])
@@ -426,6 +429,8 @@ def tile_list_asteroid_band_fluxes_kernel(
                     for cols in pieces(g, c):
                         part = root[:, g * HALF : (g + 1) * HALF].rearrange("p (t c) -> p t c", t=PACK)[:, :, cols]
                         nc.scalar.activation(part, part, ACT.Sqrt)
+            if c - 4 == SHARED_COPY:
+                store(nc.scalar.copy, sums[c - 4][:, 2:4], 2, c - 4)
             for done in COPIES_BEHIND_ROOT.get(c, ()):
                 store(nc.scalar.copy, sums[done], 0, done)
             return root
@@ -442,6 +447,8 @@ def tile_list_asteroid_band_fluxes_kernel(
                 open_sums(c - 1, *pack(staged[(c - 1) % 3][:]))
             if c < last:
                 multiply(1, c, root[:, HALF : 2 * HALF], h_bf)
+                if c - 2 == SHARED_COPY:
+                    store(nc.vector.tensor_copy, sums[c - 2][:, 0:2], 0, c - 2)
                 if c - 2 in COPIES_ON_VECTOR:
                     store(nc.vector.tensor_copy, sums[c - 2], 0, c - 2)
                 if c == last - 1:

@@ -28,11 +28,14 @@ QUADS = 4
 CHUNK = 128
 SIGNED = 2
 EARLY = 4
+STEP = 4
+LAP = 64
 SQUARES_ON_VECTOR = ((1, 0, 0), (1, 0, 1), (1, 1, 0), (1, 1, 1))
-FIRST_CASTS_ON_SCALAR = (1,)
+FIRST_ROUNDINGS_ON_SCALAR = (1, 2)
+FIRST_SLOTS = (0, 1, 3, 2)
 COPIES_ON_VECTOR = (4,)
-SHARED_COPY = 2
-COPIES_BEHIND_ROOT = {5: (0,), 6: (1, 3)}
+SHARED_COPY = 3
+COPIES_AHEAD_OF_ROOT = {6: (0, 1), 7: (2,)}
 TINY = 2.0**-80
 
 
@@ -45,7 +48,7 @@ def tile_list_asteroid_band_fluxes_kernel(
     kpasses = K // PASS
     chunks = S // CHUNK
     last = chunks - 1
-    wide = SIGNED * CHUNK
+    both = groups * CHUNK
     with ExitStack() as ctx:
         keep = ctx.enter_context(tc.tile_pool(name="keep", bufs=1))
         ring = ctx.enter_context(tc.tile_pool(name="ring", bufs=2))
@@ -56,6 +59,9 @@ def tile_list_asteroid_band_fluxes_kernel(
         def held(shape, dtype, name):
             return keep.tile(shape, dtype, name=name, align_bytes=64)
 
+        def placed(shape, dtype, name, offset):
+            return laid.tile(shape, dtype, name=name, align_bytes=64, offset=offset)
+
         def quantise(codes, scales, values):
             nc.vector.quantize_mx(out=codes.bitcast(FP8X4), scales=scales, in_=values)
 
@@ -65,25 +71,36 @@ def tile_list_asteroid_band_fluxes_kernel(
         def picks(offsets, first, count):
             return offsets[:, first // 16 : (first + count) // 16]
 
-        tab2_s = laid.tile([P, T], U8, name="tab2_s", align_bytes=64, offset=groups * PACK * wide * 4)
-        tab_s = laid.tile([P, T], U8, name="tab_s", align_bytes=64, offset=groups * PACK * wide * 4 + T)
+        at_w1 = 0
+        at_tab2_s = at_w1 + kpasses * H * 2 - LAP
+        at_w2_second = at_tab2_s + T - LAP
+        at_tab0 = at_w2_second + PACK * PASS * 4
+        at_v2_rows = at_tab0 + T * 4 - LAP
+        at_tab1 = at_v2_rows + S
+        at_v_rows = at_tab1 + T * 4 - LAP
+        at_w3 = at_v_rows + S - LAP
+        at_tab_s = at_w3 + groups * PACK * N * 4
+        at_slot1 = at_tab_s + T
+
+        tab2_s = placed([P, T], U8, "tab2_s", at_tab2_s)
+        tab_s = placed([P, T], U8, "tab_s", at_tab_s)
         w1_rows = held([P, H], U8, "w1_rows")
-        v2_rows = held([P, S], U8, "v2_rows")
-        v_rows = held([P, S], U8, "v_rows")
-        joined = held([P, S + H], U8, "joined")
-        v2_s = laid.tile([P, S], U8, name="v2_s", align_bytes=64, offset=groups * PACK * wide * 4)
-        a_s = laid.tile([P, kpasses * (S + H)], U8, name="a_s", align_bytes=64, offset=groups * PACK * wide * 4 + T)
+        v2_rows = placed([P, S], U8, "v2_rows", at_v2_rows)
+        v_rows = placed([P, S], U8, "v_rows", at_v_rows)
+        joined = placed([P, S + H], U8, "joined", at_slot1 + LAP)
+        v2_s = placed([P, S], U8, "v2_s", at_tab2_s + LAP)
+        a_s = placed([P, kpasses * (S + H)], U8, "a_s", at_tab_s)
         tab2_w = held([P, T], U16, "tab2_w")
-        tab_w = [held([P, T], I32, "tab_w%d" % a) for a in range(kpasses)]
-        w1_place = groups * PACK * wide * 4 + 2 * T
-        w1_w = laid.tile([P, kpasses * H], U16, name="w1_w", align_bytes=64, offset=w1_place)
+        tab_w = [placed([P, T], I32, "tab_w%d" % a, (at_tab0, at_tab1)[a]) for a in range(kpasses)]
+        w1_w = placed([P, kpasses * H], U16, "w1_w", at_w1)
         w1_wp = held([P, kpasses * H], U16, "w1_wp")
-        w_raw = [held([P, PACK, PASS], F32, "w_raw%d" % g) for g in range(groups)]
+        w2_raw = [held([P, PACK, PASS], F32, "w2_raw0"), placed([P, PACK, PASS], F32, "w2_raw1", at_w2_second)]
+        w3_raw = placed([P, groups, PACK, N], F32, "w3_raw", at_w3)
         emis_raw = held([groups, PASS], F32, "emis_raw")
         emis_rows = held([P, PASS], F32, "emis_rows")
         ident = held([P, P], F32, "ident")
-        inverse = held([P, groups * PACK], F32, "inverse")
-        inverse2 = held([P, groups * PACK], F32, "inverse2")
+        emis2 = held([P, groups * PACK], F32, "emis2")
+        inverse2 = placed([P, groups * PACK], F32, "inverse2", at_slot1)
         one = held([P, 1], F32, "one")
         warm = held([P, 1], F32, "warm")
 
@@ -103,42 +120,47 @@ def tile_list_asteroid_band_fluxes_kernel(
         nc.sync.dma_start(idx[:], offs)
         nc.sync.dma_start(tab2_w[:].bitcast(I32), tab2_words[0].bitcast(I32))
         nc.sync.dma_start(w1_rows[32:96:2, :].bitcast(I32), w1_scales.rearrange("a q c -> q a c").bitcast(I32))
-        nc.sync.dma_start(w_raw[0][:], w2_rows[:, :, 0:PASS])
+        nc.sync.dma_start(w2_raw[0][:], w2_rows[:, :, 0:PASS])
         nc.sync.dma_start(tab_s[32:96:2, :].bitcast(I32), tab_scales.rearrange("a q t -> q a t").bitcast(I32))
 
-        def load_w1(a):
-            nc.sync.dma_start(w1_w[:, a * H : (a + 1) * H].bitcast(I32), w1_words[a].bitcast(I32))
-
-        load_w1(0)
         nc.vector.tensor_copy(v2_rows[:], tab2_s[:].indirect(idx2[:]))
         for r in range(QUADS):
             nc.sync.dma_start(v2_s[r:P:32, :].bitcast(I32), v2_rows[P - 16 + r : P : 4, :].bitcast(I32))
-        nc.sync.dma_start(w_raw[1][:], w2_rows[:, :, PASS : 2 * PASS])
+        nc.sync.dma_start(w2_raw[1][:], w2_rows[:, :, PASS : 2 * PASS])
+        nc.sync.dma_start(
+            w1_w[:].bitcast(I32).rearrange("p (a x) -> p a x", a=kpasses), w1_words.rearrange("a p x -> p a x").bitcast(I32)
+        )
 
         def load_tab(a):
             nc.sync.dma_start(tab_w[a][:], tab_words[a].rearrange("p t i -> p (t i)").bitcast(I32))
 
         load_tab(0)
-        load_w1(1)
 
         v2_w = [held([P, HALF], U16, "v2_w%d" % j) for j in range(halves)]
         for j in range(halves):
             nc.vector.tensor_copy(v2_w[j][:], tab2_w[:].indirect(picks(idx2, j * HALF, HALF)))
 
-        first_bf = [held([P, PASS], BF16, "first_bf%d" % t) for t in range(PACK)]
-        second_bf = held([P, PASS * PACK], BF16, "second_bf")
         w2_c = [held([P, PASS], U32, "w2_c%d" % g) for g in range(groups)]
         w2_q = [held([P, PASS], U8, "w2_q%d" % g) for g in range(groups)]
-        for t in range(PACK):
-            copy = nc.scalar.copy if t in FIRST_CASTS_ON_SCALAR else nc.vector.tensor_copy
+
+        def round_w2(copy, g, t0, slots, into):
             copy(
-                first_bf[t][:].rearrange("p (b i j) -> p b j i", i=RUN, j=PACK),
-                w_raw[0][:].rearrange("p j (b t i) -> p t b j i", t=PACK, i=RUN)[:, t],
+                into.rearrange("p (t b i j) -> p b t j i", t=slots, i=RUN, j=PACK),
+                w2_raw[g][:].rearrange("p j (b t i) -> p b t j i", t=PACK, i=RUN)[:, :, t0 : t0 + slots],
             )
-            if t > 0:
-                cols = slice((t - 1) * P, t * P)
-                quantise(w2_c[0][:, cols], w2_q[0][:, cols], first_bf[t - 1][:])
-        quantise(w2_c[0][:, PASS - P : PASS], w2_q[0][:, PASS - P : PASS], first_bf[PACK - 1][:])
+
+        def quantise_w2(g, t0, slots, values):
+            cols = slice(t0 * P, (t0 + slots) * P)
+            quantise(w2_c[g][:, cols], w2_q[g][:, cols], values)
+
+        slots = [
+            placed([P, PASS], BF16, "slot%d" % t, at_slot1) if t == 1 else held([P, PASS], BF16, "slot%d" % t)
+            for t in range(PACK)
+        ]
+        for t in range(PACK):
+            round_w2(nc.scalar.copy if t in FIRST_ROUNDINGS_ON_SCALAR else nc.vector.tensor_copy, 0, t, 1, slots[t][:])
+        for t in FIRST_SLOTS:
+            quantise_w2(0, t, 1, slots[t][:])
 
         turned = banks[7]
         nc.scalar.copy(
@@ -147,16 +169,21 @@ def tile_list_asteroid_band_fluxes_kernel(
         )
         for t in range(PACK):
             nc.tensor.transpose(turned[:, t * P : (t + 1) * P], emis_rows[:, t * P : (t + 1) * P], ident[:])
-        nc.vector.reciprocal(
-            inverse[:].rearrange("p (g t) -> p t g", g=groups),
+        nc.scalar.activation(
+            emis2[:].rearrange("p (g t) -> p t g", g=groups),
             turned[:].rearrange("p (t c) -> p t c", t=PACK)[:, :, 0:groups],
+            ACT.Square,
         )
-        nc.vector.tensor_tensor(inverse2[:], inverse[:], inverse[:], MULT)
 
         def unit(g, t):
             return inverse2[:, g * PACK + t : g * PACK + t + 1]
 
-        damp = [held([P, PACK, S], F32, "damp%d" % g) for g in range(groups)]
+        damp = held([P, PACK, chunks * both], F32, "damp")
+        damp_of = damp[:].rearrange("p t (c g e) -> p t c g e", g=groups, e=CHUNK)
+        per_half = HALF // CHUNK
+
+        def by_chunk(ap):
+            return ap.rearrange("p (c e) -> p c e", e=CHUNK)
 
         def product_b(g, j, t, bank):
             cols = slice(t * P, (t + 1) * P)
@@ -170,27 +197,30 @@ def tile_list_asteroid_band_fluxes_kernel(
                 stop=True,
             )
 
+        def squared(g, j, t):
+            return damp_of[:, t, j * per_half : (j + 1) * per_half, g, :]
+
         turn = [0]
 
-        def squares_on_scalar(g):
-            for j in range(halves):
-                for t in range(PACK):
-                    if (g, j, t) not in SQUARES_ON_VECTOR:
-                        bank = banks[turn[0] % 4]
-                        turn[0] = turn[0] + 1
-                        product_b(g, j, t, bank)
-                        nc.scalar.activation(damp[g][:, t, j * HALF : (j + 1) * HALF], bank[:], ACT.Square)
+        def square_on_scalar(g, j, t):
+            bank = banks[turn[0] % 4]
+            turn[0] = turn[0] + 1
+            product_b(g, j, t, bank)
+            nc.scalar.activation(squared(g, j, t), by_chunk(bank[:]), ACT.Square)
 
-        squares_on_scalar(0)
+        for t in FIRST_SLOTS:
+            for j in range(halves):
+                square_on_scalar(0, j, t)
 
         def deal(dst, src, words):
             nc.vector.tensor_copy(
-                dst.bitcast(I32).rearrange("p g (t b w) -> p g b t w", t=PACK, w=words),
+                dst.bitcast(I32).rearrange("p (g t b w) -> p g b t w", t=PACK, b=P // RUN, w=words),
                 src.bitcast(I32).rearrange("p (g b t w) -> p g b t w", t=PACK, b=P // RUN, w=words),
             )
 
+        nc.vector.reciprocal(inverse2[:], emis2[:])
         nc.vector.tensor_copy(v_rows[:], tab_s[:].indirect(idx[:]))
-        deal(joined[:, S : S + H].rearrange("p (g c) -> p g c", g=groups), w1_rows[:], 2)
+        deal(joined[:, S : S + H], w1_rows[:], 2)
         nc.vector.tensor_copy(joined[:, 0:S].bitcast(I32), v_rows[:].bitcast(I32))
 
         def spread_a(a):
@@ -201,26 +231,18 @@ def tile_list_asteroid_band_fluxes_kernel(
         spread_a(0)
         load_tab(1)
         spread_a(1)
-
-        for u in range(2):
-            nc.vector.tensor_copy(
-                second_bf[:].rearrange("p (t b i j) -> p b t j i", t=PACK, i=RUN, j=PACK)[:, :, 2 * u : 2 * u + 2],
-                w_raw[1][:].rearrange("p j (b t i) -> p b t j i", t=PACK, i=RUN)[:, :, 2 * u : 2 * u + 2],
-            )
-        for u in range(2):
-            cols = slice(2 * u * P, (2 * u + 2) * P)
-            quantise(w2_c[1][:, cols], w2_q[1][:, cols], second_bf[:, cols.start * PACK : cols.stop * PACK])
         for g in range(groups):
             rows = w3[g * PASS : (g + 1) * PASS, :].rearrange("(b t i) n -> t b i n", t=PACK, i=RUN)
             for t in range(PACK):
-                nc.sync.dma_start(w_raw[g][:, t, :], rows[t])
+                nc.sync.dma_start(w3_raw[:, g, t, :], rows[t])
 
+        second = [held([P, 2 * PASS], BF16, "second%d" % u) for u in range(2)]
+        for u in range(2):
+            round_w2(nc.vector.tensor_copy, 1, 2 * u, 2, second[u][:])
+        for u in range(2):
+            quantise_w2(1, 2 * u, 2, second[u][:])
+        deal(w1_wp[:], w1_w[:], 4)
 
-        def deal_w1(a):
-            cols = slice(a * H, (a + 1) * H)
-            deal(w1_wp[:, cols].rearrange("p (u c) -> p u c", c=PASS), w1_w[:, cols], 4)
-
-        deal_w1(0)
         spans = [((0, HALF), (HALF, HALF)), ((HALF // 2, HALF // 2), (0, HALF // 2), (HALF, HALF))]
         words_of = {}
 
@@ -231,36 +253,34 @@ def tile_list_asteroid_band_fluxes_kernel(
                 words_of[a, c] = picked[:, c * CHUNK - first : (c + 1) * CHUNK - first]
 
         twins = [held([P, HALF], F32, "twin%d" % u) for u in range(2)] + [
-            laid.tile([P, HALF], F32, name="twin%d" % (u + 2), align_bytes=64, offset=w1_place + u * HALF * 4) for u in range(2)
+            placed([P, HALF], F32, "twin%d" % (u + 2), at_tab0 + u * HALF * 4) for u in range(len(SQUARES_ON_VECTOR) - 2)
         ]
 
         def take(u):
             nc.vector.tensor_copy(twins[u][:], banks[4 + u][:])
 
         def square(u):
-            g, j, t = SQUARES_ON_VECTOR[u]
-            nc.vector.tensor_tensor(damp[g][:, t, j * HALF : (j + 1) * HALF], banks[4 + u][:], twins[u][:], MULT)
-
-        for u, place in enumerate(SQUARES_ON_VECTOR):
-            product_b(*place, banks[4 + u])
-        for u in (0, 1):
-            take(u)
-        squares_on_scalar(1)
-        for u in (0, 1):
-            square(u)
-        gather_words(0, *spans[0][0])
-        deal_w1(1)
-        for step in (take, square):
-            for u in (2, 3):
-                step(u)
+            nc.vector.tensor_tensor(squared(*SQUARES_ON_VECTOR[u]), by_chunk(banks[4 + u][:]), by_chunk(twins[u][:]), MULT)
 
         def damping(places):
             for g, t in places:
-                part = damp[g][:, t, wide:S]
+                part = damp_of[:, t, SIGNED:chunks, g, :]
                 nc.scalar.activation(part, part, ACT.Abs_reciprocal_sqrt, bias=unit(g, t), scale=unit(g, t))
 
+        for u, place in enumerate(SQUARES_ON_VECTOR):
+            product_b(*place, banks[4 + u])
+        for u in range(PACK):
+            square_on_scalar(1, u % halves, 2 + u // halves)
+        for step in (take, square):
+            for u in (0, 1):
+                step(u)
+        for span in spans[0]:
+            gather_words(0, *span)
+        for step in (take, square):
+            for u in range(2, len(SQUARES_ON_VECTOR)):
+                step(u)
+
         damping([(g, t) for g in range(groups) for t in range(PACK)])
-        gather_words(0, *spans[0][1])
         for span in spans[1]:
             gather_words(1, *span)
 
@@ -268,7 +288,10 @@ def tile_list_asteroid_band_fluxes_kernel(
             pair = c if c < EARLY else 2 + c % 2
             return banks[groups * pair + g]
 
-        def pass_a(g, c, a):
+        def by_slot(ap):
+            return ap.rearrange("p (t e) -> p t e", t=PACK)
+
+        def pass_a(g, c, a, opens=0):
             for t in range(PACK):
                 c0 = a * (S + H) + S + g * PASS + t * P
                 w0 = a * H + g * PASS + t * P
@@ -279,49 +302,57 @@ def tile_list_asteroid_band_fluxes_kernel(
                     lhsT_scale=a_s[:, c0 : c0 + P],
                     rhs=words_of[a, c].bitcast(FP8X4),
                     rhs_scale=a_s[:, s0 : s0 + CHUNK],
-                    start=(a == 0 and t == 0),
-                    stop=(a == kpasses - 1 and t == PACK - 1),
+                    start=(a == opens and t == 0),
+                    stop=(a != opens and t == PACK - 1),
                 )
 
-        free_order = [(turn[0] + u) % 4 for u in range(4)] + [4, 5, 6, 7]
+        free_order = [4, 5] + [(turn[0] + u) % 4 for u in range(4)]
         for u in free_order:
             pass_a(u % groups, u // groups, 0)
 
-        roots = [laid.tile([P, PACK, wide], F32, name="roots%d" % g, offset=g * PACK * wide * 4) for g in range(groups)]
-        joint = held([P, PACK, groups, wide], F32, "joint")
-        flat_joint = joint[:].rearrange("p t g c -> p (t g c)")
-        spare = [flat_joint[:, PACK * groups * wide - 2 * HALF :], flat_joint[:, 0 : 2 * HALF]]
-        mags = [held([P, groups * HALF], F32, "mag%d" % u) for u in range(2)]
+        roots = held([P, PACK, SIGNED * both], F32, "roots")
+        roots_of_signed = roots[:].rearrange("p t (c g e) -> p t c g e", g=groups, e=CHUNK)
+        joint = held([P, PACK * SIGNED * both], F32, "joint")
+        joint_of = joint[:].rearrange("p (t c g e) -> p t c g e", t=PACK, g=groups, e=CHUNK)
+        spare = [joint[:, PACK * both :], joint[:, 0 : PACK * both]]
+        mags = [held([P, PACK * both], F32, "mag%d" % u) for u in range(2)] + [
+            placed([P, PACK * both], F32, "mag%d" % (u + 2), at_tab0 + (u + 1) * PACK * both * 4) for u in range(2)
+        ]
+
+        def of_group(root, g):
+            return root.rearrange("p (t g e) -> p t g e", t=PACK, g=groups)[:, :, g, :]
 
         def magnitude(g, c, into):
-            nc.scalar.activation(into[:, g * HALF : (g + 1) * HALF], bank_a(g, c)[:], ACT.Abs)
+            nc.scalar.activation(of_group(into, g), by_slot(bank_a(g, c)[:]), ACT.Abs)
 
         def join(g, c):
-            cols = slice(c * CHUNK, (c + 1) * CHUNK)
             nc.vector.scalar_tensor_tensor(
-                joint[:, :, g, cols],
-                damp[g][:, :, cols],
-                1.0,
-                bank_a(g, c)[:].rearrange("p (t c) -> p t c", t=PACK),
-                ADD,
-                MULT,
+                joint_of[:, :, c, g, :], damp_of[:, :, c, g, :], 1.0, by_slot(bank_a(g, c)[:]), ADD, MULT
             )
 
-        def joint_roots(g, cols):
+        def joint_roots(g):
             for t in range(PACK):
                 nc.scalar.activation(
-                    roots[g][:, t, cols], joint[:, t, g, cols], ACT.Abs_reciprocal_sqrt, bias=TINY, scale=unit(g, t)
+                    roots_of_signed[:, t, :, g, :],
+                    joint_of[:, t, :, g, :],
+                    ACT.Abs_reciprocal_sqrt,
+                    bias=TINY,
+                    scale=unit(g, t),
                 )
 
         for g, c in ((0, 2), (1, 2), (0, 0), (0, 1), (0, 3), (1, 0), (1, 1), (1, 3)):
-            pass_a(g, c, 1)
+            if c < EARLY - 1:
+                pass_a(g, c, 1)
+            else:
+                for a in (1, 0):
+                    pass_a(g, c, a, opens=1)
         for g in range(groups):
             magnitude(g, SIGNED, mags[0][:])
         magnitude(0, SIGNED + 1, mags[1][:])
         for g in range(groups):
             for c in range(SIGNED):
                 join(g, c)
-            joint_roots(g, slice(0, wide))
+            joint_roots(g)
         magnitude(1, SIGNED + 1, mags[1][:])
 
         w3_bf = [held([P, N * PACK], BF16, "w3_bf%d" % g) for g in range(groups)]
@@ -331,22 +362,18 @@ def tile_list_asteroid_band_fluxes_kernel(
         def round_w3(g):
             nc.vector.tensor_copy(
                 w3_bf[g][:].rearrange("p (c i j) -> p c j i", i=4, j=PACK),
-                w_raw[g][:].rearrange("p j (c i) -> p c j i", i=4),
+                w3_raw[:, g].rearrange("p j (c i) -> p c j i", i=4),
             )
 
         round_w3(0)
 
-        def weave(g, c, root, h_bf, cols=slice(0, CHUNK)):
-            first = c * CHUNK
-            return (
-                h_bf[:, g, cols.start * PACK : cols.stop * PACK].rearrange("p (c i t) -> p c t i", i=4, t=PACK),
-                root.rearrange("p (t c) -> p t c", t=PACK)[:, :, cols].rearrange("p t (c i) -> p c t i", i=4),
-                (roots if c < SIGNED else damp)[g][:, :, first + cols.start : first + cols.stop].rearrange("p t (c i) -> p c t i", i=4),
+        def multiply(into, left, right):
+            nc.vector.tensor_tensor(
+                into.rearrange("p (q i t) -> p q t i", i=STEP, t=PACK),
+                left.rearrange("p t (q i) -> p q t i", i=STEP),
+                right.rearrange("p t (q i) -> p q t i", i=STEP),
+                MULT,
             )
-
-        def multiply(g, c, root, h_bf, cols=slice(0, CHUNK)):
-            into, left, right = weave(g, c, root, h_bf, cols)
-            nc.vector.tensor_tensor(into, right, left, MULT)
 
         def flux(acc, n0, g, h_c, h_q):
             tiles = acc.shape[1]
@@ -356,8 +383,8 @@ def tile_list_asteroid_band_fluxes_kernel(
                     out=acc[:, u, :],
                     lhsT=w3_c[g][:, bands].bitcast(FP8X4),
                     lhsT_scale=w3_q[g][:, bands],
-                    rhs=h_c[:, g, :].bitcast(FP8X4),
-                    rhs_scale=h_q[:, g, :],
+                    rhs=h_c[:, g * CHUNK : (g + 1) * CHUNK].bitcast(FP8X4),
+                    rhs_scale=h_q[:, g * CHUNK : (g + 1) * CHUNK],
                     start=(g == 0 and u == 0),
                     stop=(g == groups - 1 and u == tiles - 1),
                 )
@@ -373,18 +400,14 @@ def tile_list_asteroid_band_fluxes_kernel(
             queue.dma_start(rows.rearrange("(u p) j -> p u j", p=P), res[:])
 
         def packed_tiles():
-            h_c = ring.tile([P, groups, CHUNK], U32, name="h_c", align_bytes=64, bufs=4)
-            h_q = ring.tile([P, groups, CHUNK], U8, name="h_q", align_bytes=64, bufs=4)
+            h_c = ring.tile([P, both], U32, name="h_c", align_bytes=64, bufs=4)
+            h_q = ring.tile([P, both], U8, name="h_q", align_bytes=64, bufs=4)
             return h_c, h_q
 
         def pack(h_bf):
             h_c, h_q = packed_tiles()
-            quantise(
-                h_c[:].rearrange("p g c -> p (g c)"),
-                h_q[:].rearrange("p g c -> p (g c)"),
-                h_bf.rearrange("p g c -> p (g c)"),
-            )
-            return h_c, h_q
+            quantise(h_c[:], h_q[:], h_bf)
+            return h_c[:], h_q[:]
 
         sums = {}
 
@@ -393,79 +416,80 @@ def tile_list_asteroid_band_fluxes_kernel(
             for g in range(groups):
                 flux(sums[c], 0, g, h_c, h_q)
 
-        signed = held([P, SIGNED, groups, PACK * CHUNK], BF16, "signed")
-        mirror = held([P, SIGNED * groups * PACK * CHUNK], BF16, "mirror")
-        flat = signed[:].rearrange("p c g x -> p (c g x)")
-        signed_c = held([P, SIGNED, groups, CHUNK], U32, "signed_c")
-        signed_q = held([P, SIGNED, groups, CHUNK], U8, "signed_q")
+        signed = held([P, SIGNED * both * PACK], BF16, "signed")
+        mirror = held([P, SIGNED * both * PACK], BF16, "mirror")
+        signed_c = held([P, SIGNED * both], U32, "signed_c")
+        signed_q = held([P, SIGNED * both], U8, "signed_q")
         for g in range(groups):
             for c in range(SIGNED):
-                multiply(g, c, bank_a(g, c)[:], signed[:, c])
+                at = (c * groups + g) * CHUNK * PACK
+                multiply(signed[:, at : at + CHUNK * PACK], roots_of_signed[:, :, c, g, :], by_slot(bank_a(g, c)[:]))
         quantise(w3_c[0][:], w3_q[0][:], w3_bf[0][:])
-        nc.vector.tensor_scalar(mirror[:], flat, -1.0, None, MULT)
+        nc.vector.tensor_scalar(mirror[:], signed[:], -1.0, None, MULT)
         round_w3(1)
-        nc.vector.tensor_tensor(flat, flat, mirror[:], MAX)
+        nc.vector.tensor_tensor(signed[:], signed[:], mirror[:], MAX)
         quantise(w3_c[1][:], w3_q[1][:], w3_bf[1][:])
-        quantise(signed_c[:].rearrange("p c g x -> p (c g x)"), signed_q[:].rearrange("p c g x -> p (c g x)"), flat)
+        quantise(signed_c[:], signed_q[:], signed[:])
         for c in range(SIGNED):
-            open_sums(c, signed_c[:, c], signed_q[:, c])
+            open_sums(c, signed_c[:, c * both : (c + 1) * both], signed_q[:, c * both : (c + 1) * both])
 
-        def pieces(g, c):
-            cuts = 2 if (g, c) == (groups - 1, last) else 1
-            return [slice(u * CHUNK // cuts, (u + 1) * CHUNK // cuts) for u in range(cuts)]
+        root_in = dict(enumerate(spare + [tile[:] for tile in mags], SIGNED))
+        ends = (slice(0, CHUNK), slice(CHUNK, CHUNK + CHUNK // 2), slice(CHUNK + CHUNK // 2, both))
+
+        def magnitudes(c):
+            for g in range(groups):
+                for a in range(kpasses):
+                    pass_a(g, c, a)
+                magnitude(g, c, root_in[c])
 
         def roots_of(c):
-            u = (c - SIGNED) % 2
-            if c < SIGNED + 2:
-                root = spare[u]
-                nc.scalar.activation(root, mags[u][:], ACT.Sqrt)
-            else:
-                root = mags[u][:] if c < SIGNED + 4 else spare[u]
-                for g in range(groups):
-                    for a in range(kpasses):
-                        pass_a(g, c, a)
-                    magnitude(g, c, root)
-                for g in range(groups):
-                    for cols in pieces(g, c):
-                        part = root[:, g * HALF : (g + 1) * HALF].rearrange("p (t c) -> p t c", t=PACK)[:, :, cols]
-                        nc.scalar.activation(part, part, ACT.Sqrt)
-            if c - 4 == SHARED_COPY:
-                store(nc.scalar.copy, sums[c - 4][:, 2:4], 2, c - 4)
-            for done in COPIES_BEHIND_ROOT.get(c, ()):
+            if c == last:
+                magnitudes(c)
+            for done in COPIES_AHEAD_OF_ROOT.get(c, ()):
                 store(nc.scalar.copy, sums[done], 0, done)
-            return root
+            for cols in ends if c == last else (slice(0, both),):
+                source = mags[c - SIGNED][:] if c < EARLY else root_in[c]
+                nc.scalar.activation(by_slot(root_in[c])[:, :, cols], by_slot(source)[:, :, cols], ACT.Sqrt)
+            if c + 2 < last:
+                magnitudes(c + 2)
 
-        staged = [held([P, groups, PACK * CHUNK], BF16, "staged%d" % u) for u in range(3)]
-        ahead = roots_of(SIGNED)
-        for c in range(SIGNED, chunks):
-            root = ahead
-            if c < last:
-                ahead = roots_of(c + 1)
-            h_bf = staged[c % 3][:]
-            multiply(0, c, root[:, 0:HALF], h_bf)
-            if SIGNED < c < last:
+        def product(c, h_bf, cols=slice(0, both)):
+            factor = damp[:, :, c * both + cols.start : c * both + cols.stop]
+            multiply(h_bf[:, cols.start * PACK : cols.stop * PACK], factor, by_slot(root_in[c])[:, :, cols])
+
+        staged = [held([P, both * PACK], BF16, "staged%d" % u) for u in range(3)]
+        roots_of(SIGNED)
+        for c in range(SIGNED, last):
+            if c + 1 < last:
+                roots_of(c + 1)
+            product(c, staged[c % 3][:])
+            if c > SIGNED:
                 open_sums(c - 1, *pack(staged[(c - 1) % 3][:]))
-            if c < last:
-                multiply(1, c, root[:, HALF : 2 * HALF], h_bf)
-                if c - 2 == SHARED_COPY:
-                    store(nc.vector.tensor_copy, sums[c - 2][:, 0:2], 0, c - 2)
-                if c - 2 in COPIES_ON_VECTOR:
-                    store(nc.vector.tensor_copy, sums[c - 2], 0, c - 2)
-                if c == last - 1:
-                    open_sums(c, *pack(h_bf))
-            else:
-                h_c, h_q = packed_tiles()
-                accs = [(sums_in(banks[4], 2), 0), (sums_in(banks[5], 2), 2)]
-                left, right = pieces(1, c)
-                multiply(1, c, root[:, HALF : 2 * HALF], h_bf, left)
-                quantise(h_c[:, 0, :], h_q[:, 0, :], h_bf[:, 0, :])
-                multiply(1, c, root[:, HALF : 2 * HALF], h_bf, right)
-                for cols in (left, right):
-                    quantise(h_c[:, 1, cols], h_q[:, 1, cols], h_bf[:, 1, cols.start * PACK : cols.stop * PACK])
-                for g in range(groups):
-                    for acc, n0 in accs:
-                        flux(acc, n0, g, h_c, h_q)
-                for done in (c - 2, c - 1):
-                    store(nc.scalar.copy, sums[done], 0, done)
-                store(nc.vector.tensor_copy, *accs[0], c)
-                store(nc.scalar.copy, *accs[1], c, nc.scalar)
+            if c + 1 == last:
+                roots_of(last)
+            if c - 2 == SHARED_COPY:
+                store(nc.vector.tensor_copy, sums[c - 2][:, 0:2], 0, c - 2)
+            if c - 2 in COPIES_ON_VECTOR:
+                store(nc.vector.tensor_copy, sums[c - 2], 0, c - 2)
+        open_sums(last - 1, *pack(staged[(last - 1) % 3][:]))
+        h_bf = staged[last % 3][:]
+        h_c, h_q = packed_tiles()
+        accs = [(sums_in(banks[4], 2), 0), (sums_in(banks[5], 2), 2)]
+
+        def pack_end(cols):
+            quantise(h_c[:, cols], h_q[:, cols], h_bf[:, cols.start * PACK : cols.stop * PACK])
+
+        product(last, h_bf, ends[0])
+        product(last, h_bf, ends[1])
+        pack_end(ends[0])
+        product(last, h_bf, ends[2])
+        pack_end(ends[1])
+        pack_end(ends[2])
+        for g in range(groups):
+            for acc, n0 in accs:
+                flux(acc, n0, g, h_c[:], h_q[:])
+        store(nc.scalar.copy, sums[SHARED_COPY][:, 2:4], 2, SHARED_COPY)
+        for done in (last - 2, last - 1):
+            store(nc.scalar.copy, sums[done], 0, done)
+        store(nc.vector.tensor_copy, *accs[0], last)
+        store(nc.scalar.copy, *accs[1], last, nc.scalar)

@@ -31,8 +31,8 @@ EARLY = 4
 STEP = 4
 LAP = 64
 SQUARES_ON_VECTOR = ((1, 0, 0), (1, 0, 1), (1, 1, 0), (1, 1, 1))
-FIRST_ROUNDINGS_ON_SCALAR = (1, 2)
-FIRST_SLOTS = (0, 1, 3, 2)
+FIRST_ROUNDINGS_ON_SCALAR = (0, 1, 2)
+FIRST_SLOTS = (0, 3, 1, 2)
 COPIES_ON_VECTOR = (4,)
 SHARED_COPY = 3
 COPIES_AHEAD_OF_ROOT = {6: (0, 1), 7: (2,)}
@@ -87,7 +87,7 @@ def tile_list_asteroid_band_fluxes_kernel(
         w1_rows = held([P, H], U8, "w1_rows")
         v2_rows = placed([P, S], U8, "v2_rows", at_v2_rows)
         v_rows = placed([P, S], U8, "v_rows", at_v_rows)
-        joined = placed([P, S + H], U8, "joined", at_slot1 + LAP)
+        joined = held([P, S + H], U8, "joined")
         v2_s = placed([P, S], U8, "v2_s", at_tab2_s + LAP)
         a_s = placed([P, kpasses * (S + H)], U8, "a_s", at_tab_s)
         tab2_w = held([P, T], U16, "tab2_w")
@@ -212,15 +212,16 @@ def tile_list_asteroid_band_fluxes_kernel(
             for j in range(halves):
                 square_on_scalar(0, j, t)
 
-        def deal(dst, src, words):
-            nc.vector.tensor_copy(
-                dst.bitcast(I32).rearrange("p (g t b w) -> p g b t w", t=PACK, b=P // RUN, w=words),
-                src.bitcast(I32).rearrange("p (g b t w) -> p g b t w", t=PACK, b=P // RUN, w=words),
+        def deal(copy, dst, src, words):
+            copy(
+                dst.bitcast(U32).rearrange("p (g t b w) -> p g b t w", t=PACK, b=P // RUN, w=words),
+                src.bitcast(U32).rearrange("p (g b t w) -> p g b t w", t=PACK, b=P // RUN, w=words),
             )
+
+        deal(nc.scalar.copy, joined[:, S : S + H], w1_rows[:], 2)
 
         nc.vector.reciprocal(inverse2[:], emis2[:])
         nc.vector.tensor_copy(v_rows[:], tab_s[:].indirect(idx[:]))
-        deal(joined[:, S : S + H], w1_rows[:], 2)
         nc.vector.tensor_copy(joined[:, 0:S].bitcast(I32), v_rows[:].bitcast(I32))
 
         def spread_a(a):
@@ -241,7 +242,7 @@ def tile_list_asteroid_band_fluxes_kernel(
             round_w2(nc.vector.tensor_copy, 1, 2 * u, 2, second[u][:])
         for u in range(2):
             quantise_w2(1, 2 * u, 2, second[u][:])
-        deal(w1_wp[:], w1_w[:], 4)
+        deal(nc.vector.tensor_copy, w1_wp[:], w1_w[:], 4)
 
         spans = [((0, HALF), (HALF, HALF)), ((HALF // 2, HALF // 2), (0, HALF // 2), (HALF, HALF))]
         words_of = {}

@@ -28,6 +28,8 @@ QUADS = 4
 CHUNK = 128
 SIGNED = 2
 EARLY = 4
+PAIR_OF_CHUNK = (0, 1, 2, 3, 2, 3, 0, 1)
+BANK_OF_SUMS = (4, 5, 6, 7, 0, 1, 4)
 STEP = 4
 LAP = 64
 SQUARES_ON_VECTOR = ((1, 0, 0), (1, 0, 1), (1, 1, 0), (1, 1, 1))
@@ -72,7 +74,7 @@ def tile_list_asteroid_band_fluxes_kernel(
             return offsets[:, first // 16 : (first + count) // 16]
 
         at_w1 = 0
-        at_tab2_s = at_w1 + kpasses * H * 2 - LAP
+        at_tab2_s = at_w1 + H * 2 - LAP
         at_w2_second = at_tab2_s + T - LAP
         at_tab0 = at_w2_second + PACK * PASS * 4
         at_v2_rows = at_tab0 + T * 4 - LAP
@@ -92,7 +94,7 @@ def tile_list_asteroid_band_fluxes_kernel(
         a_s = placed([P, kpasses * (S + H)], U8, "a_s", at_tab_s)
         tab2_w = held([P, T], U16, "tab2_w")
         tab_w = [placed([P, T], I32, "tab_w%d" % a, (at_tab0, at_tab1)[a]) for a in range(kpasses)]
-        w1_w = placed([P, kpasses * H], U16, "w1_w", at_w1)
+        w1_w = [held([P, H], U16, "w1_w0"), placed([P, H], U16, "w1_w1", at_w1)]
         w1_wp = held([P, kpasses * H], U16, "w1_wp")
         w2_raw = [held([P, PACK, PASS], F32, "w2_raw0"), placed([P, PACK, PASS], F32, "w2_raw1", at_w2_second)]
         w3_raw = placed([P, groups, PACK, N], F32, "w3_raw", at_w3)
@@ -123,13 +125,12 @@ def tile_list_asteroid_band_fluxes_kernel(
         nc.sync.dma_start(w2_raw[0][:], w2_rows[:, :, 0:PASS])
         nc.sync.dma_start(tab_s[32:96:2, :].bitcast(I32), tab_scales.rearrange("a q t -> q a t").bitcast(I32))
 
+        nc.sync.dma_start(w1_w[0][:].bitcast(I32), w1_words[0].bitcast(I32))
         nc.vector.tensor_copy(v2_rows[:], tab2_s[:].indirect(idx2[:]))
         for r in range(QUADS):
             nc.sync.dma_start(v2_s[r:P:32, :].bitcast(I32), v2_rows[P - 16 + r : P : 4, :].bitcast(I32))
         nc.sync.dma_start(w2_raw[1][:], w2_rows[:, :, PASS : 2 * PASS])
-        nc.sync.dma_start(
-            w1_w[:].bitcast(I32).rearrange("p (a x) -> p a x", a=kpasses), w1_words.rearrange("a p x -> p a x").bitcast(I32)
-        )
+        nc.sync.dma_start(w1_w[1][:].bitcast(I32), w1_words[1].bitcast(I32))
 
         def load_tab(a):
             nc.sync.dma_start(tab_w[a][:], tab_words[a].rearrange("p t i -> p (t i)").bitcast(I32))
@@ -242,7 +243,8 @@ def tile_list_asteroid_band_fluxes_kernel(
             round_w2(nc.vector.tensor_copy, 1, 2 * u, 2, second[u][:])
         for u in range(2):
             quantise_w2(1, 2 * u, 2, second[u][:])
-        deal(nc.vector.tensor_copy, w1_wp[:], w1_w[:], 4)
+        for a in range(kpasses):
+            deal(nc.vector.tensor_copy, w1_wp[:, a * H : (a + 1) * H], w1_w[a][:], 4)
 
         spans = [((0, HALF), (HALF, HALF)), ((HALF // 2, HALF // 2), (0, HALF // 2), (HALF, HALF))]
         words_of = {}
@@ -286,13 +288,12 @@ def tile_list_asteroid_band_fluxes_kernel(
             gather_words(1, *span)
 
         def bank_a(g, c):
-            pair = c if c < EARLY else 2 + c % 2
-            return banks[groups * pair + g]
+            return banks[groups * PAIR_OF_CHUNK[c] + g]
 
         def by_slot(ap):
             return ap.rearrange("p (t e) -> p t e", t=PACK)
 
-        def pass_a(g, c, a, opens=0):
+        def pass_a(g, c, a):
             for t in range(PACK):
                 c0 = a * (S + H) + S + g * PASS + t * P
                 w0 = a * H + g * PASS + t * P
@@ -303,11 +304,11 @@ def tile_list_asteroid_band_fluxes_kernel(
                     lhsT_scale=a_s[:, c0 : c0 + P],
                     rhs=words_of[a, c].bitcast(FP8X4),
                     rhs_scale=a_s[:, s0 : s0 + CHUNK],
-                    start=(a == opens and t == 0),
-                    stop=(a != opens and t == PACK - 1),
+                    start=(a == 0 and t == 0),
+                    stop=(a == kpasses - 1 and t == PACK - 1),
                 )
 
-        free_order = [4, 5] + [(turn[0] + u) % 4 for u in range(4)]
+        free_order = [4, 5] + [(turn[0] + u) % 4 for u in range(4)] + [6, 7]
         for u in free_order:
             pass_a(u % groups, u // groups, 0)
 
@@ -342,11 +343,7 @@ def tile_list_asteroid_band_fluxes_kernel(
                 )
 
         for g, c in ((0, 2), (1, 2), (0, 0), (0, 1), (0, 3), (1, 0), (1, 1), (1, 3)):
-            if c < EARLY - 1:
-                pass_a(g, c, 1)
-            else:
-                for a in (1, 0):
-                    pass_a(g, c, a, opens=1)
+            pass_a(g, c, 1)
         for g in range(groups):
             magnitude(g, SIGNED, mags[0][:])
         magnitude(0, SIGNED + 1, mags[1][:])
@@ -355,6 +352,14 @@ def tile_list_asteroid_band_fluxes_kernel(
                 join(g, c)
             joint_roots(g)
         magnitude(1, SIGNED + 1, mags[1][:])
+
+        def sum_a(chunk_range):
+            for c in chunk_range:
+                for g in range(groups):
+                    for a in range(kpasses):
+                        pass_a(g, c, a)
+
+        sum_a(range(EARLY, EARLY + 2))
 
         w3_bf = [held([P, N * PACK], BF16, "w3_bf%d" % g) for g in range(groups)]
         w3_c = [held([P, N], U32, "w3_c%d" % g) for g in range(groups)]
@@ -413,7 +418,7 @@ def tile_list_asteroid_band_fluxes_kernel(
         sums = {}
 
         def open_sums(c, h_c, h_q):
-            sums[c] = sums_in(banks[c % 4], N // P)
+            sums[c] = sums_in(banks[BANK_OF_SUMS[c]], N // P)
             for g in range(groups):
                 flux(sums[c], 0, g, h_c, h_q)
 
@@ -425,22 +430,19 @@ def tile_list_asteroid_band_fluxes_kernel(
             for c in range(SIGNED):
                 at = (c * groups + g) * CHUNK * PACK
                 multiply(signed[:, at : at + CHUNK * PACK], roots_of_signed[:, :, c, g, :], by_slot(bank_a(g, c)[:]))
+        sum_a(range(EARLY + 2, chunks))
         quantise(w3_c[0][:], w3_q[0][:], w3_bf[0][:])
         nc.vector.tensor_scalar(mirror[:], signed[:], -1.0, None, MULT)
         round_w3(1)
         nc.vector.tensor_tensor(signed[:], signed[:], mirror[:], MAX)
         quantise(w3_c[1][:], w3_q[1][:], w3_bf[1][:])
         quantise(signed_c[:], signed_q[:], signed[:])
-        for c in range(SIGNED):
-            open_sums(c, signed_c[:, c * both : (c + 1) * both], signed_q[:, c * both : (c + 1) * both])
 
         root_in = dict(enumerate(spare + [tile[:] for tile in mags], SIGNED))
         ends = (slice(0, CHUNK), slice(CHUNK, CHUNK + CHUNK // 2), slice(CHUNK + CHUNK // 2, both))
 
         def magnitudes(c):
             for g in range(groups):
-                for a in range(kpasses):
-                    pass_a(g, c, a)
                 magnitude(g, c, root_in[c])
 
         def roots_of(c):
@@ -460,6 +462,8 @@ def tile_list_asteroid_band_fluxes_kernel(
 
         staged = [held([P, both * PACK], BF16, "staged%d" % u) for u in range(3)]
         roots_of(SIGNED)
+        for c in range(SIGNED):
+            open_sums(c, signed_c[:, c * both : (c + 1) * both], signed_q[:, c * both : (c + 1) * both])
         for c in range(SIGNED, last):
             if c + 1 < last:
                 roots_of(c + 1)
@@ -475,7 +479,7 @@ def tile_list_asteroid_band_fluxes_kernel(
         open_sums(last - 1, *pack(staged[(last - 1) % 3][:]))
         h_bf = staged[last % 3][:]
         h_c, h_q = packed_tiles()
-        accs = [(sums_in(banks[4], 2), 0), (sums_in(banks[5], 2), 2)]
+        accs = [(sums_in(banks[2], 2), 0), (sums_in(banks[3], 2), 2)]
 
         def pack_end(cols):
             quantise(h_c[:, cols], h_q[:, cols], h_bf[:, cols.start * PACK : cols.stop * PACK])

@@ -30,7 +30,7 @@ SIGNED = 2
 EARLY = 4
 PAIR_OF_CHUNK = (0, 1, 2, 3, 2, 3, 0, 1)
 BANK_OF_SUMS = (4, 5, 6, 7, 0, 1, 4)
-STEP = 4
+STEP = 2
 LAP = 64
 SQUARES_ON_VECTOR = ((1, 0, 0), (1, 0, 1), (1, 1, 0), (1, 1, 1))
 FIRST_ROUNDINGS_ON_SCALAR = (0, 1, 2)

@@ -342,16 +342,15 @@ def tile_list_asteroid_band_fluxes_kernel(
                     scale=unit(g, t),
                 )
 
-        for g, c in ((0, 2), (1, 2), (0, 0), (0, 1), (0, 3), (1, 0), (1, 1), (1, 3)):
+        for g, c in ((0, 2), (1, 2), (0, 0), (0, 3), (0, 1), (1, 3), (1, 0), (1, 1)):
             pass_a(g, c, 1)
-        for g in range(groups):
-            magnitude(g, SIGNED, mags[0][:])
-        magnitude(0, SIGNED + 1, mags[1][:])
+        for c in range(SIGNED, EARLY):
+            for g in range(groups):
+                magnitude(g, c, mags[c - SIGNED][:])
         for g in range(groups):
             for c in range(SIGNED):
                 join(g, c)
             joint_roots(g)
-        magnitude(1, SIGNED + 1, mags[1][:])
 
         def sum_a(chunk_range):
             for c in chunk_range:
@@ -439,7 +438,7 @@ def tile_list_asteroid_band_fluxes_kernel(
         quantise(signed_c[:], signed_q[:], signed[:])
 
         root_in = dict(enumerate(spare + [tile[:] for tile in mags], SIGNED))
-        ends = (slice(0, CHUNK), slice(CHUNK, CHUNK + CHUNK // 2), slice(CHUNK + CHUNK // 2, both))
+        ends = (slice(0, CHUNK), slice(CHUNK, both))
 
         def magnitudes(c):
             for g in range(groups):
@@ -484,12 +483,10 @@ def tile_list_asteroid_band_fluxes_kernel(
         def pack_end(cols):
             quantise(h_c[:, cols], h_q[:, cols], h_bf[:, cols.start * PACK : cols.stop * PACK])
 
-        product(last, h_bf, ends[0])
-        product(last, h_bf, ends[1])
-        pack_end(ends[0])
-        product(last, h_bf, ends[2])
-        pack_end(ends[1])
-        pack_end(ends[2])
+        for cols in ends:
+            product(last, h_bf, cols)
+        for cols in ends:
+            pack_end(cols)
         for g in range(groups):
             for acc, n0 in accs:
                 flux(acc, n0, g, h_c[:], h_q[:])

@@ -74,7 +74,7 @@ def tile_list_asteroid_band_fluxes_kernel(
             return offsets[:, first // 16 : (first + count) // 16]
 
         at_w1 = 0
-        at_tab2_s = at_w1 + H * 2 - LAP
+        at_tab2_s = at_w1 + kpasses * H * 2 - LAP
         at_w2_second = at_tab2_s + T - LAP
         at_tab0 = at_w2_second + PACK * PASS * 4
         at_v2_rows = at_tab0 + T * 4 - LAP
@@ -94,7 +94,7 @@ def tile_list_asteroid_band_fluxes_kernel(
         a_s = placed([P, kpasses * (S + H)], U8, "a_s", at_tab_s)
         tab2_w = held([P, T], U16, "tab2_w")
         tab_w = [placed([P, T], I32, "tab_w%d" % a, (at_tab0, at_tab1)[a]) for a in range(kpasses)]
-        w1_w = [held([P, H], U16, "w1_w0"), placed([P, H], U16, "w1_w1", at_w1)]
+        w1_w = placed([P, kpasses * H], U16, "w1_w", at_w1)
         w1_wp = held([P, kpasses * H], U16, "w1_wp")
         w2_raw = [held([P, PACK, PASS], F32, "w2_raw0"), placed([P, PACK, PASS], F32, "w2_raw1", at_w2_second)]
         w3_raw = placed([P, groups, PACK, N], F32, "w3_raw", at_w3)
@@ -125,12 +125,13 @@ def tile_list_asteroid_band_fluxes_kernel(
         nc.sync.dma_start(w2_raw[0][:], w2_rows[:, :, 0:PASS])
         nc.sync.dma_start(tab_s[32:96:2, :].bitcast(I32), tab_scales.rearrange("a q t -> q a t").bitcast(I32))
 
-        nc.sync.dma_start(w1_w[0][:].bitcast(I32), w1_words[0].bitcast(I32))
         nc.vector.tensor_copy(v2_rows[:], tab2_s[:].indirect(idx2[:]))
         for r in range(QUADS):
             nc.sync.dma_start(v2_s[r:P:32, :].bitcast(I32), v2_rows[P - 16 + r : P : 4, :].bitcast(I32))
         nc.sync.dma_start(w2_raw[1][:], w2_rows[:, :, PASS : 2 * PASS])
-        nc.sync.dma_start(w1_w[1][:].bitcast(I32), w1_words[1].bitcast(I32))
+        nc.sync.dma_start(
+            w1_w[:].bitcast(I32).rearrange("p (a x) -> p a x", a=kpasses), w1_words.rearrange("a p x -> p a x").bitcast(I32)
+        )
 
         def load_tab(a):
             nc.sync.dma_start(tab_w[a][:], tab_words[a].rearrange("p t i -> p (t i)").bitcast(I32))
@@ -243,8 +244,7 @@ def tile_list_asteroid_band_fluxes_kernel(
             round_w2(nc.vector.tensor_copy, 1, 2 * u, 2, second[u][:])
         for u in range(2):
             quantise_w2(1, 2 * u, 2, second[u][:])
-        for a in range(kpasses):
-            deal(nc.vector.tensor_copy, w1_wp[:, a * H : (a + 1) * H], w1_w[a][:], 4)
+        deal(nc.vector.tensor_copy, w1_wp[:], w1_w[:], 4)
 
         spans = [((0, HALF), (HALF, HALF)), ((HALF // 2, HALF // 2), (0, HALF // 2), (HALF, HALF))]
         words_of = {}

from contextlib import ExitStack

import concourse.mybir as mybir
from concourse.masks import make_identity

K, K2, T, S, H, N = 1024, 512, 4096, 1024, 1024, 512
FLOPS = 2 * S * (K * H + K2 * H + H * N)

F32 = mybir.dt.float32
BF16 = mybir.dt.bfloat16
I32 = mybir.dt.int32
U32 = mybir.dt.uint32
U16 = mybir.dt.uint16
U8 = mybir.dt.uint8
FP8X4 = mybir.dt.float8_e4m3fn_x4
FP4X4 = mybir.dt.float4_e2m1fn_x4
ACT = mybir.ActivationFunctionType
MULT = mybir.AluOpType.mult
MAX = mybir.AluOpType.max
ADD = mybir.AluOpType.add

P = 128
PACK = 4
PASS = P * PACK
HALF = 512
RUN = 8
QUADS = 4
CHUNK = 128
SIGNED = 2
EARLY = 4
PAIR_OF_CHUNK = (0, 1, 2, 3, 2, 3, 0, 1)
BANK_OF_SUMS = (4, 5, 6, 7, 0, 1, 4)
STEP = 2
LAP = 64
SQUARES_ON_VECTOR = ((1, 0, 0), (1, 0, 1), (1, 1, 0), (1, 1, 1))
FIRST_ROUNDINGS_ON_SCALAR = (0, 1, 2)
FIRST_SLOTS = (0, 3, 1, 2)
COPIES_ON_VECTOR = (4,)
SHARED_COPY = 3
COPIES_AHEAD_OF_ROOT = {6: (0, 1), 7: (2,)}
TINY = 2.0**-80


def tile_list_asteroid_band_fluxes_kernel(
    tc, tab_words, tab_scales, tab2_words, tab2_scales, offs, offs2, w1_words, w1_scales, w2, emis, w3, out
):
    nc = tc.nc
    halves = S // HALF
    groups = H // PASS
    kpasses = K // PASS
    chunks = S // CHUNK
    last = chunks - 1
    both = groups * CHUNK
    with ExitStack() as ctx:
        keep = ctx.enter_context(tc.tile_pool(name="keep", bufs=1))
        ring = ctx.enter_context(tc.tile_pool(name="ring", bufs=2))
        laid = ctx.enter_context(tc.tile_pool(name="laid", bufs=1))
        psum = ctx.enter_context(tc.psum_pool(name="psum", bufs=1))
        banks = [psum.tile([P, HALF], F32, name="bank%d" % u) for u in range(8)]

        def held(shape, dtype, name):
            return keep.tile(shape, dtype, name=name, align_bytes=64)

        def placed(shape, dtype, name, offset):
            return laid.tile(shape, dtype, name=name, align_bytes=64, offset=offset)

        def quantise(codes, scales, values):
            nc.vector.quantize_mx(out=codes.bitcast(FP8X4), scales=scales, in_=values)

        idx = keep.tile([P, S // 16], U16, name="idx")
        idx2 = keep.tile([P, S // 16], U16, name="idx2")

        def picks(offsets, first, count):
            return offsets[:, first // 16 : (first + count) // 16]

        at_w1 = 0
        at_tab2_s = at_w1 + kpasses * H * 2 - LAP
        at_w2_second = at_tab2_s + T - LAP
        at_tab0 = at_w2_second + PACK * PASS * 4
        at_v2_rows = at_tab0 + T * 4 - LAP
        at_tab1 = at_v2_rows + S
        at_v_rows = at_tab1 + T * 4 - LAP
        at_w3 = at_v_rows + S - LAP
        at_tab_s = at_w3 + groups * PACK * N * 4
        at_slot1 = at_tab_s + T

        tab2_s = placed([P, T], U8, "tab2_s", at_tab2_s)
        tab_s = placed([P, T], U8, "tab_s", at_tab_s)
        w1_rows = held([P, H], U8, "w1_rows")
        v2_rows = placed([P, S], U8, "v2_rows", at_v2_rows)
        v_rows = placed([P, S], U8, "v_rows", at_v_rows)
        joined = held([P, S + H], U8, "joined")
        v2_s = placed([P, S], U8, "v2_s", at_tab2_s + LAP)
        a_s = placed([P, kpasses * (S + H)], U8, "a_s", at_tab_s)
        tab2_w = held([P, T], U16, "tab2_w")
        tab_w = [placed([P, T], I32, "tab_w%d" % a, (at_tab0, at_tab1)[a]) for a in range(kpasses)]
        w1_w = placed([P, kpasses * H], U16, "w1_w", at_w1)
        w1_wp = held([P, kpasses * H], U16, "w1_wp")
        w2_raw = [held([P, PACK, PASS], F32, "w2_raw0"), placed([P, PACK, PASS], F32, "w2_raw1", at_w2_second)]
        w3_raw = placed([P, groups, PACK, N], F32, "w3_raw", at_w3)
        emis_raw = held([groups, PASS], F32, "emis_raw")
        emis_rows = held([P, PASS], F32, "emis_rows")
        ident = held([P, P], F32, "ident")
        emis2 = held([P, groups * PACK], F32, "emis2")
        inverse2 = placed([P, groups * PACK], F32, "inverse2", at_slot1)
        one = held([P, 1], F32, "one")
        warm = held([P, 1], F32, "warm")

        nc.vector.memset(w1_rows[:].bitcast(I32), 0)
        nc.vector.memset(tab2_s[0 : P - 16, :].bitcast(I32), 0)
        nc.vector.memset(tab_s[:, 0 : T // 2].bitcast(I32), 0)
        nc.gpsimd.memset(one[:], 1.0)
        nc.gpsimd.memset(tab_s[:, T // 2 : T].bitcast(I32), 0)
        nc.scalar.dma_start(emis_raw[:], emis.rearrange("(g c) -> g c", g=groups))
        nc.scalar.activation(warm[:], one[:], ACT.Abs_reciprocal_sqrt)
        nc.scalar.activation(emis_rows[:], one[:].to_broadcast([P, PASS]), ACT.Copy, scale=0.0)
        make_identity(nc, ident[:])

        w2_rows = w2.rearrange("(p j) r -> p j r", j=PACK)
        nc.sync.dma_start(idx2[:], offs2)
        nc.sync.dma_start(tab2_s[P - 16 : P, :].bitcast(I32), tab2_scales[0].bitcast(I32))
        nc.sync.dma_start(idx[:], offs)
        nc.sync.dma_start(tab2_w[:].bitcast(I32), tab2_words[0].bitcast(I32))
        nc.sync.dma_start(w1_rows[32:96:2, :].bitcast(I32), w1_scales.rearrange("a q c -> q a c").bitcast(I32))
        nc.sync.dma_start(w2_raw[0][:], w2_rows[:, :, 0:PASS])
        nc.sync.dma_start(tab_s[32:96:2, :].bitcast(I32), tab_scales.rearrange("a q t -> q a t").bitcast(I32))

        nc.vector.tensor_copy(v2_rows[:], tab2_s[:].indirect(idx2[:]))
        for r in range(QUADS):
            nc.sync.dma_start(v2_s[r:P:32, :].bitcast(I32), v2_rows[P - 16 + r : P : 4, :].bitcast(I32))
        nc.sync.dma_start(w2_raw[1][:], w2_rows[:, :, PASS : 2 * PASS])
        nc.sync.dma_start(
            w1_w[:].bitcast(I32).rearrange("p (a x) -> p a x", a=kpasses), w1_words.rearrange("a p x -> p a x").bitcast(I32)
        )

        def load_tab(a):
            nc.sync.dma_start(tab_w[a][:], tab_words[a].rearrange("p t i -> p (t i)").bitcast(I32))

        load_tab(0)

        v2_w = [held([P, HALF], U16, "v2_w%d" % j) for j in range(halves)]
        for j in range(halves):
            nc.vector.tensor_copy(v2_w[j][:], tab2_w[:].indirect(picks(idx2, j * HALF, HALF)))

        w2_c = [held([P, PASS], U32, "w2_c%d" % g) for g in range(groups)]
        w2_q = [held([P, PASS], U8, "w2_q%d" % g) for g in range(groups)]

        def round_w2(copy, g, t0, slots, into):
            copy(
                into.rearrange("p (t b i j) -> p b t j i", t=slots, i=RUN, j=PACK),
                w2_raw[g][:].rearrange("p j (b t i) -> p b t j i", t=PACK, i=RUN)[:, :, t0 : t0 + slots],
            )

        def quantise_w2(g, t0, slots, values):
            cols = slice(t0 * P, (t0 + slots) * P)
            quantise(w2_c[g][:, cols], w2_q[g][:, cols], values)

        slots = [
            placed([P, PASS], BF16, "slot%d" % t, at_slot1) if t == 1 else held([P, PASS], BF16, "slot%d" % t)
            for t in range(PACK)
        ]
        for t in range(PACK):
            round_w2(nc.scalar.copy if t in FIRST_ROUNDINGS_ON_SCALAR else nc.vector.tensor_copy, 0, t, 1, slots[t][:])
        for t in FIRST_SLOTS:
            quantise_w2(0, t, 1, slots[t][:])

        turned = banks[7]
        nc.scalar.copy(
            emis_rows[0:groups, :].rearrange("g (t b i) -> g t b i", t=PACK, i=RUN),
            emis_raw[:].rearrange("g (b t i) -> g t b i", t=PACK, i=RUN),
        )
        for t in range(PACK):
            nc.tensor.transpose(turned[:, t * P : (t + 1) * P], emis_rows[:, t * P : (t + 1) * P], ident[:])
        nc.scalar.activation(
            emis2[:].rearrange("p (g t) -> p t g", g=groups),
            turned[:].rearrange("p (t c) -> p t c", t=PACK)[:, :, 0:groups],
            ACT.Square,
        )

        def unit(g, t):
            return inverse2[:, g * PACK + t : g * PACK + t + 1]

        damp = held([P, PACK, chunks * both], F32, "damp")
        damp_of = damp[:].rearrange("p t (c g e) -> p t c g e", g=groups, e=CHUNK)
        per_half = HALF // CHUNK

        def by_chunk(ap):
            return ap.rearrange("p (c e) -> p c e", e=CHUNK)

        def product_b(g, j, t, bank):
            cols = slice(t * P, (t + 1) * P)
            nc.tensor.matmul_mx(
                out=bank[:],
                lhsT=w2_c[g][:, cols].bitcast(FP8X4),
                lhsT_scale=w2_q[g][:, cols],
                rhs=v2_w[j][:].bitcast(FP4X4),
                rhs_scale=v2_s[:, j * HALF : (j + 1) * HALF],
                start=True,
                stop=True,
            )

        def squared(g, j, t):
            return damp_of[:, t, j * per_half : (j + 1) * per_half, g, :]

        turn = [0]

        def square_on_scalar(g, j, t):
            bank = banks[turn[0] % 4]
            turn[0] = turn[0] + 1
            product_b(g, j, t, bank)
            nc.scalar.activation(squared(g, j, t), by_chunk(bank[:]), ACT.Square)

        for t in FIRST_SLOTS:
            for j in range(halves):
                square_on_scalar(0, j, t)

        def deal(copy, dst, src, words):
            copy(
                dst.bitcast(U32).rearrange("p (g t b w) -> p g b t w", t=PACK, b=P // RUN, w=words),
                src.bitcast(U32).rearrange("p (g b t w) -> p g b t w", t=PACK, b=P // RUN, w=words),
            )

        deal(nc.scalar.copy, joined[:, S : S + H], w1_rows[:], 2)

        nc.vector.reciprocal(inverse2[:], emis2[:])
        nc.vector.tensor_copy(v_rows[:], tab_s[:].indirect(idx[:]))
        nc.vector.tensor_copy(joined[:, 0:S].bitcast(I32), v_rows[:].bitcast(I32))

        def spread_a(a):
            for r in range(QUADS):
                src = joined[32 + 2 * a + 4 * r : 96 : 16, :]
                nc.sync.dma_start(a_s[r:P:32, a * (S + H) : (a + 1) * (S + H)].bitcast(I32), src.bitcast(I32))

        spread_a(0)
        load_tab(1)
        spread_a(1)
        for g in range(groups):
            rows = w3[g * PASS : (g + 1) * PASS, :].rearrange("(b t i) n -> t b i n", t=PACK, i=RUN)
            for t in range(PACK):
                nc.sync.dma_start(w3_raw[:, g, t, :], rows[t])

        second = [held([P, 2 * PASS], BF16, "second%d" % u) for u in range(2)]
        for u in range(2):
            round_w2(nc.vector.tensor_copy, 1, 2 * u, 2, second[u][:])
        for u in range(2):
            quantise_w2(1, 2 * u, 2, second[u][:])
        deal(nc.vector.tensor_copy, w1_wp[:], w1_w[:], 4)

        spans = [((0, HALF), (HALF, HALF)), ((HALF // 2, HALF // 2), (0, HALF // 2), (HALF, HALF))]
        words_of = {}

        def gather_words(a, first, count):
            picked = held([P, count], U32, "v_w%d_%d" % (a, first))
            nc.vector.tensor_copy(picked[:], tab_w[a][:].bitcast(U32).indirect(picks(idx, first, count)))
            for c in range(first // CHUNK, (first + count) // CHUNK):
                words_of[a, c] = picked[:, c * CHUNK - first : (c + 1) * CHUNK - first]

        twins = [held([P, HALF], F32, "twin%d" % u) for u in range(2)] + [
            placed([P, HALF], F32, "twin%d" % (u + 2), at_tab0 + u * HALF * 4) for u in range(len(SQUARES_ON_VECTOR) - 2)
        ]

        def take(u):
            nc.vector.tensor_copy(twins[u][:], banks[4 + u][:])

        def square(u):
            nc.vector.tensor_tensor(squared(*SQUARES_ON_VECTOR[u]), by_chunk(banks[4 + u][:]), by_chunk(twins[u][:]), MULT)

        def damping(places):
            for g, t in places:
                part = damp_of[:, t, SIGNED:chunks, g, :]
                nc.scalar.activation(part, part, ACT.Abs_reciprocal_sqrt, bias=unit(g, t), scale=unit(g, t))

        for u, place in enumerate(SQUARES_ON_VECTOR):
            product_b(*place, banks[4 + u])
        for u in range(PACK):
            square_on_scalar(1, u % halves, 2 + u // halves)
        for step in (take, square):
            for u in (0, 1):
                step(u)
        for span in spans[0]:
            gather_words(0, *span)
        for step in (take, square):
            for u in range(2, len(SQUARES_ON_VECTOR)):
                step(u)

        damping([(g, t) for g in range(groups) for t in range(PACK)])
        for span in spans[1]:
            gather_words(1, *span)

        def bank_a(g, c):
            return banks[groups * PAIR_OF_CHUNK[c] + g]

        def by_slot(ap):
            return ap.rearrange("p (t e) -> p t e", t=PACK)

        def pass_a(g, c, a):
            for t in range(PACK):
                c0 = a * (S + H) + S + g * PASS + t * P
                w0 = a * H + g * PASS + t * P
                s0 = a * (S + H) + c * CHUNK
                nc.tensor.matmul_mx(
                    out=bank_a(g, c)[:, t * CHUNK : (t + 1) * CHUNK],
                    lhsT=w1_wp[:, w0 : w0 + P].bitcast(FP4X4),
                    lhsT_scale=a_s[:, c0 : c0 + P],
                    rhs=words_of[a, c].bitcast(FP8X4),
                    rhs_scale=a_s[:, s0 : s0 + CHUNK],
                    start=(a == 0 and t == 0),
                    stop=(a == kpasses - 1 and t == PACK - 1),
                )

        free_order = [4, 5] + [(turn[0] + u) % 4 for u in range(4)] + [6, 7]
        for u in free_order:
            pass_a(u % groups, u // groups, 0)

        roots = held([P, PACK, SIGNED * both], F32, "roots")
        roots_of_signed = roots[:].rearrange("p t (c g e) -> p t c g e", g=groups, e=CHUNK)
        joint = held([P, PACK * SIGNED * both], F32, "joint")
        joint_of = joint[:].rearrange("p (t c g e) -> p t c g e", t=PACK, g=groups, e=CHUNK)
        spare = [joint[:, PACK * both :], joint[:, 0 : PACK * both]]
        mags = [held([P, PACK * both], F32, "mag%d" % u) for u in range(2)] + [
            placed([P, PACK * both], F32, "mag%d" % (u + 2), at_tab0 + (u + 1) * PACK * both * 4) for u in range(2)
        ]

        def of_group(root, g):
            return root.rearrange("p (t g e) -> p t g e", t=PACK, g=groups)[:, :, g, :]

        def magnitude(g, c, into):
            nc.scalar.activation(of_group(into, g), by_slot(bank_a(g, c)[:]), ACT.Abs)

        def join(g, c):
            nc.vector.scalar_tensor_tensor(
                joint_of[:, :, c, g, :], damp_of[:, :, c, g, :], 1.0, by_slot(bank_a(g, c)[:]), ADD, MULT
            )

        def joint_roots(g):
            for t in range(PACK):
                nc.scalar.activation(
                    roots_of_signed[:, t, :, g, :],
                    joint_of[:, t, :, g, :],
                    ACT.Abs_reciprocal_sqrt,
                    bias=TINY,
                    scale=unit(g, t),
                )

        for g, c in ((0, 2), (1, 2), (0, 0), (0, 3), (0, 1), (1, 3), (1, 0), (1, 1)):
            pass_a(g, c, 1)
        for c in range(SIGNED, EARLY):
            for g in range(groups):
                magnitude(g, c, mags[c - SIGNED][:])
        for g in range(groups):
            for c in range(SIGNED):
                join(g, c)
            joint_roots(g)

        def sum_a(chunk_range):
            for c in chunk_range:
                for g in range(groups):
                    for a in range(kpasses):
                        pass_a(g, c, a)

        sum_a(range(EARLY, EARLY + 2))

        w3_bf = [held([P, N * PACK], BF16, "w3_bf%d" % g) for g in range(groups)]
        w3_c = [held([P, N], U32, "w3_c%d" % g) for g in range(groups)]
        w3_q = [held([P, N], U8, "w3_q%d" % g) for g in range(groups)]

        def round_w3(g):
            nc.vector.tensor_copy(
                w3_bf[g][:].rearrange("p (c i j) -> p c j i", i=4, j=PACK),
                w3_raw[:, g].rearrange("p j (c i) -> p c j i", i=4),
            )

        round_w3(0)

        def multiply(into, left, right):
            nc.vector.tensor_tensor(
                into.rearrange("p (q i t) -> p q t i", i=STEP, t=PACK),
                left.rearrange("p t (q i) -> p q t i", i=STEP),
                right.rearrange("p t (q i) -> p q t i", i=STEP),
                MULT,
            )

        def flux(acc, n0, g, h_c, h_q):
            tiles = acc.shape[1]
            for u in range(tiles):
                bands = slice((n0 + u) * P, (n0 + u + 1) * P)
                nc.tensor.matmul_mx(
                    out=acc[:, u, :],
                    lhsT=w3_c[g][:, bands].bitcast(FP8X4),
                    lhsT_scale=w3_q[g][:, bands],
                    rhs=h_c[:, g * CHUNK : (g + 1) * CHUNK].bitcast(FP8X4),
                    rhs_scale=h_q[:, g * CHUNK : (g + 1) * CHUNK],
                    start=(g == 0 and u == 0),
                    stop=(g == groups - 1 and u == tiles - 1),
                )

        def sums_in(bank, tiles):
            return bank[:, 0 : tiles * CHUNK].rearrange("p (u j) -> p u j", u=tiles)

        def store(copy, acc, n0, c, queue=nc.sync):
            tiles = acc.shape[1]
            res = ring.tile([P, tiles, CHUNK], F32, name="res", align_bytes=64, bufs=10)
            copy(res[:], acc)
            rows = out[n0 * P : (n0 + tiles) * P, c * CHUNK : (c + 1) * CHUNK]
            queue.dma_start(rows.rearrange("(u p) j -> p u j", p=P), res[:])

        def packed_tiles():
            h_c = ring.tile([P, both], U32, name="h_c", align_bytes=64, bufs=4)
            h_q = ring.tile([P, both], U8, name="h_q", align_bytes=64, bufs=4)
            return h_c, h_q

        def pack(h_bf):
            h_c, h_q = packed_tiles()
            quantise(h_c[:], h_q[:], h_bf)
            return h_c[:], h_q[:]

        sums = {}

        def open_sums(c, h_c, h_q):
            sums[c] = sums_in(banks[BANK_OF_SUMS[c]], N // P)
            for g in range(groups):
                flux(sums[c], 0, g, h_c, h_q)

        signed = held([P, SIGNED * both * PACK], BF16, "signed")
        mirror = held([P, SIGNED * both * PACK], BF16, "mirror")
        signed_c = held([P, SIGNED * both], U32, "signed_c")
        signed_q = held([P, SIGNED * both], U8, "signed_q")
        for g in range(groups):
            for c in range(SIGNED):
                at = (c * groups + g) * CHUNK * PACK
                multiply(signed[:, at : at + CHUNK * PACK], roots_of_signed[:, :, c, g, :], by_slot(bank_a(g, c)[:]))
        sum_a(range(EARLY + 2, chunks))
        quantise(w3_c[0][:], w3_q[0][:], w3_bf[0][:])
        nc.vector.tensor_scalar(mirror[:], signed[:], -1.0, None, MULT)
        round_w3(1)
        nc.vector.tensor_tensor(signed[:], signed[:], mirror[:], MAX)
        quantise(w3_c[1][:], w3_q[1][:], w3_bf[1][:])
        quantise(signed_c[:], signed_q[:], signed[:])

        root_in = dict(enumerate(spare + [tile[:] for tile in mags], SIGNED))
        ends = (slice(0, CHUNK), slice(CHUNK, both))

        def magnitudes(c):
            for g in range(groups):
                magnitude(g, c, root_in[c])

        def roots_of(c):
            if c == last:
                magnitudes(c)
            for done in COPIES_AHEAD_OF_ROOT.get(c, ()):
                store(nc.scalar.copy, sums[done], 0, done)
            for cols in ends if c == last else (slice(0, both),):
                source = mags[c - SIGNED][:] if c < EARLY else root_in[c]
                nc.scalar.activation(by_slot(root_in[c])[:, :, cols], by_slot(source)[:, :, cols], ACT.Sqrt)
            if c + 2 < last:
                magnitudes(c + 2)

        def product(c, h_bf, cols=slice(0, both)):
            factor = damp[:, :, c * both + cols.start : c * both + cols.stop]
            multiply(h_bf[:, cols.start * PACK : cols.stop * PACK], factor, by_slot(root_in[c])[:, :, cols])

        staged = [held([P, both * PACK], BF16, "staged%d" % u) for u in range(3)]
        roots_of(SIGNED)
        for c in range(SIGNED):
            open_sums(c, signed_c[:, c * both : (c + 1) * both], signed_q[:, c * both : (c + 1) * both])
        for c in range(SIGNED, last):
            if c + 1 < last:
                roots_of(c + 1)
            product(c, staged[c % 3][:])
            if c > SIGNED:
                open_sums(c - 1, *pack(staged[(c - 1) % 3][:]))
            if c + 1 == last:
                roots_of(last)
            if c - 2 == SHARED_COPY:
                store(nc.vector.tensor_copy, sums[c - 2][:, 0:2], 0, c - 2)
            if c - 2 in COPIES_ON_VECTOR:
                store(nc.vector.tensor_copy, sums[c - 2], 0, c - 2)
        open_sums(last - 1, *pack(staged[(last - 1) % 3][:]))
        h_bf = staged[last % 3][:]
        h_c, h_q = packed_tiles()
        accs = [(sums_in(banks[2], 2), 0), (sums_in(banks[3], 2), 2)]

        def pack_end(cols):
            quantise(h_c[:, cols], h_q[:, cols], h_bf[:, cols.start * PACK : cols.stop * PACK])

        for cols in ends:
            product(last, h_bf, cols)
        for cols in ends:
            pack_end(cols)
        for g in range(groups):
            for acc, n0 in accs:
                flux(acc, n0, g, h_c[:], h_q[:])
        store(nc.scalar.copy, sums[SHARED_COPY][:, 2:4], 2, SHARED_COPY)
        for done in (last - 2, last - 1):
            store(nc.scalar.copy, sums[done], 0, done)
        store(nc.vector.tensor_copy, *accs[0], last)
        store(nc.scalar.copy, *accs[1], last, nc.scalar)
